import numpy as np
import ml_dtypes


def mxq(x, axis, fmt="e4m3"):
    dtype, down = {"e4m3": (ml_dtypes.float8_e4m3fn, 7), "e5m2": (ml_dtypes.float8_e5m2, 14)}[fmt]
    v = np.moveaxis(np.asarray(x, np.float32).astype(ml_dtypes.bfloat16).astype(np.float64), axis, -1)
    blocks = v.reshape(v.shape[:-1] + (-1, 32))
    amax = np.abs(blocks).max(-1, keepdims=True)
    byte = np.maximum(np.where(amax > 0, np.frexp(amax)[1] - 1 + 127, 0) - down, 1)
    scale = np.exp2(byte - 127.0)
    codes = (blocks / scale).astype(np.float32).astype(dtype).astype(np.float64)
    return np.moveaxis((codes * scale).reshape(v.shape), -1, axis)


WIDE = False


def mx_kscale(k):
    if not WIDE:
        return np.ones(k)
    levels = np.array([10, -10, 5, -5, 0])
    if k % 512:
        return np.exp2(np.random.permutation(np.resize(levels, k // 32))).repeat(32)
    a = np.empty((k // 512, 16))
    for p in range(k // 512):
        a[p, :8] = np.random.permutation(np.resize(levels, 8))
        for g in range(8):
            far = levels[np.abs(levels - a[p, g]) >= 10]
            a[p, g + 8] = far[np.random.randint(len(far))]
    return np.exp2(a.ravel()).repeat(32)


def f64(x):
    return np.asarray(x).astype(np.float64)


def striped(idx):
    return np.tile(idx.reshape(-1, 16).T, (8, 1)).astype(np.uint16)


def unstriped(offs):
    return offs[:16].T.reshape(-1).astype(np.int64)


def pack_weight(w):
    k, n = w.shape
    w = f64(np.asarray(w, np.float32).astype(ml_dtypes.bfloat16)).reshape(k // 32, 32, n)
    amax = np.abs(w).max(1)
    byte = np.clip(np.where(amax > 0, np.frexp(amax)[1] - 1 + 127 - 7, 1), 1, 254)
    scaled = (w * np.exp2(127.0 - byte)[:, None, :]).reshape(k, n).astype(np.float32)
    words = np.ascontiguousarray(scaled.reshape(k // 512, 128, 4, n).transpose(0, 1, 3, 2)).astype(ml_dtypes.float8_e4m3fn).view(np.uint8)
    return words, np.ascontiguousarray(byte.astype(np.uint8).reshape(k // 512, 16, n))


def unpack_weight(words, scales):
    g, p, n, _ = words.shape
    vals = np.ascontiguousarray(words).view(ml_dtypes.float8_e4m3fn).astype(np.float64) * np.repeat(np.exp2(scales.astype(np.float64) - 127.0), 8, axis=1)[..., None]
    return vals.transpose(0, 1, 3, 2).reshape(g * 512, n)


def planes(y):
    n, m = y.shape
    v = y.astype(np.float32).astype(ml_dtypes.bfloat16).astype(np.float64).reshape(n // 32, 32, m)
    top = np.abs(v).max(1)
    byte = np.clip(np.where(top > 0, np.frexp(top)[1] - 1 + 127 - 7, 1), 1, 254)
    codes = (v * np.exp2(127.0 - byte)[:, None, :]).reshape(n, m).astype(np.float32).astype(ml_dtypes.float8_e4m3fn).view(np.uint8)
    words = codes.reshape(n // 512, 128, 4, m).transpose(0, 1, 3, 2)
    return np.ascontiguousarray(words), np.ascontiguousarray(byte.astype(np.uint8).reshape(n // 512, 16, m))


def relu(v):
    return np.maximum(v, 0.0)


K, T, S, D, V, H, N, U = 512, 4096, 1024, 3, 512, 512, 512, 256
P = 2 ** 7


def setup_inputs():
    n = np.random.standard_normal
    s = mx_kscale(K)[:, None]
    u = mx_kscale(H)
    near = np.random.permutation(S)
    next_ = np.random.permutation(V)
    packed_xT = pack_weight(n((K, T)) * s)
    return {
        "x_words": packed_xT[0],
        "x_scales": packed_xT[1],
        "w1": (n((K, H)) / np.sqrt(K) / s * u).astype(np.float32),
        "w2": (n((H, N)) / np.sqrt(H) / u[:, None]).astype(np.float32),
        "gate": (np.tile(np.random.uniform(0.2, 1.0, (D, 1, V)) / np.sqrt(D), (1, P, 1))).astype(np.float32),
        "gate2": (np.tile(np.random.uniform(0.2, 1.0, (D, 1, U)) / np.sqrt(D), (1, P, 1))).astype(np.float32),
        "offs": striped(np.random.permutation(T)[:S]),
        "cen": striped(np.random.permutation(S)[:V]),
        "pos1": striped(near[:V]),
        "pos2": striped(near[V:]),
        "pos3": striped(np.random.permutation(S)[:V]),
        "nxt1": striped(next_[:U]),
        "nxt2": striped(next_[U:]),
        "nxt3": striped(np.random.permutation(V)[:U]),
        "root": striped(np.random.permutation(S)[:U]),
    }


def reference(x_words, x_scales, w1, w2, gate, gate2, offs, cen, pos1, pos2, pos3, nxt1, nxt2, nxt3, root):
    xq = unpack_weight(x_words, x_scales)[:, unstriped(offs)]
    h = relu(mxq(f64(w1), 0, "e4m3").T @ xq)
    y = mxq(f64(w2), 0, "e4m3").T @ mxq(h, 0, "e4m3")
    z = 0.8 * (y[:, unstriped(pos1)] * f64(gate)[0, :1] + y[:, unstriped(pos2)] * f64(gate)[1, :1] + y[:, unstriped(pos3)] * f64(gate)[2, :1]) + 0.2 * y[:, unstriped(cen)]
    out_0 = 0.8 * (z[:, unstriped(nxt1)] * f64(gate2)[0, :1] + z[:, unstriped(nxt2)] * f64(gate2)[1, :1] + z[:, unstriped(nxt3)] * f64(gate2)[2, :1]) + 0.2 * y[:, unstriped(root)]
    return (out_0,) + planes(out_0)

@@ -1,0 +1,199 @@
+from contextlib import ExitStack
+
+import concourse.mybir as mybir
+from concourse.masks import make_identity
+
+K, T, S, D, V, H, N, U = 512, 4096, 1024, 3, 512, 512, 512, 256
+FLOPS = 2 * K * H * S + 2 * H * N * S
+
+F32 = mybir.dt.float32
+BF16 = mybir.dt.bfloat16
+I32 = mybir.dt.int32
+U32 = mybir.dt.uint32
+U16 = mybir.dt.uint16
+U8 = mybir.dt.uint8
+FP8X4 = mybir.dt.float8_e4m3fn_x4
+MULT = mybir.AluOpType.mult
+ADD = mybir.AluOpType.add
+ACT = mybir.ActivationFunctionType
+
+P = 128
+PACK = 4
+HALF = S // 2
+BLK = 128
+QTR = 256
+
+
+def tile_picked_zappnp_relu_po_kernel(
+    tc, x_words, x_scales, w1, w2, gate, gate2, offs, cen, pos1, pos2, pos3, nxt1, nxt2, nxt3, root,
+    out_0, out_1, out_2,
+):
+    nc = tc.nc
+    with ExitStack() as ctx:
+        held = ctx.enter_context(tc.tile_pool(name="held", bufs=1))
+        work = ctx.enter_context(tc.tile_pool(name="work", bufs=2))
+        psum = ctx.enter_context(tc.psum_pool(name="psum", bufs=8))
+
+        def load_list(name, src):
+            tl = held.tile(list(src.shape), U16, name=name)
+            nc.sync.dma_start(tl[:], src)
+            return tl
+
+        offs_t = load_list("offs_t", offs)
+        xw = held.tile([P, T], I32, name="xw", align_bytes=64)
+        x_rows = x_words[0].rearrange("p n t -> p (n t)").bitcast(I32)
+        nc.sync.dma_start(xw[:, : T // 2], x_rows[:, : T // 2])
+        xs = held.tile([P, T], U8, name="xs", align_bytes=64)
+        nc.vector.memset(xs[:].bitcast(I32), 0)
+        for q in range(4):
+            nc.sync.dma_start(xs[32 * q : 32 * q + 4, :].bitcast(I32), x_scales[0, 4 * q : 4 * q + 4, :].bitcast(I32))
+        nc.sync.dma_start(xw[:, T // 2 :], x_rows[:, T // 2 :])
+        w1_raw = held.tile([P, PACK, H], F32, name="w1_raw")
+        nc.sync.dma_start(w1_raw[:], w1.rearrange("(p j) c -> p j c", j=PACK))
+        w2_raw = held.tile([P, PACK, N], F32, name="w2_raw")
+        nc.sync.dma_start(w2_raw[:], w2.rearrange("(p j) c -> p j c", j=PACK))
+        g1 = held.tile([P, D, V], F32, name="g1")
+        nc.sync.dma_start(g1[:], gate.rearrange("d p v -> p d v"))
+        pos_t = [load_list("pos1_t", pos1), load_list("pos2_t", pos2), load_list("pos3_t", pos3)]
+        cen_t = load_list("cen_t", cen)
+        nxt_t = [load_list("nxt1_t", nxt1), load_list("nxt2_t", nxt2), load_list("nxt3_t", nxt3)]
+        root_t = load_list("root_t", root)
+        g2 = held.tile([P, D, U], F32, name="g2")
+        nc.sync.dma_start(g2[:], gate2.rearrange("d p v -> p d v"))
+
+        ident = held.tile([P, P], F32, name="ident")
+        make_identity(nc, ident[:])
+        quarter = held.tile([P, V], F32, name="quarter")
+        nc.gpsimd.memset(quarter[:], 0.25)
+
+        xs_g = held.tile([P, S], U8, name="xs_g", align_bytes=64)
+        nc.vector.tensor_copy(xs_g[:], xs[:].indirect(offs_t[:]))
+        xw_g = []
+        for hf in range(2):
+            tl = held.tile([P, HALF], U32, name="xw_g%d" % hf, align_bytes=64)
+            nc.vector.tensor_copy(tl[:], xw[:].bitcast(U32).indirect(offs_t[:, hf * HALF // 16 : (hf + 1) * HALF // 16]))
+            xw_g.append(tl)
+
+        def deal(engine_copy, grouped, raw, m0, m1):
+            engine_copy(
+                grouped[:].rearrange("p (t m j) -> p m j t", t=PACK, j=PACK)[:, m0:m1],
+                raw[:].rearrange("p j (m t) -> p m j t", t=PACK)[:, m0:m1],
+            )
+
+        w1_b = held.tile([P, PACK * H], BF16, name="w1_b", align_bytes=64)
+        deal(nc.vector.tensor_copy, w1_b, w1_raw, 0, 80)
+        deal(nc.scalar.copy, w1_b, w1_raw, 80, 128)
+        w1_c = held.tile([P, H], U32, name="w1_c", align_bytes=64)
+        w1_s = held.tile([P, H], U8, name="w1_s", align_bytes=64)
+        nc.vector.quantize_mx(out=w1_c[:].bitcast(FP8X4), scales=w1_s[:], in_=w1_b[:])
+
+        def w2_slot(t, engine_copy):
+            w2_b = held.tile([P, PACK * P], BF16, name="w2_b%d" % t, align_bytes=64)
+            w2_c = held.tile([P, P], U32, name="w2_c%d" % t, align_bytes=64)
+            w2_s = held.tile([P, P], U8, name="w2_s%d" % t, align_bytes=64)
+            engine_copy(
+                w2_b[:].rearrange("p (m j) -> p m j", j=PACK),
+                w2_raw[:].rearrange("p j (m t) -> p t m j", t=PACK)[:, t],
+            )
+            nc.vector.quantize_mx(out=w2_c[:].bitcast(FP8X4), scales=w2_s[:], in_=w2_b[:])
+            return w2_c, w2_s
+
+        w2_q = [w2_slot(0, nc.vector.tensor_copy)]
+
+        h_c = [held.tile([P, HALF], U32, name="h_c%d" % hf, align_bytes=64) for hf in range(2)]
+        h_s = [held.tile([P, HALF], U8, name="h_s%d" % hf, align_bytes=64) for hf in range(2)]
+        for qt in range(S // QTR):
+            h_b = held.tile([P, PACK * QTR], BF16, name="h_b%d" % qt, align_bytes=64)
+            for sub in range(QTR // BLK):
+                c0 = qt * QTR + sub * BLK
+                hf, c = divmod(c0, HALF)
+                bank = psum.tile([P, PACK, BLK], F32, name="bank")
+                for t in range(PACK):
+                    nc.tensor.matmul_mx(
+                        out=bank[:, t, :],
+                        lhsT=w1_c[:, t * P : (t + 1) * P].bitcast(FP8X4), lhsT_scale=w1_s[:, t * P : (t + 1) * P],
+                        rhs=xw_g[hf][:, c : c + BLK].bitcast(FP8X4), rhs_scale=xs_g[:, c0 : c0 + BLK],
+                        start=True, stop=True,
+                    )
+                dst = h_b[:, sub * PACK * BLK : (sub + 1) * PACK * BLK].rearrange("p (n t) -> p n t", t=PACK)
+                src = bank[:].rearrange("p t n -> p n t")
+                if c0 // BLK in (1, 4, 6):
+                    nc.vector.tensor_scalar_max(dst, src, 0.0)
+                else:
+                    nc.scalar.activation(dst, src, ACT.Relu)
+            hf, c = divmod(qt * QTR, HALF)
+            nc.vector.quantize_mx(out=h_c[hf][:, c : c + QTR].bitcast(FP8X4), scales=h_s[hf][:, c : c + QTR], in_=h_b[:])
+
+        y = []
+        for t in range(PACK):
+            if t > 0:
+                w2_q.append(w2_slot(t, nc.scalar.copy))
+            w2_c, w2_s = w2_q[t]
+            y_t = held.tile([P, S], F32, name="y%d" % t)
+            for hf in range(2):
+                bank = psum.tile([P, HALF], F32, name="bank")
+                nc.tensor.matmul_mx(
+                    out=bank[:],
+                    lhsT=w2_c[:].bitcast(FP8X4), lhsT_scale=w2_s[:],
+                    rhs=h_c[hf][:].bitcast(FP8X4), rhs_scale=h_s[hf][:],
+                    start=True, stop=True,
+                )
+                if t == 0 and hf == 1:
+                    nc.vector.tensor_scalar_mul(y_t[:, hf * HALF : (hf + 1) * HALF], bank[:], 0.8)
+                else:
+                    nc.scalar.activation(y_t[:, hf * HALF : (hf + 1) * HALF], bank[:], ACT.Copy, scale=0.8)
+            y.append(y_t)
+
+        def terms(tag, width, window, lists, gates, own_window, own_list):
+            a = [work.tile([P, width], F32, name="%s_a%d" % (tag, d)) for d in range(D + 1)]
+            nc.vector.tensor_tensor(a[D][:], own_window[:].indirect(own_list[:]), quarter[:, :width], MULT)
+            for d in range(D):
+                nc.vector.tensor_tensor(a[d][:], window[:].indirect(lists[d][:]), gates[:, d, :], MULT)
+            return a
+
+        def add_in_psum(tag, width, a, dst, factor):
+            turned = psum.tile([P, width], F32, name="bank")
+            for b in range(width // P):
+                cols = slice(b * P, (b + 1) * P)
+                for d in range(D + 1):
+                    nc.tensor.matmul(turned[:, cols], a[d][:, cols], ident[:], start=(d == 0), stop=(d == D), is_transpose=True)
+            total = work.tile([P, width], F32, name=tag + "_sum")
+            nc.scalar.copy(total[:], turned[:])
+            back = psum.tile([P, width], F32, name="bank")
+            for b in range(width // P):
+                cols = slice(b * P, (b + 1) * P)
+                nc.tensor.transpose(back[:, cols], total[:, cols], ident[:])
+            if factor is None:
+                nc.scalar.copy(dst, back[:])
+            else:
+                nc.scalar.activation(dst, back[:], ACT.Copy, scale=factor)
+
+        res = held.tile([P, PACK, U], F32, name="res")
+        out_rows = out_0.rearrange("(p t) x -> p t x", t=PACK)
+        z = [held.tile([P, V], F32, name="z%d" % t) for t in range(PACK)]
+        for t in range(PACK):
+            add_in_psum("z", V, terms("z", V, y[t], pos_t, g1, y[t], cen_t), z[t][:], 0.8)
+        for t in range(PACK):
+            a = terms("o", U, z[t], nxt_t, g2, y[t], root_t)
+            if t < PACK - 1:
+                add_in_psum("o", U, a, res[:, t, :], None)
+            else:
+                s0 = work.tile([P, U], F32, name="s0")
+                s1 = work.tile([P, U], F32, name="s1")
+                nc.vector.tensor_tensor(s0[:], a[D][:], a[0][:], ADD)
+                nc.vector.tensor_tensor(s1[:], a[1][:], a[2][:], ADD)
+                nc.vector.tensor_tensor(res[:, t, :], s0[:], s1[:], ADD)
+            nc.sync.dma_start(out_rows[:, t, :], res[:, t, :])
+
+        res_b = held.tile([P, PACK * U], BF16, name="res_b", align_bytes=64)
+        nc.vector.tensor_copy(
+            res_b[:].rearrange("p (c i t) -> p c t i", i=4, t=PACK),
+            res[:].rearrange("p t (c i) -> p c t i", i=4),
+        )
+        res_c = held.tile([P, U], I32, name="res_c", align_bytes=64)
+        res_s = held.tile([P, U], U8, name="res_s", align_bytes=64)
+        nc.vector.quantize_mx(out=res_c[:].bitcast(FP8X4), scales=res_s[:], in_=res_b[:])
+        nc.sync.dma_start(out_1[0].rearrange("p n t -> p (n t)").bitcast(I32), res_c[:])
+        for q in range(4):
+            eng = nc.scalar if q % 2 else nc.sync
+            eng.dma_start(out_2[0, 4 * q : 4 * q + 4, :].bitcast(I32), res_s[32 * q : 32 * q + 4, :].bitcast(I32))

@@ -40,16 +40,14 @@ def tile_picked_zappnp_relu_po_kernel(
             return tl
 
         offs_t = load_list("offs_t", offs)
-        xw = held.tile([P, T], I32, name="xw", align_bytes=64)
-        x_rows = x_words[0].rearrange("p n t -> p (n t)").bitcast(I32)
-        nc.sync.dma_start(xw[:, : T // 2], x_rows[:, : T // 2])
+        w1_raw = held.tile([P, PACK, H], F32, name="w1_raw")
+        nc.sync.dma_start(w1_raw[:], w1.rearrange("(p j) c -> p j c", j=PACK))
         xs = held.tile([P, T], U8, name="xs", align_bytes=64)
         nc.vector.memset(xs[:].bitcast(I32), 0)
         for q in range(4):
             nc.sync.dma_start(xs[32 * q : 32 * q + 4, :].bitcast(I32), x_scales[0, 4 * q : 4 * q + 4, :].bitcast(I32))
-        nc.sync.dma_start(xw[:, T // 2 :], x_rows[:, T // 2 :])
-        w1_raw = held.tile([P, PACK, H], F32, name="w1_raw")
-        nc.sync.dma_start(w1_raw[:], w1.rearrange("(p j) c -> p j c", j=PACK))
+        xw = held.tile([P, T], I32, name="xw", align_bytes=64)
+        nc.sync.dma_start(xw[:], x_words[0].rearrange("p n t -> p (n t)").bitcast(I32))
         w2_raw = held.tile([P, PACK, N], F32, name="w2_raw")
         nc.sync.dma_start(w2_raw[:], w2.rearrange("(p j) c -> p j c", j=PACK))
         g1 = held.tile([P, D, V], F32, name="g1")
@@ -66,6 +64,16 @@ def tile_picked_zappnp_relu_po_kernel(
         quarter = held.tile([P, V], F32, name="quarter")
         nc.gpsimd.memset(quarter[:], 0.25)
 
+        def round_slot(engine_copy, dst, raw, t):
+            engine_copy(dst.rearrange("p (m j) -> p m j", j=PACK), raw[:].rearrange("p j (m t) -> p t m j", t=PACK)[:, t])
+
+        w1_b = held.tile([P, PACK * H], BF16, name="w1_b", align_bytes=64)
+        for t in range(PACK):
+            round_slot(nc.vector.tensor_copy if t < 2 else nc.scalar.copy, w1_b[:, t * H : (t + 1) * H], w1_raw, t)
+        w1_c = held.tile([P, H], U32, name="w1_c", align_bytes=64)
+        w1_s = held.tile([P, H], U8, name="w1_s", align_bytes=64)
+        nc.vector.quantize_mx(out=w1_c[:].bitcast(FP8X4), scales=w1_s[:], in_=w1_b[:])
+
         xs_g = held.tile([P, S], U8, name="xs_g", align_bytes=64)
         nc.vector.tensor_copy(xs_g[:], xs[:].indirect(offs_t[:]))
         xw_g = []
@@ -74,27 +82,11 @@ def tile_picked_zappnp_relu_po_kernel(
             nc.vector.tensor_copy(tl[:], xw[:].bitcast(U32).indirect(offs_t[:, hf * HALF // 16 : (hf + 1) * HALF // 16]))
             xw_g.append(tl)
 
-        def deal(engine_copy, grouped, raw, m0, m1):
-            engine_copy(
-                grouped[:].rearrange("p (t m j) -> p m j t", t=PACK, j=PACK)[:, m0:m1],
-                raw[:].rearrange("p j (m t) -> p m j t", t=PACK)[:, m0:m1],
-            )
-
-        w1_b = held.tile([P, PACK * H], BF16, name="w1_b", align_bytes=64)
-        deal(nc.vector.tensor_copy, w1_b, w1_raw, 0, 80)
-        deal(nc.scalar.copy, w1_b, w1_raw, 80, 128)
-        w1_c = held.tile([P, H], U32, name="w1_c", align_bytes=64)
-        w1_s = held.tile([P, H], U8, name="w1_s", align_bytes=64)
-        nc.vector.quantize_mx(out=w1_c[:].bitcast(FP8X4), scales=w1_s[:], in_=w1_b[:])
-
         def w2_slot(t, engine_copy):
-            w2_b = held.tile([P, PACK * P], BF16, name="w2_b%d" % t, align_bytes=64)
+            w2_b = held.tile([P, PACK * P], BF16, name="w2_b%d" % t, tag="w2_b0" if t == 0 else "h_b3", align_bytes=64)
             w2_c = held.tile([P, P], U32, name="w2_c%d" % t, align_bytes=64)
             w2_s = held.tile([P, P], U8, name="w2_s%d" % t, align_bytes=64)
-            engine_copy(
-                w2_b[:].rearrange("p (m j) -> p m j", j=PACK),
-                w2_raw[:].rearrange("p j (m t) -> p t m j", t=PACK)[:, t],
-            )
+            round_slot(engine_copy, w2_b[:], w2_raw, t)
             nc.vector.quantize_mx(out=w2_c[:].bitcast(FP8X4), scales=w2_s[:], in_=w2_b[:])
             return w2_c, w2_s
 
@@ -117,7 +109,7 @@ def tile_picked_zappnp_relu_po_kernel(
                     )
                 dst = h_b[:, sub * PACK * BLK : (sub + 1) * PACK * BLK].rearrange("p (n t) -> p n t", t=PACK)
                 src = bank[:].rearrange("p t n -> p n t")
-                if c0 // BLK in (1, 4, 6):
+                if c0 // BLK in (3, 6):
                     nc.vector.tensor_scalar_max(dst, src, 0.0)
                 else:
                     nc.scalar.activation(dst, src, ACT.Relu)
@@ -130,18 +122,20 @@ def tile_picked_zappnp_relu_po_kernel(
                 w2_q.append(w2_slot(t, nc.scalar.copy))
             w2_c, w2_s = w2_q[t]
             y_t = held.tile([P, S], F32, name="y%d" % t)
-            for hf in range(2):
-                bank = psum.tile([P, HALF], F32, name="bank")
+            width = QTR if t == 0 else HALF
+            for c0 in range(0, S, width):
+                hf, c = divmod(c0, HALF)
+                bank = psum.tile([P, width], F32, name="bank")
                 nc.tensor.matmul_mx(
                     out=bank[:],
                     lhsT=w2_c[:].bitcast(FP8X4), lhsT_scale=w2_s[:],
-                    rhs=h_c[hf][:].bitcast(FP8X4), rhs_scale=h_s[hf][:],
+                    rhs=h_c[hf][:, c : c + width].bitcast(FP8X4), rhs_scale=h_s[hf][:, c : c + width],
                     start=True, stop=True,
                 )
-                if t == 0 and hf == 1:
-                    nc.vector.tensor_scalar_mul(y_t[:, hf * HALF : (hf + 1) * HALF], bank[:], 0.8)
+                if t == 0 and c0 + width == S:
+                    nc.vector.tensor_scalar_mul(y_t[:, c0 : c0 + width], bank[:], 0.8)
                 else:
-                    nc.scalar.activation(y_t[:, hf * HALF : (hf + 1) * HALF], bank[:], ACT.Copy, scale=0.8)
+                    nc.scalar.activation(y_t[:, c0 : c0 + width], bank[:], ACT.Copy, scale=0.8)
             y.append(y_t)
 
         def terms(tag, width, window, lists, gates, own_window, own_list):

@@ -61,8 +61,9 @@ def tile_picked_zappnp_relu_po_kernel(
 
         ident = held.tile([P, P], F32, name="ident")
         make_identity(nc, ident[:])
-        quarter = held.tile([P, V], F32, name="quarter")
-        nc.gpsimd.memset(quarter[:], 0.25)
+        g1x4 = held.tile([P, D, V], F32, name="g1x4")
+        for d in range(D):
+            nc.gpsimd.tensor_scalar(g1x4[:, d, :], g1[:, d, :], 4.0, 0.0, MULT, ADD)
 
         def round_slot(engine_copy, dst, raw, t):
             engine_copy(dst.rearrange("p (m j) -> p m j", j=PACK), raw[:].rearrange("p j (m t) -> p t m j", t=PACK)[:, t])
@@ -133,16 +134,19 @@ def tile_picked_zappnp_relu_po_kernel(
                     start=True, stop=True,
                 )
                 if t == 0 and c0 + width == S:
-                    nc.vector.tensor_scalar_mul(y_t[:, c0 : c0 + width], bank[:], 0.8)
+                    nc.vector.tensor_scalar_mul(y_t[:, c0 : c0 + width], bank[:], 0.2)
                 else:
-                    nc.scalar.activation(y_t[:, c0 : c0 + width], bank[:], ACT.Copy, scale=0.8)
+                    nc.scalar.activation(y_t[:, c0 : c0 + width], bank[:], ACT.Copy, scale=0.2)
             y.append(y_t)
 
         def terms(tag, width, window, lists, gates, own_window, own_list):
             a = [work.tile([P, width], F32, name="%s_a%d" % (tag, d)) for d in range(D + 1)]
-            nc.vector.tensor_tensor(a[D][:], own_window[:].indirect(own_list[:]), quarter[:, :width], MULT)
-            for d in range(D):
+            for d in range(D - 1):
                 nc.vector.tensor_tensor(a[d][:], window[:].indirect(lists[d][:]), gates[:, d, :], MULT)
+            picked = work.tile([P, width], F32, name=tag + "_picked")
+            nc.vector.tensor_copy(picked[:], window[:].indirect(lists[D - 1][:]))
+            nc.gpsimd.tensor_tensor(a[D - 1][:], picked[:], gates[:, D - 1, :], MULT)
+            nc.vector.tensor_copy(a[D][:], own_window[:].indirect(own_list[:]))
             return a
 
         def add_in_psum(tag, width, a, dst, factor):
@@ -166,16 +170,18 @@ def tile_picked_zappnp_relu_po_kernel(
         out_rows = out_0.rearrange("(p t) x -> p t x", t=PACK)
         z = [held.tile([P, V], F32, name="z%d" % t) for t in range(PACK)]
         for t in range(PACK):
-            add_in_psum("z", V, terms("z", V, y[t], pos_t, g1, y[t], cen_t), z[t][:], 0.8)
+            add_in_psum("z", V, terms("z", V, y[t], pos_t, g1x4, y[t], cen_t), z[t][:], 0.8)
         for t in range(PACK):
-            a = terms("o", U, z[t], nxt_t, g2, y[t], root_t)
             if t < PACK - 1:
-                add_in_psum("o", U, a, res[:, t, :], None)
+                add_in_psum("o", U, terms("o", U, z[t], nxt_t, g2, y[t], root_t), res[:, t, :], None)
             else:
+                b = [work.tile([P, U], F32, name="last%d" % d) for d in range(D)]
+                for d in range(D):
+                    nc.vector.tensor_tensor(b[d][:], z[t][:].indirect(nxt_t[d][:]), g2[:, d, :], MULT)
                 s0 = work.tile([P, U], F32, name="s0")
                 s1 = work.tile([P, U], F32, name="s1")
-                nc.vector.tensor_tensor(s0[:], a[D][:], a[0][:], ADD)
-                nc.vector.tensor_tensor(s1[:], a[1][:], a[2][:], ADD)
+                nc.vector.tensor_tensor(s0[:], y[t][:].indirect(root_t[:]), b[0][:], ADD)
+                nc.vector.tensor_tensor(s1[:], b[1][:], b[2][:], ADD)
                 nc.vector.tensor_tensor(res[:, t, :], s0[:], s1[:], ADD)
             nc.sync.dma_start(out_rows[:, t, :], res[:, t, :])
 

@@ -22,6 +22,7 @@ PACK = 4
 HALF = S // 2
 BLK = 128
 QTR = 256
+H_PIECES = ((0, 256), (256, 256), (512, 256), (768, 128), (896, 128))
 
 
 def tile_picked_zappnp_relu_po_kernel(
@@ -31,7 +32,7 @@ def tile_picked_zappnp_relu_po_kernel(
     nc = tc.nc
     with ExitStack() as ctx:
         held = ctx.enter_context(tc.tile_pool(name="held", bufs=1))
-        work = ctx.enter_context(tc.tile_pool(name="work", bufs=2))
+        work = ctx.enter_context(tc.tile_pool(name="work", bufs=4))
         psum = ctx.enter_context(tc.psum_pool(name="psum", bufs=8))
 
         def load_list(name, src):
@@ -46,12 +47,14 @@ def tile_picked_zappnp_relu_po_kernel(
         nc.vector.memset(xs[:].bitcast(I32), 0)
         for q in range(4):
             nc.sync.dma_start(xs[32 * q : 32 * q + 4, :].bitcast(I32), x_scales[0, 4 * q : 4 * q + 4, :].bitcast(I32))
+        gate_rows = held.tile([P, P], F32, name="gate_rows")
+        nc.gpsimd.memset(gate_rows[:], 0.0)
+        pieces = D * V // P
+        nc.sync.dma_start(gate_rows[:pieces, :], gate.rearrange("d p (b c) -> (d p b) c", c=P)[0 : D * V : P + 1, :])
         xw = held.tile([P, T], I32, name="xw", align_bytes=64)
         nc.sync.dma_start(xw[:], x_words[0].rearrange("p n t -> p (n t)").bitcast(I32))
         w2_raw = held.tile([P, PACK, N], F32, name="w2_raw")
         nc.sync.dma_start(w2_raw[:], w2.rearrange("(p j) c -> p j c", j=PACK))
-        g1 = held.tile([P, D, V], F32, name="g1")
-        nc.sync.dma_start(g1[:], gate.rearrange("d p v -> p d v"))
         pos_t = [load_list("pos1_t", pos1), load_list("pos2_t", pos2), load_list("pos3_t", pos3)]
         cen_t = load_list("cen_t", cen)
         nxt_t = [load_list("nxt1_t", nxt1), load_list("nxt2_t", nxt2), load_list("nxt3_t", nxt3)]
@@ -61,9 +64,6 @@ def tile_picked_zappnp_relu_po_kernel(
 
         ident = held.tile([P, P], F32, name="ident")
         make_identity(nc, ident[:])
-        g1x4 = held.tile([P, D, V], F32, name="g1x4")
-        for d in range(D):
-            nc.gpsimd.tensor_scalar(g1x4[:, d, :], g1[:, d, :], 4.0, 0.0, MULT, ADD)
 
         def round_slot(engine_copy, dst, raw, t):
             engine_copy(dst.rearrange("p (m j) -> p m j", j=PACK), raw[:].rearrange("p j (m t) -> p t m j", t=PACK)[:, t])
@@ -75,6 +75,18 @@ def tile_picked_zappnp_relu_po_kernel(
         w1_s = held.tile([P, H], U8, name="w1_s", align_bytes=64)
         nc.vector.quantize_mx(out=w1_c[:].bitcast(FP8X4), scales=w1_s[:], in_=w1_b[:])
 
+        bank = psum.tile([P, P], F32, name="bank")
+        nc.tensor.transpose(bank[:], gate_rows[:], ident[:])
+        gate_cols = held.tile([P, pieces], F32, name="gate_cols")
+        nc.scalar.copy(gate_cols[:], bank[:, :pieces])
+        g1 = held.tile([P, D, V], F32, name="g1")
+        for d in range(D):
+            bank = psum.tile([P, V], F32, name="bank")
+            for b in range(V // P):
+                j = d * V // P + b
+                nc.tensor.transpose(bank[:, b * P : (b + 1) * P], gate_cols[:, j : j + 1].to_broadcast([P, P]), ident[:])
+            nc.scalar.activation(g1[:, d, :], bank[:], ACT.Copy, scale=4.0)
+
         xs_g = held.tile([P, S], U8, name="xs_g", align_bytes=64)
         nc.vector.tensor_copy(xs_g[:], xs[:].indirect(offs_t[:]))
         xw_g = []
@@ -84,7 +96,7 @@ def tile_picked_zappnp_relu_po_kernel(
             xw_g.append(tl)
 
         def w2_slot(t, engine_copy):
-            w2_b = held.tile([P, PACK * P], BF16, name="w2_b%d" % t, tag="w2_b0" if t == 0 else "h_b3", align_bytes=64)
+            w2_b = held.tile([P, PACK * P], BF16, name="w2_b%d" % t, tag="w2_b0" if t == 0 else "h_b896", align_bytes=64)
             w2_c = held.tile([P, P], U32, name="w2_c%d" % t, align_bytes=64)
             w2_s = held.tile([P, P], U8, name="w2_s%d" % t, align_bytes=64)
             round_slot(engine_copy, w2_b[:], w2_raw, t)
@@ -95,10 +107,10 @@ def tile_picked_zappnp_relu_po_kernel(
 
         h_c = [held.tile([P, HALF], U32, name="h_c%d" % hf, align_bytes=64) for hf in range(2)]
         h_s = [held.tile([P, HALF], U8, name="h_s%d" % hf, align_bytes=64) for hf in range(2)]
-        for qt in range(S // QTR):
-            h_b = held.tile([P, PACK * QTR], BF16, name="h_b%d" % qt, align_bytes=64)
-            for sub in range(QTR // BLK):
-                c0 = qt * QTR + sub * BLK
+        for p0, width in H_PIECES:
+            h_b = held.tile([P, PACK * width], BF16, name="h_b%d" % p0, align_bytes=64)
+            for sub in range(width // BLK):
+                c0 = p0 + sub * BLK
                 hf, c = divmod(c0, HALF)
                 bank = psum.tile([P, PACK, BLK], F32, name="bank")
                 for t in range(PACK):
@@ -110,12 +122,12 @@ def tile_picked_zappnp_relu_po_kernel(
                     )
                 dst = h_b[:, sub * PACK * BLK : (sub + 1) * PACK * BLK].rearrange("p (n t) -> p n t", t=PACK)
                 src = bank[:].rearrange("p t n -> p n t")
-                if c0 // BLK in (3, 6):
+                if c0 // BLK in (1, 5):
                     nc.vector.tensor_scalar_max(dst, src, 0.0)
                 else:
                     nc.scalar.activation(dst, src, ACT.Relu)
-            hf, c = divmod(qt * QTR, HALF)
-            nc.vector.quantize_mx(out=h_c[hf][:, c : c + QTR].bitcast(FP8X4), scales=h_s[hf][:, c : c + QTR], in_=h_b[:])
+            hf, c = divmod(p0, HALF)
+            nc.vector.quantize_mx(out=h_c[hf][:, c : c + width].bitcast(FP8X4), scales=h_s[hf][:, c : c + width], in_=h_b[:])
 
         y = []
         for t in range(PACK):
@@ -123,8 +135,7 @@ def tile_picked_zappnp_relu_po_kernel(
                 w2_q.append(w2_slot(t, nc.scalar.copy))
             w2_c, w2_s = w2_q[t]
             y_t = held.tile([P, S], F32, name="y%d" % t)
-            width = QTR if t == 0 else HALF
-            for c0 in range(0, S, width):
+            for c0, width in H_PIECES if t == 0 else ((0, HALF), (HALF, HALF)):
                 hf, c = divmod(c0, HALF)
                 bank = psum.tile([P, width], F32, name="bank")
                 nc.tensor.matmul_mx(
@@ -133,7 +144,7 @@ def tile_picked_zappnp_relu_po_kernel(
                     rhs=h_c[hf][:, c : c + width].bitcast(FP8X4), rhs_scale=h_s[hf][:, c : c + width],
                     start=True, stop=True,
                 )
-                if t == 0 and c0 + width == S:
+                if t == 0 and width == BLK:
                     nc.vector.tensor_scalar_mul(y_t[:, c0 : c0 + width], bank[:], 0.2)
                 else:
                     nc.scalar.activation(y_t[:, c0 : c0 + width], bank[:], ACT.Copy, scale=0.2)
@@ -141,20 +152,17 @@ def tile_picked_zappnp_relu_po_kernel(
 
         def terms(tag, width, window, lists, gates, own_window, own_list):
             a = [work.tile([P, width], F32, name="%s_a%d" % (tag, d)) for d in range(D + 1)]
-            for d in range(D - 1):
-                nc.vector.tensor_tensor(a[d][:], window[:].indirect(lists[d][:]), gates[:, d, :], MULT)
-            picked = work.tile([P, width], F32, name=tag + "_picked")
-            nc.vector.tensor_copy(picked[:], window[:].indirect(lists[D - 1][:]))
-            nc.gpsimd.tensor_tensor(a[D - 1][:], picked[:], gates[:, D - 1, :], MULT)
             nc.vector.tensor_copy(a[D][:], own_window[:].indirect(own_list[:]))
-            return a
+            for d in range(D):
+                nc.vector.tensor_tensor(a[d][:], window[:].indirect(lists[d][:]), gates[:, d, :], MULT)
+            return [a[D]] + a[:D]
 
         def add_in_psum(tag, width, a, dst, factor):
             turned = psum.tile([P, width], F32, name="bank")
             for b in range(width // P):
                 cols = slice(b * P, (b + 1) * P)
-                for d in range(D + 1):
-                    nc.tensor.matmul(turned[:, cols], a[d][:, cols], ident[:], start=(d == 0), stop=(d == D), is_transpose=True)
+                for d, term in enumerate(a):
+                    nc.tensor.matmul(turned[:, cols], term[:, cols], ident[:], start=(d == 0), stop=(d == len(a) - 1), is_transpose=True)
             total = work.tile([P, width], F32, name=tag + "_sum")
             nc.scalar.copy(total[:], turned[:])
             back = psum.tile([P, width], F32, name="bank")
@@ -170,19 +178,19 @@ def tile_picked_zappnp_relu_po_kernel(
         out_rows = out_0.rearrange("(p t) x -> p t x", t=PACK)
         z = [held.tile([P, V], F32, name="z%d" % t) for t in range(PACK)]
         for t in range(PACK):
-            add_in_psum("z", V, terms("z", V, y[t], pos_t, g1x4, y[t], cen_t), z[t][:], 0.8)
+            add_in_psum("z", V, terms("z", V, y[t], pos_t, g1, y[t], cen_t), z[t][:], 0.8)
         for t in range(PACK):
+            b = [work.tile([P, U], F32, name="o_b%d" % d) for d in range(D)]
+            for d in range(D):
+                nc.vector.tensor_tensor(b[d][:], z[t][:].indirect(nxt_t[d][:]), g2[:, d, :], MULT)
+            mixed = work.tile([P, U], F32, name="mixed")
             if t < PACK - 1:
-                add_in_psum("o", U, terms("o", U, z[t], nxt_t, g2, y[t], root_t), res[:, t, :], None)
+                add_in_psum("o", U, b, mixed[:], None)
             else:
-                b = [work.tile([P, U], F32, name="last%d" % d) for d in range(D)]
-                for d in range(D):
-                    nc.vector.tensor_tensor(b[d][:], z[t][:].indirect(nxt_t[d][:]), g2[:, d, :], MULT)
-                s0 = work.tile([P, U], F32, name="s0")
-                s1 = work.tile([P, U], F32, name="s1")
-                nc.vector.tensor_tensor(s0[:], y[t][:].indirect(root_t[:]), b[0][:], ADD)
-                nc.vector.tensor_tensor(s1[:], b[1][:], b[2][:], ADD)
-                nc.vector.tensor_tensor(res[:, t, :], s0[:], s1[:], ADD)
+                pair = work.tile([P, U], F32, name="pair")
+                nc.vector.tensor_tensor(pair[:], b[0][:], b[1][:], ADD)
+                nc.vector.tensor_tensor(mixed[:], pair[:], b[2][:], ADD)
+            nc.vector.tensor_tensor(res[:, t, :], y[t][:].indirect(root_t[:]), mixed[:], ADD)
             nc.sync.dma_start(out_rows[:, t, :], res[:, t, :])
 
         res_b = held.tile([P, PACK * U], BF16, name="res_b", align_bytes=64)

@@ -152,10 +152,10 @@ def tile_picked_zappnp_relu_po_kernel(
 
         def terms(tag, width, window, lists, gates, own_window, own_list):
             a = [work.tile([P, width], F32, name="%s_a%d" % (tag, d)) for d in range(D + 1)]
-            nc.vector.tensor_copy(a[D][:], own_window[:].indirect(own_list[:]))
             for d in range(D):
                 nc.vector.tensor_tensor(a[d][:], window[:].indirect(lists[d][:]), gates[:, d, :], MULT)
-            return [a[D]] + a[:D]
+            nc.vector.tensor_tensor(a[D][:], own_window[:].indirect(own_list[:]), a[0][:], ADD)
+            return a[1:]
 
         def add_in_psum(tag, width, a, dst, factor):
             turned = psum.tile([P, width], F32, name="bank")

@@ -22,7 +22,8 @@ PACK = 4
 HALF = S // 2
 BLK = 128
 QTR = 256
-H_PIECES = ((0, 256), (256, 256), (512, 256), (768, 128), (896, 128))
+WARM_UPS = 3
+H_PIECES = ((0, 512), (512, 256), (768, 128), (896, 128))
 
 
 def tile_picked_zappnp_relu_po_kernel(
@@ -50,17 +51,17 @@ def tile_picked_zappnp_relu_po_kernel(
         gate_rows = held.tile([P, P], F32, name="gate_rows")
         nc.gpsimd.memset(gate_rows[:], 0.0)
         pieces = D * V // P
-        nc.sync.dma_start(gate_rows[:pieces, :], gate.rearrange("d p (b c) -> (d p b) c", c=P)[0 : D * V : P + 1, :])
+        nc.scalar.dma_start(gate_rows[:pieces, :], gate.rearrange("d p (b c) -> (d p b) c", c=P)[0 : D * V : P + 1, :])
         xw = held.tile([P, T], I32, name="xw", align_bytes=64)
         nc.sync.dma_start(xw[:], x_words[0].rearrange("p n t -> p (n t)").bitcast(I32))
         w2_raw = held.tile([P, PACK, N], F32, name="w2_raw")
         nc.sync.dma_start(w2_raw[:], w2.rearrange("(p j) c -> p j c", j=PACK))
         pos_t = [load_list("pos1_t", pos1), load_list("pos2_t", pos2), load_list("pos3_t", pos3)]
         cen_t = load_list("cen_t", cen)
-        nxt_t = [load_list("nxt1_t", nxt1), load_list("nxt2_t", nxt2), load_list("nxt3_t", nxt3)]
-        root_t = load_list("root_t", root)
         g2 = held.tile([P, D, U], F32, name="g2")
         nc.sync.dma_start(g2[:], gate2.rearrange("d p v -> p d v"))
+        nxt_t = [load_list("nxt1_t", nxt1), load_list("nxt2_t", nxt2), load_list("nxt3_t", nxt3)]
+        root_t = load_list("root_t", root)
 
         ident = held.tile([P, P], F32, name="ident")
         make_identity(nc, ident[:])
@@ -69,8 +70,10 @@ def tile_picked_zappnp_relu_po_kernel(
             engine_copy(dst.rearrange("p (m j) -> p m j", j=PACK), raw[:].rearrange("p j (m t) -> p t m j", t=PACK)[:, t])
 
         w1_b = held.tile([P, PACK * H], BF16, name="w1_b", align_bytes=64)
-        for t in range(PACK):
-            round_slot(nc.vector.tensor_copy if t < 2 else nc.scalar.copy, w1_b[:, t * H : (t + 1) * H], w1_raw, t)
+        nc.vector.tensor_copy(
+            w1_b[:].rearrange("p (t m j) -> p m j t", t=PACK, j=PACK),
+            w1_raw[:].rearrange("p j (m t) -> p m j t", t=PACK),
+        )
         w1_c = held.tile([P, H], U32, name="w1_c", align_bytes=64)
         w1_s = held.tile([P, H], U8, name="w1_s", align_bytes=64)
         nc.vector.quantize_mx(out=w1_c[:].bitcast(FP8X4), scales=w1_s[:], in_=w1_b[:])
@@ -89,6 +92,12 @@ def tile_picked_zappnp_relu_po_kernel(
 
         xs_g = held.tile([P, S], U8, name="xs_g", align_bytes=64)
         nc.vector.tensor_copy(xs_g[:], xs[:].indirect(offs_t[:]))
+        for i in range(WARM_UPS):
+            bank = psum.tile([P, HALF], F32, name="bank")
+            nc.tensor.matmul_mx(
+                out=bank[:], lhsT=w1_c[:, :P].bitcast(FP8X4), lhsT_scale=w1_s[:, :P],
+                rhs=w1_c[:].bitcast(FP8X4), rhs_scale=xs_g[:, :HALF], start=True, stop=True,
+            )
         xw_g = []
         for hf in range(2):
             tl = held.tile([P, HALF], U32, name="xw_g%d" % hf, align_bytes=64)
@@ -122,7 +131,7 @@ def tile_picked_zappnp_relu_po_kernel(
                     )
                 dst = h_b[:, sub * PACK * BLK : (sub + 1) * PACK * BLK].rearrange("p (n t) -> p n t", t=PACK)
                 src = bank[:].rearrange("p t n -> p n t")
-                if c0 // BLK in (1, 5):
+                if c0 // BLK in (5,):
                     nc.vector.tensor_scalar_max(dst, src, 0.0)
                 else:
                     nc.scalar.activation(dst, src, ACT.Relu)
@@ -174,30 +183,50 @@ def tile_picked_zappnp_relu_po_kernel(
             else:
                 nc.scalar.activation(dst, back[:], ACT.Copy, scale=factor)
 
-        res = held.tile([P, PACK, U], F32, name="res")
         out_rows = out_0.rearrange("(p t) x -> p t x", t=PACK)
         z = [held.tile([P, V], F32, name="z%d" % t) for t in range(PACK)]
         for t in range(PACK):
-            add_in_psum("z", V, terms("z", V, y[t], pos_t, g1, y[t], cen_t), z[t][:], 0.8)
+            z_terms = terms("z", V, y[t], pos_t, g1, y[t], cen_t)
+            add_in_psum("z", V, z_terms, z[t][:], 0.8)
+        res = [held.tile([P, 2, U], F32, name="res01", tag="z3"), held.tile([P, 2, U], F32, name="res23")]
+        mixed = []
         for t in range(PACK):
             b = [work.tile([P, U], F32, name="o_b%d" % d) for d in range(D)]
             for d in range(D):
                 nc.vector.tensor_tensor(b[d][:], z[t][:].indirect(nxt_t[d][:]), g2[:, d, :], MULT)
-            mixed = work.tile([P, U], F32, name="mixed")
+            summed = b if t < PACK - 1 else b[:2]
+            turned = [psum.tile([P, P], F32, name="bank") for c in range(U // P)]
+            for d, term in enumerate(summed):
+                for c in range(U // P):
+                    nc.tensor.matmul(turned[c][:], term[:, c * P : (c + 1) * P], ident[:], start=(d == 0), stop=(d == len(summed) - 1), is_transpose=True)
             if t < PACK - 1:
-                add_in_psum("o", U, b, mixed[:], None)
+                total = work.tile([P, U], F32, name="o_sum")
             else:
-                pair = work.tile([P, U], F32, name="pair")
-                nc.vector.tensor_tensor(pair[:], b[0][:], b[1][:], ADD)
-                nc.vector.tensor_tensor(mixed[:], pair[:], b[2][:], ADD)
-            nc.vector.tensor_tensor(res[:, t, :], y[t][:].indirect(root_t[:]), mixed[:], ADD)
-            nc.sync.dma_start(out_rows[:, t, :], res[:, t, :])
+                total = held.tile([P, U], F32, name="last_sum", tag="res_b", align_bytes=64)
+            back = psum.tile([P, U], F32, name="bank")
+            for c in range(U // P):
+                cols = slice(c * P, (c + 1) * P)
+                nc.scalar.copy(total[:, cols], turned[c][:])
+                nc.tensor.transpose(back[:, cols], total[:, cols], ident[:])
+            if t < PACK - 1:
+                mixed.append(work.tile([P, U], F32, name="mixed"))
+                nc.scalar.copy(mixed[t][:], back[:])
 
         res_b = held.tile([P, PACK * U], BF16, name="res_b", align_bytes=64)
-        nc.vector.tensor_copy(
-            res_b[:].rearrange("p (c i t) -> p c t i", i=4, t=PACK),
-            res[:].rearrange("p t (c i) -> p c t i", i=4),
-        )
+        res_bv = res_b[:].rearrange("p (c t) -> p c t", t=PACK)
+        last = work.tile([P, U], F32, name="last")
+        nc.vector.tensor_tensor(last[:], y[PACK - 1][:].indirect(root_t[:]), b[D - 1][:], ADD)
+        for t in range(PACK - 1):
+            pair, s = divmod(t, 2)
+            if t == 2:
+                nc.vector.tensor_tensor(res[1][:, 1, :], last[:], back[:], ADD)
+                nc.sync.dma_start(out_rows[:, 3, :], res[1][:, 1, :])
+            nc.vector.tensor_tensor(res[pair][:, s, :], y[t][:].indirect(root_t[:]), mixed[t][:], ADD)
+            if t == 1:
+                nc.sync.dma_start(out_rows[:, 0:2, :], res[0][:])
+                nc.scalar.copy(res_bv[:, :, 0:2], res[0][:].rearrange("p t c -> p c t"))
+        nc.sync.dma_start(out_rows[:, 2, :], res[1][:, 0, :])
+        nc.vector.tensor_copy(res_bv[:, :, 2:4], res[1][:].rearrange("p t c -> p c t"))
         res_c = held.tile([P, U], I32, name="res_c", align_bytes=64)
         res_s = held.tile([P, U], U8, name="res_s", align_bytes=64)
         nc.vector.quantize_mx(out=res_c[:].bitcast(FP8X4), scales=res_s[:], in_=res_b[:])

@@ -22,7 +22,7 @@ PACK = 4
 HALF = S // 2
 BLK = 128
 QTR = 256
-WARM_UPS = 3
+WARM_UPS = 4
 H_PIECES = ((0, 512), (512, 256), (768, 128), (896, 128))
 
 
@@ -46,34 +46,40 @@ def tile_picked_zappnp_relu_po_kernel(
         nc.sync.dma_start(w1_raw[:], w1.rearrange("(p j) c -> p j c", j=PACK))
         xs = held.tile([P, T], U8, name="xs", align_bytes=64)
         nc.vector.memset(xs[:].bitcast(I32), 0)
-        for q in range(4):
-            nc.sync.dma_start(xs[32 * q : 32 * q + 4, :].bitcast(I32), x_scales[0, 4 * q : 4 * q + 4, :].bitcast(I32))
+        for hf in range(2):
+            nc.sync.dma_start(xs[64 * hf : 64 * hf + 32 : 4, :].bitcast(I32), x_scales[0, 8 * hf : 8 * hf + 8, :].bitcast(I32))
         gate_rows = held.tile([P, P], F32, name="gate_rows")
         nc.gpsimd.memset(gate_rows[:], 0.0)
         pieces = D * V // P
         nc.scalar.dma_start(gate_rows[:pieces, :], gate.rearrange("d p (b c) -> (d p b) c", c=P)[0 : D * V : P + 1, :])
         xw = held.tile([P, T], I32, name="xw", align_bytes=64)
         nc.sync.dma_start(xw[:], x_words[0].rearrange("p n t -> p (n t)").bitcast(I32))
+        xs_picked = held.tile([P, S], U8, name="xs_picked", align_bytes=64)
+        nc.vector.tensor_copy(xs_picked[:], xs[:].indirect(offs_t[:]))
+        xs_g = held.tile([P, S], U8, name="xs_g", align_bytes=64)
+        nc.gpsimd.memset(xs_g[:].bitcast(I32), 0)
+        for q in range(4):
+            first = 64 * (q // 2) + 16 * (q % 2)
+            nc.sync.dma_start(xs_g[32 * q : 32 * q + 4, :].bitcast(I32), xs_picked[first : first + 16 : 4, :].bitcast(I32))
         w2_raw = held.tile([P, PACK, N], F32, name="w2_raw")
         nc.sync.dma_start(w2_raw[:], w2.rearrange("(p j) c -> p j c", j=PACK))
         pos_t = [load_list("pos1_t", pos1), load_list("pos2_t", pos2), load_list("pos3_t", pos3)]
         cen_t = load_list("cen_t", cen)
-        g2 = held.tile([P, D, U], F32, name="g2")
-        nc.sync.dma_start(g2[:], gate2.rearrange("d p v -> p d v"))
+        g2 = [held.tile([P, U], F32, name="g2_%d" % d) for d in range(D)]
+        for d in range(D):
+            nc.sync.dma_start(g2[d][:], gate2[d])
         nxt_t = [load_list("nxt1_t", nxt1), load_list("nxt2_t", nxt2), load_list("nxt3_t", nxt3)]
         root_t = load_list("root_t", root)
 
         ident = held.tile([P, P], F32, name="ident")
         make_identity(nc, ident[:])
 
-        def round_slot(engine_copy, dst, raw, t):
-            engine_copy(dst.rearrange("p (m j) -> p m j", j=PACK), raw[:].rearrange("p j (m t) -> p t m j", t=PACK)[:, t])
-
         w1_b = held.tile([P, PACK * H], BF16, name="w1_b", align_bytes=64)
-        nc.vector.tensor_copy(
-            w1_b[:].rearrange("p (t m j) -> p m j t", t=PACK, j=PACK),
-            w1_raw[:].rearrange("p j (m t) -> p m j t", t=PACK),
-        )
+        for copy, m in ((nc.vector.tensor_copy, slice(0, P // 2)), (nc.scalar.copy, slice(P // 2, P))):
+            copy(
+                w1_b[:].rearrange("p (t m j) -> p m j t", t=PACK, j=PACK)[:, m],
+                w1_raw[:].rearrange("p j (m t) -> p m j t", t=PACK)[:, m],
+            )
         w1_c = held.tile([P, H], U32, name="w1_c", align_bytes=64)
         w1_s = held.tile([P, H], U8, name="w1_s", align_bytes=64)
         nc.vector.quantize_mx(out=w1_c[:].bitcast(FP8X4), scales=w1_s[:], in_=w1_b[:])
@@ -90,13 +96,11 @@ def tile_picked_zappnp_relu_po_kernel(
                 nc.tensor.transpose(bank[:, b * P : (b + 1) * P], gate_cols[:, j : j + 1].to_broadcast([P, P]), ident[:])
             nc.scalar.activation(g1[:, d, :], bank[:], ACT.Copy, scale=4.0)
 
-        xs_g = held.tile([P, S], U8, name="xs_g", align_bytes=64)
-        nc.vector.tensor_copy(xs_g[:], xs[:].indirect(offs_t[:]))
         for i in range(WARM_UPS):
             bank = psum.tile([P, HALF], F32, name="bank")
             nc.tensor.matmul_mx(
                 out=bank[:], lhsT=w1_c[:, :P].bitcast(FP8X4), lhsT_scale=w1_s[:, :P],
-                rhs=w1_c[:].bitcast(FP8X4), rhs_scale=xs_g[:, :HALF], start=True, stop=True,
+                rhs=w1_c[:].bitcast(FP8X4), rhs_scale=w1_s[:], start=True, stop=True,
             )
         xw_g = []
         for hf in range(2):
@@ -104,15 +108,18 @@ def tile_picked_zappnp_relu_po_kernel(
             nc.vector.tensor_copy(tl[:], xw[:].bitcast(U32).indirect(offs_t[:, hf * HALF // 16 : (hf + 1) * HALF // 16]))
             xw_g.append(tl)
 
-        def w2_slot(t, engine_copy):
-            w2_b = held.tile([P, PACK * P], BF16, name="w2_b%d" % t, tag="w2_b0" if t == 0 else "h_b896", align_bytes=64)
-            w2_c = held.tile([P, P], U32, name="w2_c%d" % t, align_bytes=64)
-            w2_s = held.tile([P, P], U8, name="w2_s%d" % t, align_bytes=64)
-            round_slot(engine_copy, w2_b[:], w2_raw, t)
+        def w2_pair(pair, engine_copy, tag):
+            w2_b = held.tile([P, 2 * PACK * P], BF16, name="w2_b%d" % pair, tag=tag, align_bytes=64)
+            w2_c = held.tile([P, 2 * P], U32, name="w2_c%d" % pair, align_bytes=64)
+            w2_s = held.tile([P, 2 * P], U8, name="w2_s%d" % pair, align_bytes=64)
+            engine_copy(
+                w2_b[:].rearrange("p (t m j) -> p m j t", t=2, j=PACK),
+                w2_raw[:].rearrange("p j (m t) -> p m j t", t=PACK)[:, :, :, 2 * pair : 2 * pair + 2],
+            )
             nc.vector.quantize_mx(out=w2_c[:].bitcast(FP8X4), scales=w2_s[:], in_=w2_b[:])
             return w2_c, w2_s
 
-        w2_q = [w2_slot(0, nc.vector.tensor_copy)]
+        w2_q = [w2_pair(0, nc.vector.tensor_copy, "w2_b0")]
 
         h_c = [held.tile([P, HALF], U32, name="h_c%d" % hf, align_bytes=64) for hf in range(2)]
         h_s = [held.tile([P, HALF], U8, name="h_s%d" % hf, align_bytes=64) for hf in range(2)]
@@ -131,7 +138,7 @@ def tile_picked_zappnp_relu_po_kernel(
                     )
                 dst = h_b[:, sub * PACK * BLK : (sub + 1) * PACK * BLK].rearrange("p (n t) -> p n t", t=PACK)
                 src = bank[:].rearrange("p t n -> p n t")
-                if c0 // BLK in (5,):
+                if c0 // BLK in (4,):
                     nc.vector.tensor_scalar_max(dst, src, 0.0)
                 else:
                     nc.scalar.activation(dst, src, ACT.Relu)
@@ -140,84 +147,84 @@ def tile_picked_zappnp_relu_po_kernel(
 
         y = []
         for t in range(PACK):
-            if t > 0:
-                w2_q.append(w2_slot(t, nc.scalar.copy))
-            w2_c, w2_s = w2_q[t]
-            y_t = held.tile([P, S], F32, name="y%d" % t)
+            if t == 1:
+                w2_q.append(w2_pair(1, nc.scalar.copy, "h_b896"))
+            w2_c, w2_s = w2_q[t // 2]
+            rows = slice(t % 2 * P, (t % 2 + 1) * P)
+            y_t = held.tile([P, S], F32, name="y%d" % t, tag="w2_raw" if t == 1 else "y%d" % t)
             for c0, width in H_PIECES if t == 0 else ((0, HALF), (HALF, HALF)):
                 hf, c = divmod(c0, HALF)
                 bank = psum.tile([P, width], F32, name="bank")
                 nc.tensor.matmul_mx(
                     out=bank[:],
-                    lhsT=w2_c[:].bitcast(FP8X4), lhsT_scale=w2_s[:],
+                    lhsT=w2_c[:, rows].bitcast(FP8X4), lhsT_scale=w2_s[:, rows],
                     rhs=h_c[hf][:, c : c + width].bitcast(FP8X4), rhs_scale=h_s[hf][:, c : c + width],
                     start=True, stop=True,
                 )
-                if t == 0 and width == BLK:
+                if t == 0 and c0 >= HALF:
                     nc.vector.tensor_scalar_mul(y_t[:, c0 : c0 + width], bank[:], 0.2)
                 else:
                     nc.scalar.activation(y_t[:, c0 : c0 + width], bank[:], ACT.Copy, scale=0.2)
             y.append(y_t)
 
-        def terms(tag, width, window, lists, gates, own_window, own_list):
-            a = [work.tile([P, width], F32, name="%s_a%d" % (tag, d)) for d in range(D + 1)]
+        def terms(tag, width, window, lists, gates, own_window, own_list, first):
+            a = [
+                held.tile([P, width], F32, name="first_a2", tag="h_b896", align_bytes=64) if first and d == D - 1
+                else work.tile([P, width], F32, name="%s_a%d" % (tag, d))
+                for d in range(D + 1)
+            ]
             for d in range(D):
                 nc.vector.tensor_tensor(a[d][:], window[:].indirect(lists[d][:]), gates[:, d, :], MULT)
             nc.vector.tensor_tensor(a[D][:], own_window[:].indirect(own_list[:]), a[0][:], ADD)
             return a[1:]
 
-        def add_in_psum(tag, width, a, dst, factor):
-            turned = psum.tile([P, width], F32, name="bank")
-            for b in range(width // P):
-                cols = slice(b * P, (b + 1) * P)
+        def add_in_psum(a, width, total, bank_each):
+            blocks = [slice(b * P, (b + 1) * P) for b in range(width // P)]
+            last = len(a) - 1
+            if bank_each:
+                turned = [psum.tile([P, P], F32, name="bank") for cols in blocks]
                 for d, term in enumerate(a):
-                    nc.tensor.matmul(turned[:, cols], term[:, cols], ident[:], start=(d == 0), stop=(d == len(a) - 1), is_transpose=True)
-            total = work.tile([P, width], F32, name=tag + "_sum")
-            nc.scalar.copy(total[:], turned[:])
-            back = psum.tile([P, width], F32, name="bank")
-            for b in range(width // P):
-                cols = slice(b * P, (b + 1) * P)
-                nc.tensor.transpose(back[:, cols], total[:, cols], ident[:])
-            if factor is None:
-                nc.scalar.copy(dst, back[:])
+                    for bank, cols in zip(turned, blocks):
+                        nc.tensor.matmul(bank[:], term[:, cols], ident[:], start=(d == 0), stop=(d == last), is_transpose=True)
+                for bank, cols in zip(turned, blocks):
+                    nc.scalar.copy(total[:, cols], bank[:])
             else:
-                nc.scalar.activation(dst, back[:], ACT.Copy, scale=factor)
+                turned = psum.tile([P, width], F32, name="bank")
+                for cols in blocks:
+                    for d, term in enumerate(a):
+                        nc.tensor.matmul(turned[:, cols], term[:, cols], ident[:], start=(d == 0), stop=(d == last), is_transpose=True)
+                nc.scalar.copy(total[:], turned[:])
+            back = psum.tile([P, width], F32, name="bank")
+            for cols in blocks:
+                nc.tensor.transpose(back[:, cols], total[:, cols], ident[:])
+            return back
 
         out_rows = out_0.rearrange("(p t) x -> p t x", t=PACK)
         z = [held.tile([P, V], F32, name="z%d" % t) for t in range(PACK)]
         for t in range(PACK):
-            z_terms = terms("z", V, y[t], pos_t, g1, y[t], cen_t)
-            add_in_psum("z", V, z_terms, z[t][:], 0.8)
-        res = [held.tile([P, 2, U], F32, name="res01", tag="z3"), held.tile([P, 2, U], F32, name="res23")]
+            z_terms = terms("z", V, y[t], pos_t, g1, y[t], cen_t, t == 0)
+            back = add_in_psum(z_terms, V, work.tile([P, V], F32, name="z_sum"), t == PACK - 1)
+            nc.scalar.activation(z[t][:], back[:], ACT.Copy, scale=0.8)
+        res = [held.tile([P, 2, U], F32, name="res01", tag="g2_1"), held.tile([P, 2, U], F32, name="res23")]
         mixed = []
         for t in range(PACK):
             b = [work.tile([P, U], F32, name="o_b%d" % d) for d in range(D)]
             for d in range(D):
-                nc.vector.tensor_tensor(b[d][:], z[t][:].indirect(nxt_t[d][:]), g2[:, d, :], MULT)
-            summed = b if t < PACK - 1 else b[:2]
-            turned = [psum.tile([P, P], F32, name="bank") for c in range(U // P)]
-            for d, term in enumerate(summed):
-                for c in range(U // P):
-                    nc.tensor.matmul(turned[c][:], term[:, c * P : (c + 1) * P], ident[:], start=(d == 0), stop=(d == len(summed) - 1), is_transpose=True)
+                nc.vector.tensor_tensor(b[d][:], z[t][:].indirect(nxt_t[d][:]), g2[d][:], MULT)
             if t < PACK - 1:
-                total = work.tile([P, U], F32, name="o_sum")
-            else:
-                total = held.tile([P, U], F32, name="last_sum", tag="res_b", align_bytes=64)
-            back = psum.tile([P, U], F32, name="bank")
-            for c in range(U // P):
-                cols = slice(c * P, (c + 1) * P)
-                nc.scalar.copy(total[:, cols], turned[c][:])
-                nc.tensor.transpose(back[:, cols], total[:, cols], ident[:])
-            if t < PACK - 1:
+                back = add_in_psum(b, U, work.tile([P, U], F32, name="o_sum"), True)
                 mixed.append(work.tile([P, U], F32, name="mixed"))
                 nc.scalar.copy(mixed[t][:], back[:])
+            else:
+                back = add_in_psum(b[:2], U, held.tile([P, U], F32, name="last_sum", tag="res_b", align_bytes=64), True)
 
         res_b = held.tile([P, PACK * U], BF16, name="res_b", align_bytes=64)
         res_bv = res_b[:].rearrange("p (c t) -> p c t", t=PACK)
         last = work.tile([P, U], F32, name="last")
-        nc.vector.tensor_tensor(last[:], y[PACK - 1][:].indirect(root_t[:]), b[D - 1][:], ADD)
         for t in range(PACK - 1):
             pair, s = divmod(t, 2)
+            if t == 1:
+                nc.vector.tensor_tensor(last[:], y[PACK - 1][:].indirect(root_t[:]), b[D - 1][:], ADD)
             if t == 2:
                 nc.vector.tensor_tensor(res[1][:, 1, :], last[:], back[:], ADD)
                 nc.sync.dma_start(out_rows[:, 3, :], res[1][:, 1, :])

@@ -21,9 +21,11 @@ P = 128
 PACK = 4
 HALF = S // 2
 BLK = 128
-QTR = 256
+RELU_BLOCKS = ((0, 128), (128, 128), (448, 64), (256, 128), (384, 64), (512, 128), (640, 128), (768, 128), (896, 128))
+RELU_ON_VECTOR = (448, 512)
 WARM_UPS = 4
-H_PIECES = ((0, 512), (512, 256), (768, 128), (896, 128))
+H_PIECES = ((0, 256), (256, 256), (512, 256), (768, 128), (896, 128))
+Y_PIECES = ((0, 512), (512, 256), (768, 128), (896, 128))
 
 
 def tile_picked_zappnp_relu_po_kernel(
@@ -108,51 +110,56 @@ def tile_picked_zappnp_relu_po_kernel(
             nc.vector.tensor_copy(tl[:], xw[:].bitcast(U32).indirect(offs_t[:, hf * HALF // 16 : (hf + 1) * HALF // 16]))
             xw_g.append(tl)
 
-        def w2_pair(pair, engine_copy, tag):
+        def round_w2_pair(pair, engine_copy, tag):
             w2_b = held.tile([P, 2 * PACK * P], BF16, name="w2_b%d" % pair, tag=tag, align_bytes=64)
-            w2_c = held.tile([P, 2 * P], U32, name="w2_c%d" % pair, align_bytes=64)
-            w2_s = held.tile([P, 2 * P], U8, name="w2_s%d" % pair, align_bytes=64)
             engine_copy(
                 w2_b[:].rearrange("p (t m j) -> p m j t", t=2, j=PACK),
                 w2_raw[:].rearrange("p j (m t) -> p m j t", t=PACK)[:, :, :, 2 * pair : 2 * pair + 2],
             )
+            return w2_b
+
+        def quantise_w2_pair(pair, w2_b):
+            w2_c = held.tile([P, 2 * P], U32, name="w2_c%d" % pair, align_bytes=64)
+            w2_s = held.tile([P, 2 * P], U8, name="w2_s%d" % pair, align_bytes=64)
             nc.vector.quantize_mx(out=w2_c[:].bitcast(FP8X4), scales=w2_s[:], in_=w2_b[:])
             return w2_c, w2_s
 
-        w2_q = [w2_pair(0, nc.vector.tensor_copy, "w2_b0")]
+        w2_first = round_w2_pair(0, nc.vector.tensor_copy, "w2_b0")
+        w2_q = []
 
         h_c = [held.tile([P, HALF], U32, name="h_c%d" % hf, align_bytes=64) for hf in range(2)]
         h_s = [held.tile([P, HALF], U8, name="h_s%d" % hf, align_bytes=64) for hf in range(2)]
         for p0, width in H_PIECES:
             h_b = held.tile([P, PACK * width], BF16, name="h_b%d" % p0, align_bytes=64)
-            for sub in range(width // BLK):
-                c0 = p0 + sub * BLK
+            for c0, n in [blk for blk in RELU_BLOCKS if p0 <= blk[0] < p0 + width]:
                 hf, c = divmod(c0, HALF)
-                bank = psum.tile([P, PACK, BLK], F32, name="bank")
+                bank = psum.tile([P, PACK, n], F32, name="bank")
                 for t in range(PACK):
                     nc.tensor.matmul_mx(
                         out=bank[:, t, :],
                         lhsT=w1_c[:, t * P : (t + 1) * P].bitcast(FP8X4), lhsT_scale=w1_s[:, t * P : (t + 1) * P],
-                        rhs=xw_g[hf][:, c : c + BLK].bitcast(FP8X4), rhs_scale=xs_g[:, c0 : c0 + BLK],
+                        rhs=xw_g[hf][:, c : c + n].bitcast(FP8X4), rhs_scale=xs_g[:, c0 : c0 + n],
                         start=True, stop=True,
                     )
-                dst = h_b[:, sub * PACK * BLK : (sub + 1) * PACK * BLK].rearrange("p (n t) -> p n t", t=PACK)
+                dst = h_b[:, PACK * (c0 - p0) : PACK * (c0 - p0 + n)].rearrange("p (n t) -> p n t", t=PACK)
                 src = bank[:].rearrange("p t n -> p n t")
-                if c0 // BLK in (4,):
+                if c0 in RELU_ON_VECTOR:
                     nc.vector.tensor_scalar_max(dst, src, 0.0)
                 else:
                     nc.scalar.activation(dst, src, ACT.Relu)
             hf, c = divmod(p0, HALF)
             nc.vector.quantize_mx(out=h_c[hf][:, c : c + width].bitcast(FP8X4), scales=h_s[hf][:, c : c + width], in_=h_b[:])
+            if p0 == 0:
+                w2_q.append(quantise_w2_pair(0, w2_first))
 
         y = []
         for t in range(PACK):
             if t == 1:
-                w2_q.append(w2_pair(1, nc.scalar.copy, "h_b896"))
+                w2_q.append(quantise_w2_pair(1, round_w2_pair(1, nc.scalar.copy, "h_b896")))
             w2_c, w2_s = w2_q[t // 2]
             rows = slice(t % 2 * P, (t % 2 + 1) * P)
             y_t = held.tile([P, S], F32, name="y%d" % t, tag="w2_raw" if t == 1 else "y%d" % t)
-            for c0, width in H_PIECES if t == 0 else ((0, HALF), (HALF, HALF)):
+            for c0, width in Y_PIECES if t == 0 else ((0, HALF), (HALF, HALF)):
                 hf, c = divmod(c0, HALF)
                 bank = psum.tile([P, width], F32, name="bank")
                 nc.tensor.matmul_mx(
@@ -161,24 +168,24 @@ def tile_picked_zappnp_relu_po_kernel(
                     rhs=h_c[hf][:, c : c + width].bitcast(FP8X4), rhs_scale=h_s[hf][:, c : c + width],
                     start=True, stop=True,
                 )
-                if t == 0 and c0 >= HALF:
+                if t == 0 and HALF <= c0 < S - BLK:
                     nc.vector.tensor_scalar_mul(y_t[:, c0 : c0 + width], bank[:], 0.2)
                 else:
                     nc.scalar.activation(y_t[:, c0 : c0 + width], bank[:], ACT.Copy, scale=0.2)
             y.append(y_t)
 
-        def terms(tag, width, window, lists, gates, own_window, own_list, first):
-            a = [
-                held.tile([P, width], F32, name="first_a2", tag="h_b896", align_bytes=64) if first and d == D - 1
-                else work.tile([P, width], F32, name="%s_a%d" % (tag, d))
-                for d in range(D + 1)
-            ]
+        def terms(tag, width, window, lists, gates, own_window, own_list):
+            a = [work.tile([P, width], F32, name="%s_a%d" % (tag, d)) for d in range(D + 1)]
             for d in range(D):
                 nc.vector.tensor_tensor(a[d][:], window[:].indirect(lists[d][:]), gates[:, d, :], MULT)
             nc.vector.tensor_tensor(a[D][:], own_window[:].indirect(own_list[:]), a[0][:], ADD)
             return a[1:]
 
-        def add_in_psum(a, width, total, bank_each):
+        def in_blocks(tl, width):
+            return [tl[:, b * P : (b + 1) * P] for b in range(width // P)]
+
+        def add_in_psum(a, totals, bank_each, total=None):
+            width = P * len(totals)
             blocks = [slice(b * P, (b + 1) * P) for b in range(width // P)]
             last = len(a) - 1
             if bank_each:
@@ -186,8 +193,8 @@ def tile_picked_zappnp_relu_po_kernel(
                 for d, term in enumerate(a):
                     for bank, cols in zip(turned, blocks):
                         nc.tensor.matmul(bank[:], term[:, cols], ident[:], start=(d == 0), stop=(d == last), is_transpose=True)
-                for bank, cols in zip(turned, blocks):
-                    nc.scalar.copy(total[:, cols], bank[:])
+                for bank, part in zip(turned, totals):
+                    nc.scalar.copy(part, bank[:])
             else:
                 turned = psum.tile([P, width], F32, name="bank")
                 for cols in blocks:
@@ -195,15 +202,16 @@ def tile_picked_zappnp_relu_po_kernel(
                         nc.tensor.matmul(turned[:, cols], term[:, cols], ident[:], start=(d == 0), stop=(d == last), is_transpose=True)
                 nc.scalar.copy(total[:], turned[:])
             back = psum.tile([P, width], F32, name="bank")
-            for cols in blocks:
-                nc.tensor.transpose(back[:, cols], total[:, cols], ident[:])
+            for cols, part in zip(blocks, totals):
+                nc.tensor.transpose(back[:, cols], part, ident[:])
             return back
 
         out_rows = out_0.rearrange("(p t) x -> p t x", t=PACK)
         z = [held.tile([P, V], F32, name="z%d" % t) for t in range(PACK)]
         for t in range(PACK):
-            z_terms = terms("z", V, y[t], pos_t, g1, y[t], cen_t, t == 0)
-            back = add_in_psum(z_terms, V, work.tile([P, V], F32, name="z_sum"), t == PACK - 1)
+            z_terms = terms("z", V, y[t], pos_t, g1, y[t], cen_t)
+            z_sum = work.tile([P, V], F32, name="z_sum")
+            back = add_in_psum(z_terms, in_blocks(z_sum, V), True) if t == PACK - 1 else add_in_psum(z_terms, in_blocks(z_sum, V), False, z_sum)
             nc.scalar.activation(z[t][:], back[:], ACT.Copy, scale=0.8)
         res = [held.tile([P, 2, U], F32, name="res01", tag="g2_1"), held.tile([P, 2, U], F32, name="res23")]
         mixed = []
@@ -212,32 +220,37 @@ def tile_picked_zappnp_relu_po_kernel(
             for d in range(D):
                 nc.vector.tensor_tensor(b[d][:], z[t][:].indirect(nxt_t[d][:]), g2[d][:], MULT)
             if t < PACK - 1:
-                back = add_in_psum(b, U, work.tile([P, U], F32, name="o_sum"), True)
+                back = add_in_psum(b, in_blocks(work.tile([P, U], F32, name="o_sum"), U), True)
                 mixed.append(work.tile([P, U], F32, name="mixed"))
                 nc.scalar.copy(mixed[t][:], back[:])
             else:
-                back = add_in_psum(b[:2], U, held.tile([P, U], F32, name="last_sum", tag="res_b", align_bytes=64), True)
+                last_sum = [held.tile([P, P], F32, name="last_sum%d" % c, tag="res_b%d" % c, align_bytes=64)[:] for c in range(U // P)]
+                back = add_in_psum(b[1:], last_sum, True)
 
-        res_b = held.tile([P, PACK * U], BF16, name="res_b", align_bytes=64)
-        res_bv = res_b[:].rearrange("p (c t) -> p c t", t=PACK)
+        halves = (slice(0, U // 2), slice(U // 2, U))
+        res_b = [held.tile([P, PACK * U // 2], BF16, name="res_b%d" % c, align_bytes=64) for c in range(2)]
+        res_bv = [tl[:].rearrange("p (c t) -> p c t", t=PACK) for tl in res_b]
         last = work.tile([P, U], F32, name="last")
         for t in range(PACK - 1):
             pair, s = divmod(t, 2)
             if t == 1:
-                nc.vector.tensor_tensor(last[:], y[PACK - 1][:].indirect(root_t[:]), b[D - 1][:], ADD)
+                nc.vector.tensor_tensor(last[:], y[PACK - 1][:].indirect(root_t[:]), b[0][:], ADD)
             if t == 2:
                 nc.vector.tensor_tensor(res[1][:, 1, :], last[:], back[:], ADD)
                 nc.sync.dma_start(out_rows[:, 3, :], res[1][:, 1, :])
             nc.vector.tensor_tensor(res[pair][:, s, :], y[t][:].indirect(root_t[:]), mixed[t][:], ADD)
             if t == 1:
                 nc.sync.dma_start(out_rows[:, 0:2, :], res[0][:])
-                nc.scalar.copy(res_bv[:, :, 0:2], res[0][:].rearrange("p t c -> p c t"))
+                for dst, cols in zip(res_bv, halves):
+                    nc.scalar.copy(dst[:, :, 0:2], res[0][:].rearrange("p t c -> p c t")[:, cols])
         nc.sync.dma_start(out_rows[:, 2, :], res[1][:, 0, :])
-        nc.vector.tensor_copy(res_bv[:, :, 2:4], res[1][:].rearrange("p t c -> p c t"))
         res_c = held.tile([P, U], I32, name="res_c", align_bytes=64)
         res_s = held.tile([P, U], U8, name="res_s", align_bytes=64)
-        nc.vector.quantize_mx(out=res_c[:].bitcast(FP8X4), scales=res_s[:], in_=res_b[:])
-        nc.sync.dma_start(out_1[0].rearrange("p n t -> p (n t)").bitcast(I32), res_c[:])
+        for copy, dst, cols in zip((nc.scalar.copy, nc.vector.tensor_copy), res_bv, halves):
+            copy(dst[:, :, 2:4], res[1][:].rearrange("p t c -> p c t")[:, cols])
+        for rounded, cols in zip(res_b, halves):
+            nc.vector.quantize_mx(out=res_c[:, cols].bitcast(FP8X4), scales=res_s[:, cols], in_=rounded[:])
+            nc.sync.dma_start(out_1[0].rearrange("p n t -> p (n t)").bitcast(I32)[:, cols], res_c[:, cols])
         for q in range(4):
-            eng = nc.scalar if q % 2 else nc.sync
+            eng = nc.sync if q == 3 else nc.scalar
             eng.dma_start(out_2[0, 4 * q : 4 * q + 4, :].bitcast(I32), res_s[32 * q : 32 * q + 4, :].bitcast(I32))

@@ -59,7 +59,7 @@ def tile_picked_zappnp_relu_po_kernel(
         xs_picked = held.tile([P, S], U8, name="xs_picked", align_bytes=64)
         nc.vector.tensor_copy(xs_picked[:], xs[:].indirect(offs_t[:]))
         xs_g = held.tile([P, S], U8, name="xs_g", align_bytes=64)
-        nc.gpsimd.memset(xs_g[:].bitcast(I32), 0)
+        nc.vector.memset(xs_g[:].bitcast(I32), 0)
         for q in range(4):
             first = 64 * (q // 2) + 16 * (q % 2)
             nc.sync.dma_start(xs_g[32 * q : 32 * q + 4, :].bitcast(I32), xs_picked[first : first + 16 : 4, :].bitcast(I32))
@@ -74,10 +74,11 @@ def tile_picked_zappnp_relu_po_kernel(
         root_t = load_list("root_t", root)
 
         ident = held.tile([P, P], F32, name="ident")
-        make_identity(nc, ident[:])
+        nc.vector.memset(ident[:], 0.0)
+        make_identity(nc, ident[:], nomemset=True)
 
         w1_b = held.tile([P, PACK * H], BF16, name="w1_b", align_bytes=64)
-        for copy, m in ((nc.vector.tensor_copy, slice(0, P // 2)), (nc.scalar.copy, slice(P // 2, P))):
+        for copy, m in ((nc.vector.tensor_copy, slice(0, P // 4)), (nc.scalar.copy, slice(P // 4, P))):
             copy(
                 w1_b[:].rearrange("p (t m j) -> p m j t", t=PACK, j=PACK)[:, m],
                 w1_raw[:].rearrange("p j (m t) -> p m j t", t=PACK)[:, m],

@@ -221,8 +221,8 @@ def tile_picked_zappnp_relu_po_kernel(
             for d in range(D):
                 nc.vector.tensor_tensor(b[d][:], z[t][:].indirect(nxt_t[d][:]), g2[d][:], MULT)
             if t < PACK - 1:
-                back = add_in_psum(b, in_blocks(work.tile([P, U], F32, name="o_sum"), U), True)
-                mixed.append(work.tile([P, U], F32, name="mixed"))
+                back = add_in_psum(b, in_blocks(held.tile([P, U], F32, name="o_sum%d" % t), U), True)
+                mixed.append(held.tile([P, U], F32, name="mixed%d" % t))
                 nc.scalar.copy(mixed[t][:], back[:])
             else:
                 last_sum = [held.tile([P, P], F32, name="last_sum%d" % c, tag="res_b%d" % c, align_bytes=64)[:] for c in range(U // P)]

@@ -35,8 +35,8 @@ def tile_picked_zappnp_relu_po_kernel(
     nc = tc.nc
     with ExitStack() as ctx:
         held = ctx.enter_context(tc.tile_pool(name="held", bufs=1))
-        work = ctx.enter_context(tc.tile_pool(name="work", bufs=4))
-        psum = ctx.enter_context(tc.psum_pool(name="psum", bufs=8))
+        psum = ctx.enter_context(tc.psum_pool(name="psum", bufs=6))
+        sums = ctx.enter_context(tc.psum_pool(name="sums", bufs=1))
 
         def load_list(name, src):
             tl = held.tile(list(src.shape), U16, name=name)
@@ -91,13 +91,13 @@ def tile_picked_zappnp_relu_po_kernel(
         nc.tensor.transpose(bank[:], gate_rows[:], ident[:])
         gate_cols = held.tile([P, pieces], F32, name="gate_cols")
         nc.scalar.copy(gate_cols[:], bank[:, :pieces])
-        g1 = held.tile([P, D, V], F32, name="g1")
+        g1 = [held.tile([P, V], F32, name="g1_%d" % d) for d in range(D)]
         for d in range(D):
             bank = psum.tile([P, V], F32, name="bank")
             for b in range(V // P):
                 j = d * V // P + b
                 nc.tensor.transpose(bank[:, b * P : (b + 1) * P], gate_cols[:, j : j + 1].to_broadcast([P, P]), ident[:])
-            nc.scalar.activation(g1[:, d, :], bank[:], ACT.Copy, scale=4.0)
+            nc.scalar.activation(g1[d][:], bank[:], ACT.Copy, scale=4.0)
 
         for i in range(WARM_UPS):
             bank = psum.tile([P, HALF], F32, name="bank")
@@ -153,13 +153,11 @@ def tile_picked_zappnp_relu_po_kernel(
             if p0 == 0:
                 w2_q.append(quantise_w2_pair(0, w2_first))
 
-        y = []
-        for t in range(PACK):
-            if t == 1:
-                w2_q.append(quantise_w2_pair(1, round_w2_pair(1, nc.scalar.copy, "h_b896")))
+        y = [held.tile([P, S], F32, name="y%d" % t, tag="w2_raw" if t == 1 else "y%d" % t) for t in range(PACK)]
+
+        def second_product(t):
             w2_c, w2_s = w2_q[t // 2]
             rows = slice(t % 2 * P, (t % 2 + 1) * P)
-            y_t = held.tile([P, S], F32, name="y%d" % t, tag="w2_raw" if t == 1 else "y%d" % t)
             for c0, width in Y_PIECES if t == 0 else ((0, HALF), (HALF, HALF)):
                 hf, c = divmod(c0, HALF)
                 bank = psum.tile([P, width], F32, name="bank")
@@ -170,81 +168,106 @@ def tile_picked_zappnp_relu_po_kernel(
                     start=True, stop=True,
                 )
                 if t == 0 and HALF <= c0 < S - BLK:
-                    nc.vector.tensor_scalar_mul(y_t[:, c0 : c0 + width], bank[:], 0.2)
+                    nc.vector.tensor_scalar_mul(y[t][:, c0 : c0 + width], bank[:], 0.2)
                 else:
-                    nc.scalar.activation(y_t[:, c0 : c0 + width], bank[:], ACT.Copy, scale=0.2)
-            y.append(y_t)
+                    nc.scalar.activation(y[t][:, c0 : c0 + width], bank[:], ACT.Copy, scale=0.2)
 
-        def terms(tag, width, window, lists, gates, own_window, own_list):
-            a = [work.tile([P, width], F32, name="%s_a%d" % (tag, d)) for d in range(D + 1)]
-            for d in range(D):
-                nc.vector.tensor_tensor(a[d][:], window[:].indirect(lists[d][:]), gates[:, d, :], MULT)
-            nc.vector.tensor_tensor(a[D][:], own_window[:].indirect(own_list[:]), a[0][:], ADD)
-            return a[1:]
+        def plain_gather(name, window, offsets, width):
+            term = held.tile([P, width], F32, name=name)
+            nc.scalar.activation(term[:], window[:].indirect(offsets[:]), ACT.Copy)
+            return term
 
-        def in_blocks(tl, width):
-            return [tl[:, b * P : (b + 1) * P] for b in range(width // P)]
+        def gated_gather(name, window, offsets, gates, width, tag=None):
+            term = held.tile([P, width], F32, name=name, tag=tag or name)
+            nc.vector.tensor_tensor(term[:], window[:].indirect(offsets[:]), gates, MULT)
+            return term
 
-        def add_in_psum(a, totals, bank_each, total=None):
-            width = P * len(totals)
+        def turn_and_add(terms, width, side):
+            turned = sums.tile([P, width], F32, name="turned", tag="sum_%d" % side)
             blocks = [slice(b * P, (b + 1) * P) for b in range(width // P)]
-            last = len(a) - 1
-            if bank_each:
-                turned = [psum.tile([P, P], F32, name="bank") for cols in blocks]
-                for d, term in enumerate(a):
-                    for bank, cols in zip(turned, blocks):
-                        nc.tensor.matmul(bank[:], term[:, cols], ident[:], start=(d == 0), stop=(d == last), is_transpose=True)
-                for bank, part in zip(turned, totals):
-                    nc.scalar.copy(part, bank[:])
-            else:
-                turned = psum.tile([P, width], F32, name="bank")
-                for cols in blocks:
-                    for d, term in enumerate(a):
-                        nc.tensor.matmul(turned[:, cols], term[:, cols], ident[:], start=(d == 0), stop=(d == last), is_transpose=True)
-                nc.scalar.copy(total[:], turned[:])
-            back = psum.tile([P, width], F32, name="bank")
-            for cols, part in zip(blocks, totals):
-                nc.tensor.transpose(back[:, cols], part, ident[:])
+            for d, term in enumerate(terms):
+                for b, cols in enumerate(blocks):
+                    nc.tensor.matmul(
+                        turned[:, cols], term[:, cols], ident[:], is_transpose=True,
+                        start=(d == 0 and b == 0), stop=(d == len(terms) - 1 and b == len(blocks) - 1),
+                    )
+            return turned
+
+        def turn_back(name, turned, width, back):
+            total = held.tile([P, width], F32, name=name)
+            nc.scalar.copy(total[:], turned[:])
+            for b in range(width // P):
+                cols = slice(b * P, (b + 1) * P)
+                nc.tensor.transpose(back[:, cols], total[:, cols], ident[:])
             return back
 
-        out_rows = out_0.rearrange("(p t) x -> p t x", t=PACK)
-        z = [held.tile([P, V], F32, name="z%d" % t) for t in range(PACK)]
-        for t in range(PACK):
-            z_terms = terms("z", V, y[t], pos_t, g1, y[t], cen_t)
-            z_sum = work.tile([P, V], F32, name="z_sum")
-            back = add_in_psum(z_terms, in_blocks(z_sum, V), True) if t == PACK - 1 else add_in_psum(z_terms, in_blocks(z_sum, V), False, z_sum)
-            nc.scalar.activation(z[t][:], back[:], ACT.Copy, scale=0.8)
-        res = [held.tile([P, 2, U], F32, name="res01", tag="g2_1"), held.tile([P, 2, U], F32, name="res23")]
-        mixed = []
-        for t in range(PACK):
-            b = [work.tile([P, U], F32, name="o_b%d" % d) for d in range(D)]
-            for d in range(D):
-                nc.vector.tensor_tensor(b[d][:], z[t][:].indirect(nxt_t[d][:]), g2[d][:], MULT)
-            if t < PACK - 1:
-                back = add_in_psum(b, in_blocks(held.tile([P, U], F32, name="o_sum%d" % t), U), True)
-                mixed.append(held.tile([P, U], F32, name="mixed%d" % t))
-                nc.scalar.copy(mixed[t][:], back[:])
-            else:
-                last_sum = [held.tile([P, P], F32, name="last_sum%d" % c, tag="res_b%d" % c, align_bytes=64)[:] for c in range(U // P)]
-                back = add_in_psum(b[1:], last_sum, True)
+        def own(t):
+            return plain_gather("own%d" % t, y[t], cen_t, V)
 
+        def root_term(t):
+            return plain_gather("root%d" % t, y[t], root_t, U)
+
+        def turn_z(t, own_term):
+            near = [gated_gather("near%d_%d" % (t, d), y[t], pos_t[d], g1[d][:], V) for d in range(D)]
+            return turn_and_add(near[:2] + [own_term] + near[2:], V, t % 2)
+
+        def z_back(t, turned):
+            if t == PACK - 1:
+                back = sums.tile([P, V], F32, name="back", tag="sum_0")
+            else:
+                back = psum.tile([P, V], F32, name="bank")
+            return turn_back("z_sum%d" % t, turned, V, back)
+
+        z = [held.tile([P, V], F32, name="z%d" % t) for t in range(PACK)]
+
+        def finish_z(t, back):
+            nc.scalar.activation(z[t][:], back[:], ACT.Copy, scale=0.8)
+
+        second_product(0)
+        w2_q.append(quantise_w2_pair(1, round_w2_pair(1, nc.scalar.copy, "h_b896")))
+        second_product(1)
+        turned = turn_z(0, own(0))
+        second_product(2)
+        second_product(3)
+        roots = []
+        for t in range(1, PACK):
+            back = z_back(t - 1, turned)
+            own_term = own(t)
+            if t == 3:
+                roots.append(root_term(1))
+            finish_z(t - 1, back)
+            if t == 2:
+                roots.append(root_term(0))
+            turned = turn_z(t, own_term)
+        roots.append(root_term(2))
+        back = z_back(PACK - 1, turned)
+        roots.append(root_term(3))
+        finish_z(PACK - 1, back)
+
+        out_rows = out_0.rearrange("(p t) x -> p t x", t=PACK)
+        res = [held.tile([P, 2, U], F32, name="res%d" % pair) for pair in range(2)]
         halves = (slice(0, U // 2), slice(U // 2, U))
         res_b = [held.tile([P, PACK * U // 2], BF16, name="res_b%d" % c, align_bytes=64) for c in range(2)]
         res_bv = [tl[:].rearrange("p (c t) -> p c t", t=PACK) for tl in res_b]
-        last = work.tile([P, U], F32, name="last")
-        for t in range(PACK - 1):
-            pair, s = divmod(t, 2)
-            if t == 1:
-                nc.vector.tensor_tensor(last[:], y[PACK - 1][:].indirect(root_t[:]), b[0][:], ADD)
-            if t == 2:
-                nc.vector.tensor_tensor(res[1][:, 1, :], last[:], back[:], ADD)
-                nc.sync.dma_start(out_rows[:, 3, :], res[1][:, 1, :])
-            nc.vector.tensor_tensor(res[pair][:, s, :], y[t][:].indirect(root_t[:]), mixed[t][:], ADD)
-            if t == 1:
-                nc.sync.dma_start(out_rows[:, 0:2, :], res[0][:])
-                for dst, cols in zip(res_bv, halves):
-                    nc.scalar.copy(dst[:, :, 0:2], res[0][:].rearrange("p t c -> p c t")[:, cols])
-        nc.sync.dma_start(out_rows[:, 2, :], res[1][:, 0, :])
+        backs = []
+        for t in range(PACK):
+            terms = [roots[t]] + [
+                gated_gather("next%d_%d" % (t, d), z[t], nxt_t[d], g2[d][:], U, tag="g1_%d" % d if t == 0 else None)
+                for d in range(D if t < 2 else D - 1)
+            ]
+            back = psum.tile([P, U], F32, name="bank")
+            turn_back("o_sum%d" % t, turn_and_add(terms, U, (t + 1) % 2), U, back)
+            if t < 2:
+                nc.scalar.copy(res[0][:, t, :], back[:])
+            else:
+                backs.append(back)
+        nc.sync.dma_start(out_rows[:, 0:2, :], res[0][:])
+        for dst, cols in zip(res_bv, halves):
+            nc.scalar.copy(dst[:, :, 0:2], res[0][:].rearrange("p t c -> p c t")[:, cols])
+        late = [gated_gather("next2_2", z[2], nxt_t[2], g2[2][:], U, tag="g2_1"), gated_gather("next3_2", z[3], nxt_t[2], g2[2][:], U)]
+        for s in range(2):
+            nc.vector.tensor_tensor(res[1][:, s, :], late[s][:], backs[s][:], ADD)
+            nc.sync.dma_start(out_rows[:, 2 + s, :], res[1][:, s, :])
         res_c = held.tile([P, U], I32, name="res_c", align_bytes=64)
         res_s = held.tile([P, U], U8, name="res_s", align_bytes=64)
         for copy, dst, cols in zip((nc.scalar.copy, nc.vector.tensor_copy), res_bv, halves):

@@ -24,6 +24,7 @@ BLK = 128
 RELU_BLOCKS = ((0, 128), (128, 128), (448, 64), (256, 128), (384, 64), (512, 128), (640, 128), (768, 128), (896, 128))
 RELU_ON_VECTOR = (448, 512)
 WARM_UPS = 4
+ROUND_ON_SCALAR = 96
 H_PIECES = ((0, 256), (256, 256), (512, 256), (768, 128), (896, 128))
 Y_PIECES = ((0, 512), (512, 256), (768, 128), (896, 128))
 
@@ -35,7 +36,7 @@ def tile_picked_zappnp_relu_po_kernel(
     nc = tc.nc
     with ExitStack() as ctx:
         held = ctx.enter_context(tc.tile_pool(name="held", bufs=1))
-        psum = ctx.enter_context(tc.psum_pool(name="psum", bufs=6))
+        psum = ctx.enter_context(tc.psum_pool(name="psum", bufs=5))
         sums = ctx.enter_context(tc.psum_pool(name="sums", bufs=1))
 
         def load_list(name, src):
@@ -67,7 +68,7 @@ def tile_picked_zappnp_relu_po_kernel(
         nc.sync.dma_start(w2_raw[:], w2.rearrange("(p j) c -> p j c", j=PACK))
         pos_t = [load_list("pos1_t", pos1), load_list("pos2_t", pos2), load_list("pos3_t", pos3)]
         cen_t = load_list("cen_t", cen)
-        g2 = [held.tile([P, U], F32, name="g2_%d" % d) for d in range(D)]
+        g2 = [held.tile([P, U], F32, name="g2_%d" % d, align_bytes=64) for d in range(D)]
         for d in range(D):
             nc.sync.dma_start(g2[d][:], gate2[d])
         nxt_t = [load_list("nxt1_t", nxt1), load_list("nxt2_t", nxt2), load_list("nxt3_t", nxt3)]
@@ -91,7 +92,7 @@ def tile_picked_zappnp_relu_po_kernel(
         nc.tensor.transpose(bank[:], gate_rows[:], ident[:])
         gate_cols = held.tile([P, pieces], F32, name="gate_cols")
         nc.scalar.copy(gate_cols[:], bank[:, :pieces])
-        g1 = [held.tile([P, V], F32, name="g1_%d" % d) for d in range(D)]
+        g1 = [held.tile([P, V], F32, name="g1_%d" % d, align_bytes=64) for d in range(D)]
         for d in range(D):
             bank = psum.tile([P, V], F32, name="bank")
             for b in range(V // P):
@@ -134,7 +135,10 @@ def tile_picked_zappnp_relu_po_kernel(
             h_b = held.tile([P, PACK * width], BF16, name="h_b%d" % p0, align_bytes=64)
             for c0, n in [blk for blk in RELU_BLOCKS if p0 <= blk[0] < p0 + width]:
                 hf, c = divmod(c0, HALF)
-                bank = psum.tile([P, PACK, n], F32, name="bank")
+                if c0 in (512, 640, 768):
+                    bank = sums.tile([P, PACK, n], F32, name="relu_bank", tag="sum_%d" % (c0 // BLK % 3))
+                else:
+                    bank = psum.tile([P, PACK, n], F32, name="bank")
                 for t in range(PACK):
                     nc.tensor.matmul_mx(
                         out=bank[:, t, :],
@@ -158,6 +162,7 @@ def tile_picked_zappnp_relu_po_kernel(
         def second_product(t):
             w2_c, w2_s = w2_q[t // 2]
             rows = slice(t % 2 * P, (t % 2 + 1) * P)
+            pieces_out = []
             for c0, width in Y_PIECES if t == 0 else ((0, HALF), (HALF, HALF)):
                 hf, c = divmod(c0, HALF)
                 bank = psum.tile([P, width], F32, name="bank")
@@ -167,34 +172,43 @@ def tile_picked_zappnp_relu_po_kernel(
                     rhs=h_c[hf][:, c : c + width].bitcast(FP8X4), rhs_scale=h_s[hf][:, c : c + width],
                     start=True, stop=True,
                 )
+                pieces_out.append((c0, width, bank))
+            return pieces_out
+
+        def fetch_y(t, banks):
+            for c0, width, bank in banks:
                 if t == 0 and HALF <= c0 < S - BLK:
                     nc.vector.tensor_scalar_mul(y[t][:, c0 : c0 + width], bank[:], 0.2)
                 else:
                     nc.scalar.activation(y[t][:, c0 : c0 + width], bank[:], ACT.Copy, scale=0.2)
 
-        def plain_gather(name, window, offsets, width):
-            term = held.tile([P, width], F32, name=name)
+        def plain_gather(name, window, offsets, width, tag=None):
+            term = held.tile([P, width], F32, name=name, tag=tag or name, align_bytes=64)
             nc.scalar.activation(term[:], window[:].indirect(offsets[:]), ACT.Copy)
             return term
 
         def gated_gather(name, window, offsets, gates, width, tag=None):
-            term = held.tile([P, width], F32, name=name, tag=tag or name)
+            term = held.tile([P, width], F32, name=name, tag=tag or name, align_bytes=64)
             nc.vector.tensor_tensor(term[:], window[:].indirect(offsets[:]), gates, MULT)
             return term
 
-        def turn_and_add(terms, width, side):
+        def turn_and_add(parts, side):
+            width = sum(terms[0].shape[1] for terms in parts)
             turned = sums.tile([P, width], F32, name="turned", tag="sum_%d" % side)
-            blocks = [slice(b * P, (b + 1) * P) for b in range(width // P)]
-            for d, term in enumerate(terms):
-                for b, cols in enumerate(blocks):
-                    nc.tensor.matmul(
-                        turned[:, cols], term[:, cols], ident[:], is_transpose=True,
-                        start=(d == 0 and b == 0), stop=(d == len(terms) - 1 and b == len(blocks) - 1),
-                    )
+            passes = []
+            first = 0
+            for terms in parts:
+                for term in terms:
+                    passes = passes + [(first + c, term[:, c : c + P]) for c in range(0, term.shape[1], P)]
+                first = first + terms[0].shape[1]
+            for i, (c, block) in enumerate(passes):
+                nc.tensor.matmul(
+                    turned[:, c : c + P], block, ident[:], is_transpose=True, start=(i == 0), stop=(i == len(passes) - 1)
+                )
             return turned
 
         def turn_back(name, turned, width, back):
-            total = held.tile([P, width], F32, name=name)
+            total = held.tile([P, width], F32, name=name, align_bytes=64)
             nc.scalar.copy(total[:], turned[:])
             for b in range(width // P):
                 cols = slice(b * P, (b + 1) * P)
@@ -204,16 +218,16 @@ def tile_picked_zappnp_relu_po_kernel(
         def own(t):
             return plain_gather("own%d" % t, y[t], cen_t, V)
 
-        def root_term(t):
-            return plain_gather("root%d" % t, y[t], root_t, U)
+        def root_term(t, tag):
+            return plain_gather("root%d" % t, y[t], root_t, U, tag)
 
         def turn_z(t, own_term):
-            near = [gated_gather("near%d_%d" % (t, d), y[t], pos_t[d], g1[d][:], V) for d in range(D)]
-            return turn_and_add(near[:2] + [own_term] + near[2:], V, t % 2)
+            near = [gated_gather("near%d_%d" % (t, d), y[t], pos_t[d], g1[d][:], V, tag="h_b896" if (t, d) == (0, 2) else None) for d in range(D)]
+            return turn_and_add([near + [own_term] if t < 2 else [own_term] + near], t % 2)
 
         def z_back(t, turned):
-            if t == PACK - 1:
-                back = sums.tile([P, V], F32, name="back", tag="sum_0")
+            if t >= 2:
+                back = sums.tile([P, V], F32, name="back", tag="sum_2" if t == 2 else "sum_0")
             else:
                 back = psum.tile([P, V], F32, name="bank")
             return turn_back("z_sum%d" % t, turned, V, back)
@@ -223,57 +237,62 @@ def tile_picked_zappnp_relu_po_kernel(
         def finish_z(t, back):
             nc.scalar.activation(z[t][:], back[:], ACT.Copy, scale=0.8)
 
-        second_product(0)
+        fetch_y(0, second_product(0))
         w2_q.append(quantise_w2_pair(1, round_w2_pair(1, nc.scalar.copy, "h_b896")))
-        second_product(1)
-        turned = turn_z(0, own(0))
-        second_product(2)
-        second_product(3)
-        roots = []
-        for t in range(1, PACK):
-            back = z_back(t - 1, turned)
-            own_term = own(t)
-            if t == 3:
-                roots.append(root_term(1))
-            finish_z(t - 1, back)
-            if t == 2:
-                roots.append(root_term(0))
-            turned = turn_z(t, own_term)
-        roots.append(root_term(2))
-        back = z_back(PACK - 1, turned)
-        roots.append(root_term(3))
-        finish_z(PACK - 1, back)
+        y_banks = [second_product(t) for t in range(1, PACK)]
+        fetch_y(1, y_banks[0])
+        turned = [turn_z(0, own(0))]
+        fetch_y(2, y_banks[1])
+        fetch_y(3, y_banks[2])
+        turned.append(turn_z(1, own(1)))
+        backs = [z_back(0, turned[0])]
+        turned.append(turn_z(2, own(2)))
+        finish_z(0, backs[0])
+        backs.append(z_back(1, turned[1]))
+        turned.append(turn_z(3, own(3)))
+        finish_z(1, backs[1])
+        backs.append(z_back(2, turned[2]))
+        roots = [root_term(0, None), root_term(1, None)]
+        finish_z(2, backs[2])
+        roots.append(root_term(2, None))
+        backs.append(z_back(3, turned[3]))
+        roots.append(root_term(3, None))
+        finish_z(3, backs[3])
 
         out_rows = out_0.rearrange("(p t) x -> p t x", t=PACK)
-        res = [held.tile([P, 2, U], F32, name="res%d" % pair) for pair in range(2)]
+        res = held.tile([P, PACK, U], F32, name="res")
         halves = (slice(0, U // 2), slice(U // 2, U))
-        res_b = [held.tile([P, PACK * U // 2], BF16, name="res_b%d" % c, align_bytes=64) for c in range(2)]
-        res_bv = [tl[:].rearrange("p (c t) -> p c t", t=PACK) for tl in res_b]
-        backs = []
-        for t in range(PACK):
-            terms = [roots[t]] + [
+        def out_terms(t, lists):
+            return [roots[t]] + [
                 gated_gather("next%d_%d" % (t, d), z[t], nxt_t[d], g2[d][:], U, tag="g1_%d" % d if t == 0 else None)
-                for d in range(D if t < 2 else D - 1)
+                for d in range(lists)
             ]
-            back = psum.tile([P, U], F32, name="bank")
-            turn_back("o_sum%d" % t, turn_and_add(terms, U, (t + 1) % 2), U, back)
-            if t < 2:
-                nc.scalar.copy(res[0][:, t, :], back[:])
+
+        first_back = psum.tile([P, 2 * U], F32, name="bank")
+        turn_back("o_sum01", turn_and_add([out_terms(0, D), out_terms(1, D - 1)], 2), 2 * U, first_back)
+        backs = [psum.tile([P, U], F32, name="bank")[:] for t in range(2)]
+        turn_back("o_sum2", turn_and_add([out_terms(2, D - 1)], 1), U, backs[0])
+        nc.scalar.copy(res[:, 0, :], first_back[:, :U])
+        turn_back("o_sum3", turn_and_add([out_terms(3, D - 1)], 0), U, backs[1])
+        backs = [first_back[:, U:]] + backs
+        late = [
+            gated_gather("next%d_2" % t, z[t], nxt_t[2], g2[2][:], U, tag={1: "g2_1", 2: "g2_0"}.get(t)) for t in range(1, PACK)
+        ]
+        for t in range(1, PACK):
+            nc.vector.tensor_tensor(res[:, t, :], late[t - 1][:], backs[t - 1], ADD)
+            if t == 1:
+                nc.sync.dma_start(out_rows[:, 0:2, :], res[:, 0:2, :])
             else:
-                backs.append(back)
-        nc.sync.dma_start(out_rows[:, 0:2, :], res[0][:])
-        for dst, cols in zip(res_bv, halves):
-            nc.scalar.copy(dst[:, :, 0:2], res[0][:].rearrange("p t c -> p c t")[:, cols])
-        late = [gated_gather("next2_2", z[2], nxt_t[2], g2[2][:], U, tag="g2_1"), gated_gather("next3_2", z[3], nxt_t[2], g2[2][:], U)]
-        for s in range(2):
-            nc.vector.tensor_tensor(res[1][:, s, :], late[s][:], backs[s][:], ADD)
-            nc.sync.dma_start(out_rows[:, 2 + s, :], res[1][:, s, :])
+                nc.sync.dma_start(out_rows[:, t, :], res[:, t, :])
+        res_b = held.tile([P, PACK * U], BF16, name="res_b", align_bytes=64)
+        for copy, cols in ((nc.scalar.copy, slice(0, ROUND_ON_SCALAR)), (nc.vector.tensor_copy, slice(ROUND_ON_SCALAR, U))):
+            copy(res_b[:].rearrange("p (c t) -> p c t", t=PACK)[:, cols], res[:].rearrange("p t c -> p c t")[:, cols])
         res_c = held.tile([P, U], I32, name="res_c", align_bytes=64)
         res_s = held.tile([P, U], U8, name="res_s", align_bytes=64)
-        for copy, dst, cols in zip((nc.scalar.copy, nc.vector.tensor_copy), res_bv, halves):
-            copy(dst[:, :, 2:4], res[1][:].rearrange("p t c -> p c t")[:, cols])
-        for rounded, cols in zip(res_b, halves):
-            nc.vector.quantize_mx(out=res_c[:, cols].bitcast(FP8X4), scales=res_s[:, cols], in_=rounded[:])
+        for cols in halves:
+            nc.vector.quantize_mx(
+                out=res_c[:, cols].bitcast(FP8X4), scales=res_s[:, cols], in_=res_b[:, PACK * cols.start : PACK * cols.stop]
+            )
             nc.sync.dma_start(out_1[0].rearrange("p n t -> p (n t)").bitcast(I32)[:, cols], res_c[:, cols])
         for q in range(4):
             eng = nc.sync if q == 3 else nc.scalar

@@ -192,45 +192,41 @@ def tile_picked_zappnp_relu_po_kernel(
             nc.vector.tensor_tensor(term[:], window[:].indirect(offsets[:]), gates, MULT)
             return term
 
-        def turn_and_add(parts, side):
-            width = sum(terms[0].shape[1] for terms in parts)
-            turned = sums.tile([P, width], F32, name="turned", tag="sum_%d" % side)
-            passes = []
-            first = 0
-            for terms in parts:
-                for term in terms:
-                    passes = passes + [(first + c, term[:, c : c + P]) for c in range(0, term.shape[1], P)]
-                first = first + terms[0].shape[1]
-            for i, (c, block) in enumerate(passes):
-                nc.tensor.matmul(
-                    turned[:, c : c + P], block, ident[:], is_transpose=True, start=(i == 0), stop=(i == len(passes) - 1)
-                )
-            return turned
+        def sum_bank(width, side):
+            return sums.tile([P, width], F32, name="turned", tag="sum_%d" % side)
 
-        def turn_back(name, turned, width, back):
-            total = held.tile([P, width], F32, name=name, align_bytes=64)
+        def turn(turned, term, first_column=0, opens=False, closes=False):
+            width = term.shape[1]
+            for c in range(0, width, P):
+                nc.tensor.matmul(
+                    turned[:, first_column + c : first_column + c + P], term[:, c : c + P], ident[:], is_transpose=True,
+                    start=(opens and c == 0), stop=(closes and c == width - P),
+                )
+
+        def fetch_sum(name, turned):
+            total = held.tile(list(turned.shape), F32, name=name, align_bytes=64)
             nc.scalar.copy(total[:], turned[:])
-            for b in range(width // P):
-                cols = slice(b * P, (b + 1) * P)
-                nc.tensor.transpose(back[:, cols], total[:, cols], ident[:])
+            return total
+
+        def turn_back(total, back):
+            for c in range(0, total.shape[1], P):
+                nc.tensor.transpose(back[:, c : c + P], total[:, c : c + P], ident[:])
             return back
 
         def own(t):
             return plain_gather("own%d" % t, y[t], cen_t, V)
 
-        def root_term(t, tag):
-            return plain_gather("root%d" % t, y[t], root_t, U, tag)
+        def root_term(t):
+            return plain_gather("root%d" % t, y[t], root_t, U, ("near2_2", "near3_1", "near3_2", "g1_0")[t])
 
-        def turn_z(t, own_term):
-            near = [gated_gather("near%d_%d" % (t, d), y[t], pos_t[d], g1[d][:], V, tag="h_b896" if (t, d) == (0, 2) else None) for d in range(D)]
-            return turn_and_add([near + [own_term] if t < 2 else [own_term] + near], t % 2)
+        def near(t, d, tag=None):
+            return gated_gather("near%d_%d" % (t, d), y[t], pos_t[d], g1[d][:], V, tag)
 
-        def z_back(t, turned):
-            if t >= 2:
-                back = sums.tile([P, V], F32, name="back", tag="sum_2" if t == 2 else "sum_0")
-            else:
-                back = psum.tile([P, V], F32, name="bank")
-            return turn_back("z_sum%d" % t, turned, V, back)
+        def onward(t, d, tag=None):
+            return gated_gather("next%d_%d" % (t, d), z[t], nxt_t[d], g2[d][:], U, tag)
+
+        def free_bank(width):
+            return psum.tile([P, width], F32, name="bank")
 
         z = [held.tile([P, V], F32, name="z%d" % t) for t in range(PACK)]
 
@@ -239,51 +235,68 @@ def tile_picked_zappnp_relu_po_kernel(
 
         fetch_y(0, second_product(0))
         w2_q.append(quantise_w2_pair(1, round_w2_pair(1, nc.scalar.copy, "h_b896")))
-        y_banks = [second_product(t) for t in range(1, PACK)]
-        fetch_y(1, y_banks[0])
-        turned = [turn_z(0, own(0))]
-        fetch_y(2, y_banks[1])
-        fetch_y(3, y_banks[2])
-        turned.append(turn_z(1, own(1)))
-        backs = [z_back(0, turned[0])]
-        turned.append(turn_z(2, own(2)))
-        finish_z(0, backs[0])
-        backs.append(z_back(1, turned[1]))
-        turned.append(turn_z(3, own(3)))
-        finish_z(1, backs[1])
-        backs.append(z_back(2, turned[2]))
-        roots = [root_term(0, None), root_term(1, None)]
-        finish_z(2, backs[2])
-        roots.append(root_term(2, None))
-        backs.append(z_back(3, turned[3]))
-        roots.append(root_term(3, None))
-        finish_z(3, backs[3])
+        fetch_y(1, second_product(1))
+        turned = [sum_bank(V, 0)]
+        turn(turned[0], near(0, 0), opens=True)
+        turn(turned[0], near(0, 1))
+        y_banks = [second_product(t) for t in range(2, PACK)]
+        turn(turned[0], near(0, 2, "h_b896"))
+        turn(turned[0], own(0), closes=True)
+        fetch_y(2, y_banks[0])
+        turned.append(sum_bank(V, 1))
+        turn(turned[1], near(1, 0), opens=True)
+        turn(turned[1], near(1, 1))
+        turn(turned[1], own(1))
+        turn(turned[1], near(1, 2), closes=True)
+        fetch_y(3, y_banks[1])
+        back0 = turn_back(fetch_sum("z_sum0", turned[0]), free_bank(V))
+        turned.append(sum_bank(V, 0))
+        turn(turned[2], near(2, 0), opens=True)
+        turn(turned[2], own(2))
+        turn(turned[2], near(2, 1))
+        back1 = turn_back(fetch_sum("z_sum1", turned[1]), free_bank(V))
+        finish_z(0, back0)
+        turn(turned[2], near(2, 2), closes=True)
+        turned.append(sum_bank(V, 1))
+        turn(turned[3], own(3), opens=True)
+        turn(turned[3], near(3, 0))
+        finish_z(1, back1)
+        back2 = turn_back(fetch_sum("z_sum2", turned[2]), sum_bank(V, 2))
+        turn(turned[3], near(3, 1))
+        turn(turned[3], near(3, 2), closes=True)
+        roots = [root_term(0), root_term(1)]
+        finish_z(2, back2)
+        roots.append(root_term(2))
+        back3 = turn_back(fetch_sum("z_sum3", turned[3]), sum_bank(V, 0))
+        finish_z(3, back3)
 
         out_rows = out_0.rearrange("(p t) x -> p t x", t=PACK)
         res = held.tile([P, PACK, U], F32, name="res")
         halves = (slice(0, U // 2), slice(U // 2, U))
-        def out_terms(t, lists):
-            return [roots[t]] + [
-                gated_gather("next%d_%d" % (t, d), z[t], nxt_t[d], g2[d][:], U, tag="g1_%d" % d if t == 0 else None)
-                for d in range(lists)
-            ]
-
-        first_back = psum.tile([P, 2 * U], F32, name="bank")
-        turn_back("o_sum01", turn_and_add([out_terms(0, D), out_terms(1, D - 1)], 2), 2 * U, first_back)
-        backs = [psum.tile([P, U], F32, name="bank")[:] for t in range(2)]
-        turn_back("o_sum2", turn_and_add([out_terms(2, D - 1)], 1), U, backs[0])
-        nc.scalar.copy(res[:, 0, :], first_back[:, :U])
-        turn_back("o_sum3", turn_and_add([out_terms(3, D - 1)], 0), U, backs[1])
-        backs = [first_back[:, U:]] + backs
-        late = [
-            gated_gather("next%d_2" % t, z[t], nxt_t[2], g2[2][:], U, tag={1: "g2_1", 2: "g2_0"}.get(t)) for t in range(1, PACK)
-        ]
-        for t in range(1, PACK):
-            nc.vector.tensor_tensor(res[:, t, :], late[t - 1][:], backs[t - 1], ADD)
-            if t == 1:
-                nc.sync.dma_start(out_rows[:, 0:2, :], res[:, 0:2, :])
-            else:
-                nc.sync.dma_start(out_rows[:, t, :], res[:, t, :])
+        pair_back = free_bank(2 * U)
+        for t in range(2):
+            bank = sum_bank(U, 2 - 2 * t)
+            turn(bank, roots[t], opens=True)
+            for d in range(D):
+                turn(bank, onward(t, d, "g1_%d" % d if t == 0 else None), closes=(d == D - 1))
+            turn_back(fetch_sum("o_sum%d" % t, bank), pair_back[:, t * U : (t + 1) * U])
+        roots.append(root_term(3))
+        third = sum_bank(U, 2)
+        turn(third, roots[2], opens=True)
+        turn(third, onward(2, 0))
+        turn(third, onward(2, 1), closes=True)
+        third_back = turn_back(fetch_sum("o_sum2", third), free_bank(U))
+        nc.scalar.copy(res[:, 0:2, :], pair_back[:].rearrange("p (t c) -> p t c", t=2))
+        nc.sync.dma_start(out_rows[:, 0:2, :], res[:, 0:2, :])
+        last = [onward(3, d) for d in range(D)]
+        late = onward(2, 2, "g2_1")
+        part = [held.tile([P, U], F32, name="part%d" % i) for i in range(2)]
+        nc.vector.tensor_tensor(part[0][:], last[0][:], roots[3][:], ADD)
+        nc.vector.tensor_tensor(part[1][:], last[1][:], last[2][:], ADD)
+        nc.vector.tensor_tensor(res[:, 2, :], late[:], third_back[:], ADD)
+        nc.sync.dma_start(out_rows[:, 2, :], res[:, 2, :])
+        nc.vector.tensor_tensor(res[:, 3, :], part[0][:], part[1][:], ADD)
+        nc.sync.dma_start(out_rows[:, 3, :], res[:, 3, :])
         res_b = held.tile([P, PACK * U], BF16, name="res_b", align_bytes=64)
         for copy, cols in ((nc.scalar.copy, slice(0, ROUND_ON_SCALAR)), (nc.vector.tensor_copy, slice(ROUND_ON_SCALAR, U))):
             copy(res_b[:].rearrange("p (c t) -> p c t", t=PACK)[:, cols], res[:].rearrange("p t c -> p c t")[:, cols])

@@ -21,10 +21,10 @@ P = 128
 PACK = 4
 HALF = S // 2
 BLK = 128
-RELU_BLOCKS = ((0, 128), (128, 128), (448, 64), (256, 128), (384, 64), (512, 128), (640, 128), (768, 128), (896, 128))
-RELU_ON_VECTOR = (448, 512)
+RELU_BLOCKS = tuple((c, BLK) for c in range(0, S, BLK))
+RELU_ON_VECTOR = (512,)
+X_PIECES = ((0, 256), (256, 256), (512, 512))
 WARM_UPS = 4
-ROUND_ON_SCALAR = 96
 H_PIECES = ((0, 256), (256, 256), (512, 256), (768, 128), (896, 128))
 Y_PIECES = ((0, 512), (512, 256), (768, 128), (896, 128))
 
@@ -68,9 +68,10 @@ def tile_picked_zappnp_relu_po_kernel(
         nc.sync.dma_start(w2_raw[:], w2.rearrange("(p j) c -> p j c", j=PACK))
         pos_t = [load_list("pos1_t", pos1), load_list("pos2_t", pos2), load_list("pos3_t", pos3)]
         cen_t = load_list("cen_t", cen)
-        g2 = [held.tile([P, U], F32, name="g2_%d" % d, align_bytes=64) for d in range(D)]
+        g2_all = held.tile([P, D, U], F32, name="g2_all")
+        g2 = [g2_all[:, d, :] for d in range(D)]
         for d in range(D):
-            nc.sync.dma_start(g2[d][:], gate2[d])
+            nc.sync.dma_start(g2[d], gate2[d])
         nxt_t = [load_list("nxt1_t", nxt1), load_list("nxt2_t", nxt2), load_list("nxt3_t", nxt3)]
         root_t = load_list("root_t", root)
 
@@ -107,10 +108,10 @@ def tile_picked_zappnp_relu_po_kernel(
                 rhs=w1_c[:].bitcast(FP8X4), rhs_scale=w1_s[:], start=True, stop=True,
             )
         xw_g = []
-        for hf in range(2):
-            tl = held.tile([P, HALF], U32, name="xw_g%d" % hf, align_bytes=64)
-            nc.vector.tensor_copy(tl[:], xw[:].bitcast(U32).indirect(offs_t[:, hf * HALF // 16 : (hf + 1) * HALF // 16]))
-            xw_g.append(tl)
+        for c0, width in X_PIECES:
+            tl = held.tile([P, width], U32, name="xw_g%d" % c0, align_bytes=64)
+            nc.vector.tensor_copy(tl[:], xw[:].bitcast(U32).indirect(offs_t[:, c0 // 16 : (c0 + width) // 16]))
+            xw_g = xw_g + [tl[:, c : c + BLK] for c in range(0, width, BLK)]
 
         def round_w2_pair(pair, engine_copy, tag):
             w2_b = held.tile([P, 2 * PACK * P], BF16, name="w2_b%d" % pair, tag=tag, align_bytes=64)
@@ -134,7 +135,6 @@ def tile_picked_zappnp_relu_po_kernel(
         for p0, width in H_PIECES:
             h_b = held.tile([P, PACK * width], BF16, name="h_b%d" % p0, align_bytes=64)
             for c0, n in [blk for blk in RELU_BLOCKS if p0 <= blk[0] < p0 + width]:
-                hf, c = divmod(c0, HALF)
                 if c0 in (512, 640, 768):
                     bank = sums.tile([P, PACK, n], F32, name="relu_bank", tag="sum_%d" % (c0 // BLK % 3))
                 else:
@@ -143,7 +143,7 @@ def tile_picked_zappnp_relu_po_kernel(
                     nc.tensor.matmul_mx(
                         out=bank[:, t, :],
                         lhsT=w1_c[:, t * P : (t + 1) * P].bitcast(FP8X4), lhsT_scale=w1_s[:, t * P : (t + 1) * P],
-                        rhs=xw_g[hf][:, c : c + n].bitcast(FP8X4), rhs_scale=xs_g[:, c0 : c0 + n],
+                        rhs=xw_g[c0 // BLK].bitcast(FP8X4), rhs_scale=xs_g[:, c0 : c0 + n],
                         start=True, stop=True,
                     )
                 dst = h_b[:, PACK * (c0 - p0) : PACK * (c0 - p0 + n)].rearrange("p (n t) -> p n t", t=PACK)
@@ -157,7 +157,7 @@ def tile_picked_zappnp_relu_po_kernel(
             if p0 == 0:
                 w2_q.append(quantise_w2_pair(0, w2_first))
 
-        y = [held.tile([P, S], F32, name="y%d" % t, tag="w2_raw" if t == 1 else "y%d" % t) for t in range(PACK)]
+        y = [held.tile([P, S], F32, name="y%d" % t) for t in range(PACK)]
 
         def second_product(t):
             w2_c, w2_s = w2_q[t // 2]
@@ -217,13 +217,13 @@ def tile_picked_zappnp_relu_po_kernel(
             return plain_gather("own%d" % t, y[t], cen_t, V)
 
         def root_term(t):
-            return plain_gather("root%d" % t, y[t], root_t, U, ("near2_2", "near3_1", "near3_2", "g1_0")[t])
+            return plain_gather("root%d" % t, y[t], root_t, U, ("near1_2", "near2_0", "near2_2")[t])
 
         def near(t, d, tag=None):
             return gated_gather("near%d_%d" % (t, d), y[t], pos_t[d], g1[d][:], V, tag)
 
         def onward(t, d, tag=None):
-            return gated_gather("next%d_%d" % (t, d), z[t], nxt_t[d], g2[d][:], U, tag)
+            return gated_gather("next%d_%d" % (t, d), z[t], nxt_t[d], g2[d], U, tag)
 
         def free_bank(width):
             return psum.tile([P, width], F32, name="bank")
@@ -234,13 +234,13 @@ def tile_picked_zappnp_relu_po_kernel(
             nc.scalar.activation(z[t][:], back[:], ACT.Copy, scale=0.8)
 
         fetch_y(0, second_product(0))
-        w2_q.append(quantise_w2_pair(1, round_w2_pair(1, nc.scalar.copy, "h_b896")))
+        w2_q.append(quantise_w2_pair(1, round_w2_pair(1, nc.vector.tensor_copy, "h_b896")))
         fetch_y(1, second_product(1))
+        y_banks = [second_product(t) for t in range(2, PACK)]
         turned = [sum_bank(V, 0)]
         turn(turned[0], near(0, 0), opens=True)
         turn(turned[0], near(0, 1))
-        y_banks = [second_product(t) for t in range(2, PACK)]
-        turn(turned[0], near(0, 2, "h_b896"))
+        turn(turned[0], near(0, 2))
         turn(turned[0], own(0), closes=True)
         fetch_y(2, y_banks[0])
         turned.append(sum_bank(V, 1))
@@ -261,17 +261,32 @@ def tile_picked_zappnp_relu_po_kernel(
         turn(turned[3], own(3), opens=True)
         turn(turned[3], near(3, 0))
         finish_z(1, back1)
+        roots = [root_term(0), root_term(1)]
         back2 = turn_back(fetch_sum("z_sum2", turned[2]), sum_bank(V, 2))
         turn(turned[3], near(3, 1))
         turn(turned[3], near(3, 2), closes=True)
-        roots = [root_term(0), root_term(1)]
+        four = {}
+        plain = {t: held.tile([P, D - 1, U], F32, name="plain%d" % t) for t in (2, 3)}
+
+        def root_as_fourth(t):
+            four[t] = held.tile([P, D + 1, U], F32, name="four%d" % t)
+            nc.scalar.activation(four[t][:, D, :], y[t][:].indirect(root_t[:]), ACT.Copy)
+
+        def plain_onward(t, d):
+            nc.scalar.activation(plain[t][:, d - 1, :], z[t][:].indirect(nxt_t[d][:]), ACT.Copy)
+
+        root_as_fourth(2)
         finish_z(2, back2)
-        roots.append(root_term(2))
+        root_as_fourth(3)
+        plain_onward(2, 1)
         back3 = turn_back(fetch_sum("z_sum3", turned[3]), sum_bank(V, 0))
+        plain_onward(2, 2)
         finish_z(3, back3)
+        for d in range(1, D):
+            plain_onward(3, d)
 
         out_rows = out_0.rearrange("(p t) x -> p t x", t=PACK)
-        res = held.tile([P, PACK, U], F32, name="res")
+        res = [held.tile([P, 2, U], F32, name="res%d" % pair) for pair in range(2)]
         halves = (slice(0, U // 2), slice(U // 2, U))
         pair_back = free_bank(2 * U)
         for t in range(2):
@@ -280,32 +295,28 @@ def tile_picked_zappnp_relu_po_kernel(
             for d in range(D):
                 turn(bank, onward(t, d, "g1_%d" % d if t == 0 else None), closes=(d == D - 1))
             turn_back(fetch_sum("o_sum%d" % t, bank), pair_back[:, t * U : (t + 1) * U])
-        roots.append(root_term(3))
-        third = sum_bank(U, 2)
-        turn(third, roots[2], opens=True)
-        turn(third, onward(2, 0))
-        turn(third, onward(2, 1), closes=True)
-        third_back = turn_back(fetch_sum("o_sum2", third), free_bank(U))
-        nc.scalar.copy(res[:, 0:2, :], pair_back[:].rearrange("p (t c) -> p t c", t=2))
-        nc.sync.dma_start(out_rows[:, 0:2, :], res[:, 0:2, :])
-        last = [onward(3, d) for d in range(D)]
-        late = onward(2, 2, "g2_1")
-        part = [held.tile([P, U], F32, name="part%d" % i) for i in range(2)]
-        nc.vector.tensor_tensor(part[0][:], last[0][:], roots[3][:], ADD)
-        nc.vector.tensor_tensor(part[1][:], last[1][:], last[2][:], ADD)
-        nc.vector.tensor_tensor(res[:, 2, :], late[:], third_back[:], ADD)
-        nc.sync.dma_start(out_rows[:, 2, :], res[:, 2, :])
-        nc.vector.tensor_tensor(res[:, 3, :], part[0][:], part[1][:], ADD)
-        nc.sync.dma_start(out_rows[:, 3, :], res[:, 3, :])
-        res_b = held.tile([P, PACK * U], BF16, name="res_b", align_bytes=64)
-        for copy, cols in ((nc.scalar.copy, slice(0, ROUND_ON_SCALAR)), (nc.vector.tensor_copy, slice(ROUND_ON_SCALAR, U))):
-            copy(res_b[:].rearrange("p (c t) -> p c t", t=PACK)[:, cols], res[:].rearrange("p t c -> p c t")[:, cols])
+        nc.scalar.copy(res[0][:], pair_back[:].rearrange("p (t c) -> p t c", t=2))
+        nc.sync.dma_start(out_rows[:, 0:2, :], res[0][:])
+        res_b = [held.tile([P, PACK * U // 2], BF16, name="res_b%d" % c, align_bytes=64) for c in range(2)]
+        res_bv = [tl[:].rearrange("p (c t) -> p c t", t=PACK) for tl in res_b]
+        for dst, cols in zip(res_bv, halves):
+            nc.scalar.copy(dst[:, :, 0:2], res[0][:].rearrange("p t c -> p c t")[:, cols])
+        parts = {}
+        for t in (2, 3):
+            nc.vector.tensor_tensor(four[t][:, 0, :], z[t][:].indirect(nxt_t[0][:]), g2[0], MULT)
+            nc.vector.tensor_tensor(four[t][:, 1:D, :], plain[t][:], g2_all[:, 1:, :], MULT)
+        for t in (2, 3):
+            parts[t] = held.tile([P, 2, U], F32, name="parts%d" % t, tag="plain%d" % (5 - t))
+            nc.vector.tensor_tensor(parts[t][:], four[t][:, :2, :], four[t][:, 2:, :], ADD)
+        for t in (2, 3):
+            nc.vector.tensor_tensor(res[1][:, t - 2, :], parts[t][:, 0, :], parts[t][:, 1, :], ADD)
+        nc.sync.dma_start(out_rows[:, 2:4, :], res[1][:])
+        for copy, dst, cols in zip((nc.scalar.copy, nc.vector.tensor_copy), res_bv, halves):
+            copy(dst[:, :, 2:4], res[1][:].rearrange("p t c -> p c t")[:, cols])
         res_c = held.tile([P, U], I32, name="res_c", align_bytes=64)
         res_s = held.tile([P, U], U8, name="res_s", align_bytes=64)
-        for cols in halves:
-            nc.vector.quantize_mx(
-                out=res_c[:, cols].bitcast(FP8X4), scales=res_s[:, cols], in_=res_b[:, PACK * cols.start : PACK * cols.stop]
-            )
+        for rounded, cols in zip(res_b, halves):
+            nc.vector.quantize_mx(out=res_c[:, cols].bitcast(FP8X4), scales=res_s[:, cols], in_=rounded[:])
             nc.sync.dma_start(out_1[0].rearrange("p n t -> p (n t)").bitcast(I32)[:, cols], res_c[:, cols])
         for q in range(4):
             eng = nc.sync if q == 3 else nc.scalar

@@ -24,7 +24,7 @@ BLK = 128
 RELU_BLOCKS = tuple((c, BLK) for c in range(0, S, BLK))
 RELU_ON_VECTOR = (512,)
 X_PIECES = ((0, 256), (256, 256), (512, 512))
-WARM_UPS = 4
+WARM_UPS = 3
 H_PIECES = ((0, 256), (256, 256), (512, 256), (768, 128), (896, 128))
 Y_PIECES = ((0, 512), (512, 256), (768, 128), (896, 128))
 
@@ -217,7 +217,7 @@ def tile_picked_zappnp_relu_po_kernel(
             return plain_gather("own%d" % t, y[t], cen_t, V)
 
         def root_term(t):
-            return plain_gather("root%d" % t, y[t], root_t, U, ("near1_2", "near2_0", "near2_2")[t])
+            return plain_gather("root%d" % t, y[t], root_t, U, ("near1_2", "near2_0")[t])
 
         def near(t, d, tag=None):
             return gated_gather("near%d_%d" % (t, d), y[t], pos_t[d], g1[d][:], V, tag)
@@ -254,32 +254,33 @@ def tile_picked_zappnp_relu_po_kernel(
         turn(turned[2], near(2, 0), opens=True)
         turn(turned[2], own(2))
         turn(turned[2], near(2, 1))
-        back1 = turn_back(fetch_sum("z_sum1", turned[1]), free_bank(V))
         finish_z(0, back0)
+        own3 = own(3)
+        back1 = turn_back(fetch_sum("z_sum1", turned[1]), free_bank(V))
         turn(turned[2], near(2, 2), closes=True)
-        turned.append(sum_bank(V, 1))
-        turn(turned[3], own(3), opens=True)
-        turn(turned[3], near(3, 0))
-        finish_z(1, back1)
         roots = [root_term(0), root_term(1)]
+        finish_z(1, back1)
         back2 = turn_back(fetch_sum("z_sum2", turned[2]), sum_bank(V, 2))
+        turned.append(sum_bank(V, 0))
+        turn(turned[3], own3, opens=True)
+        turn(turned[3], near(3, 0))
         turn(turned[3], near(3, 1))
         turn(turned[3], near(3, 2), closes=True)
         four = {}
         plain = {t: held.tile([P, D - 1, U], F32, name="plain%d" % t) for t in (2, 3)}
 
         def root_as_fourth(t):
-            four[t] = held.tile([P, D + 1, U], F32, name="four%d" % t)
+            four[t] = held.tile([P, D + 1, U], F32, name="four%d" % t, tag={2: "near2_2", 3: "near2_1"}[t], align_bytes=64)
             nc.scalar.activation(four[t][:, D, :], y[t][:].indirect(root_t[:]), ACT.Copy)
 
         def plain_onward(t, d):
             nc.scalar.activation(plain[t][:, d - 1, :], z[t][:].indirect(nxt_t[d][:]), ACT.Copy)
 
         root_as_fourth(2)
-        finish_z(2, back2)
         root_as_fourth(3)
+        finish_z(2, back2)
         plain_onward(2, 1)
-        back3 = turn_back(fetch_sum("z_sum3", turned[3]), sum_bank(V, 0))
+        back3 = turn_back(fetch_sum("z_sum3", turned[3]), sum_bank(V, 1))
         plain_onward(2, 2)
         finish_z(3, back3)
         for d in range(1, D):
@@ -290,7 +291,7 @@ def tile_picked_zappnp_relu_po_kernel(
         halves = (slice(0, U // 2), slice(U // 2, U))
         pair_back = free_bank(2 * U)
         for t in range(2):
-            bank = sum_bank(U, 2 - 2 * t)
+            bank = sum_bank(U, 2 - t)
             turn(bank, roots[t], opens=True)
             for d in range(D):
                 turn(bank, onward(t, d, "g1_%d" % d if t == 0 else None), closes=(d == D - 1))

@@ -25,6 +25,7 @@ RELU_BLOCKS = tuple((c, BLK) for c in range(0, S, BLK))
 RELU_ON_VECTOR = (512,)
 X_PIECES = ((0, 256), (256, 256), (512, 512))
 WARM_UPS = 3
+ROUND_ON_SCALAR = 96
 H_PIECES = ((0, 256), (256, 256), (512, 256), (768, 128), (896, 128))
 Y_PIECES = ((0, 512), (512, 256), (768, 128), (896, 128))
 
@@ -36,7 +37,7 @@ def tile_picked_zappnp_relu_po_kernel(
     nc = tc.nc
     with ExitStack() as ctx:
         held = ctx.enter_context(tc.tile_pool(name="held", bufs=1))
-        psum = ctx.enter_context(tc.psum_pool(name="psum", bufs=5))
+        psum = ctx.enter_context(tc.psum_pool(name="psum", bufs=6))
         sums = ctx.enter_context(tc.psum_pool(name="sums", bufs=1))
 
         def load_list(name, src):
@@ -135,8 +136,8 @@ def tile_picked_zappnp_relu_po_kernel(
         for p0, width in H_PIECES:
             h_b = held.tile([P, PACK * width], BF16, name="h_b%d" % p0, align_bytes=64)
             for c0, n in [blk for blk in RELU_BLOCKS if p0 <= blk[0] < p0 + width]:
-                if c0 in (512, 640, 768):
-                    bank = sums.tile([P, PACK, n], F32, name="relu_bank", tag="sum_%d" % (c0 // BLK % 3))
+                if c0 in (640, 768):
+                    bank = sums.tile([P, PACK, n], F32, name="relu_bank", tag="sum_%d" % (c0 // BLK % 2))
                 else:
                     bank = psum.tile([P, PACK, n], F32, name="bank")
                 for t in range(PACK):
@@ -260,12 +261,16 @@ def tile_picked_zappnp_relu_po_kernel(
         turn(turned[2], near(2, 2), closes=True)
         roots = [root_term(0), root_term(1)]
         finish_z(1, back1)
-        back2 = turn_back(fetch_sum("z_sum2", turned[2]), sum_bank(V, 2))
-        turned.append(sum_bank(V, 0))
-        turn(turned[3], own3, opens=True)
-        turn(turned[3], near(3, 0))
-        turn(turned[3], near(3, 1))
-        turn(turned[3], near(3, 2), closes=True)
+        back2 = turn_back(fetch_sum("z_sum2", turned[2]), sum_bank(V, 1))
+        z_halves = (slice(0, V // 2), slice(V // 2, V))
+        last_turned = [sum_bank(V // 2, side) for side in range(2)]
+        for i, term in enumerate((own3, near(3, 0), near(3, 1))):
+            for bank, cols in zip(last_turned, z_halves):
+                turn(bank, term[:, cols], opens=(i == 0))
+        for bank, cols in zip(last_turned, z_halves):
+            term = held.tile([P, V // 2], F32, name="near3_2_%d" % cols.start)
+            nc.vector.tensor_tensor(term[:], y[3][:].indirect(pos_t[2][:, cols.start // 16 : cols.stop // 16]), g1[2][:, cols], MULT)
+            turn(bank, term, closes=True)
         four = {}
         plain = {t: held.tile([P, D - 1, U], F32, name="plain%d" % t) for t in (2, 3)}
 
@@ -280,28 +285,34 @@ def tile_picked_zappnp_relu_po_kernel(
         root_as_fourth(3)
         finish_z(2, back2)
         plain_onward(2, 1)
-        back3 = turn_back(fetch_sum("z_sum3", turned[3]), sum_bank(V, 1))
         plain_onward(2, 2)
-        finish_z(3, back3)
-        for d in range(1, D):
-            plain_onward(3, d)
+        last_back = [turn_back(fetch_sum("z_sum3_%d" % i, bank), free_bank(V // 2)) for i, bank in enumerate(last_turned)]
+
+        def finish_last_z(i):
+            nc.scalar.activation(z[3][:, z_halves[i]], last_back[i][:], ACT.Copy, scale=0.8)
+
+        finish_last_z(0)
 
         out_rows = out_0.rearrange("(p t) x -> p t x", t=PACK)
-        res = [held.tile([P, 2, U], F32, name="res%d" % pair) for pair in range(2)]
+        res_all = held.tile([P, PACK, U], F32, name="res_all")
+        res = [res_all[:, 0:2, :], res_all[:, 2:4, :]]
         halves = (slice(0, U // 2), slice(U // 2, U))
-        pair_back = free_bank(2 * U)
+        pair_sums = []
         for t in range(2):
-            bank = sum_bank(U, 2 - t)
+            if t == 1:
+                finish_last_z(1)
+                for d in range(1, D):
+                    plain_onward(3, d)
+            bank = sum_bank(U, t)
             turn(bank, roots[t], opens=True)
             for d in range(D):
                 turn(bank, onward(t, d, "g1_%d" % d if t == 0 else None), closes=(d == D - 1))
-            turn_back(fetch_sum("o_sum%d" % t, bank), pair_back[:, t * U : (t + 1) * U])
-        nc.scalar.copy(res[0][:], pair_back[:].rearrange("p (t c) -> p t c", t=2))
-        nc.sync.dma_start(out_rows[:, 0:2, :], res[0][:])
-        res_b = [held.tile([P, PACK * U // 2], BF16, name="res_b%d" % c, align_bytes=64) for c in range(2)]
-        res_bv = [tl[:].rearrange("p (c t) -> p c t", t=PACK) for tl in res_b]
-        for dst, cols in zip(res_bv, halves):
-            nc.scalar.copy(dst[:, :, 0:2], res[0][:].rearrange("p t c -> p c t")[:, cols])
+            pair_sums.append(fetch_sum("o_sum%d" % t, bank))
+        pair_back = sum_bank(2 * U, 1)
+        for t in range(2):
+            turn_back(pair_sums[t], pair_back[:, t * U : (t + 1) * U])
+        nc.scalar.copy(res[0], pair_back[:].rearrange("p (t c) -> p t c", t=2))
+        nc.sync.dma_start(out_rows[:, 0:2, :], res[0])
         parts = {}
         for t in (2, 3):
             nc.vector.tensor_tensor(four[t][:, 0, :], z[t][:].indirect(nxt_t[0][:]), g2[0], MULT)
@@ -311,13 +322,16 @@ def tile_picked_zappnp_relu_po_kernel(
             nc.vector.tensor_tensor(parts[t][:], four[t][:, :2, :], four[t][:, 2:, :], ADD)
         for t in (2, 3):
             nc.vector.tensor_tensor(res[1][:, t - 2, :], parts[t][:, 0, :], parts[t][:, 1, :], ADD)
-        nc.sync.dma_start(out_rows[:, 2:4, :], res[1][:])
-        for copy, dst, cols in zip((nc.scalar.copy, nc.vector.tensor_copy), res_bv, halves):
-            copy(dst[:, :, 2:4], res[1][:].rearrange("p t c -> p c t")[:, cols])
+        nc.sync.dma_start(out_rows[:, 2:4, :], res[1])
+        res_b = held.tile([P, PACK * U], BF16, name="res_b", align_bytes=64)
+        for copy, cols in ((nc.scalar.copy, slice(0, ROUND_ON_SCALAR)), (nc.vector.tensor_copy, slice(ROUND_ON_SCALAR, U))):
+            copy(res_b[:].rearrange("p (c t) -> p c t", t=PACK)[:, cols], res_all[:].rearrange("p t c -> p c t")[:, cols])
         res_c = held.tile([P, U], I32, name="res_c", align_bytes=64)
         res_s = held.tile([P, U], U8, name="res_s", align_bytes=64)
-        for rounded, cols in zip(res_b, halves):
-            nc.vector.quantize_mx(out=res_c[:, cols].bitcast(FP8X4), scales=res_s[:, cols], in_=rounded[:])
+        for cols in halves:
+            nc.vector.quantize_mx(
+                out=res_c[:, cols].bitcast(FP8X4), scales=res_s[:, cols], in_=res_b[:, PACK * cols.start : PACK * cols.stop]
+            )
             nc.sync.dma_start(out_1[0].rearrange("p n t -> p (n t)").bitcast(I32)[:, cols], res_c[:, cols])
         for q in range(4):
             eng = nc.sync if q == 3 else nc.scalar

@@ -322,7 +322,7 @@ def tile_picked_zappnp_relu_po_kernel(
             nc.vector.tensor_tensor(parts[t][:], four[t][:, :2, :], four[t][:, 2:, :], ADD)
         for t in (2, 3):
             nc.vector.tensor_tensor(res[1][:, t - 2, :], parts[t][:, 0, :], parts[t][:, 1, :], ADD)
-        nc.sync.dma_start(out_rows[:, 2:4, :], res[1])
+            nc.sync.dma_start(out_rows[:, t, :], res[1][:, t - 2, :])
         res_b = held.tile([P, PACK * U], BF16, name="res_b", align_bytes=64)
         for copy, cols in ((nc.scalar.copy, slice(0, ROUND_ON_SCALAR)), (nc.vector.tensor_copy, slice(ROUND_ON_SCALAR, U))):
             copy(res_b[:].rearrange("p (c t) -> p c t", t=PACK)[:, cols], res_all[:].rearrange("p t c -> p c t")[:, cols])

@@ -25,7 +25,6 @@ RELU_BLOCKS = tuple((c, BLK) for c in range(0, S, BLK))
 RELU_ON_VECTOR = (512,)
 X_PIECES = ((0, 256), (256, 256), (512, 512))
 WARM_UPS = 3
-ROUND_ON_SCALAR = 96
 H_PIECES = ((0, 256), (256, 256), (512, 256), (768, 128), (896, 128))
 Y_PIECES = ((0, 512), (512, 256), (768, 128), (896, 128))
 
@@ -69,8 +68,9 @@ def tile_picked_zappnp_relu_po_kernel(
         nc.sync.dma_start(w2_raw[:], w2.rearrange("(p j) c -> p j c", j=PACK))
         pos_t = [load_list("pos1_t", pos1), load_list("pos2_t", pos2), load_list("pos3_t", pos3)]
         cen_t = load_list("cen_t", cen)
-        g2_all = held.tile([P, D, U], F32, name="g2_all")
-        g2 = [g2_all[:, d, :] for d in range(D)]
+        g2_first = held.tile([P, U], F32, name="g2_first", align_bytes=64)
+        g2_rest = held.tile([P, D - 1, U], F32, name="g2_rest")
+        g2 = [g2_first[:]] + [g2_rest[:, d, :] for d in range(D - 1)]
         for d in range(D):
             nc.sync.dma_start(g2[d], gate2[d])
         nxt_t = [load_list("nxt1_t", nxt1), load_list("nxt2_t", nxt2), load_list("nxt3_t", nxt3)]
@@ -178,7 +178,7 @@ def tile_picked_zappnp_relu_po_kernel(
 
         def fetch_y(t, banks):
             for c0, width, bank in banks:
-                if t == 0 and HALF <= c0 < S - BLK:
+                if t == 0 and c0 == HALF:
                     nc.vector.tensor_scalar_mul(y[t][:, c0 : c0 + width], bank[:], 0.2)
                 else:
                     nc.scalar.activation(y[t][:, c0 : c0 + width], bank[:], ACT.Copy, scale=0.2)
@@ -313,25 +313,27 @@ def tile_picked_zappnp_relu_po_kernel(
             turn_back(pair_sums[t], pair_back[:, t * U : (t + 1) * U])
         nc.scalar.copy(res[0], pair_back[:].rearrange("p (t c) -> p t c", t=2))
         nc.sync.dma_start(out_rows[:, 0:2, :], res[0])
-        parts = {}
         for t in (2, 3):
             nc.vector.tensor_tensor(four[t][:, 0, :], z[t][:].indirect(nxt_t[0][:]), g2[0], MULT)
-            nc.vector.tensor_tensor(four[t][:, 1:D, :], plain[t][:], g2_all[:, 1:, :], MULT)
-        for t in (2, 3):
-            parts[t] = held.tile([P, 2, U], F32, name="parts%d" % t, tag="plain%d" % (5 - t))
-            nc.vector.tensor_tensor(parts[t][:], four[t][:, :2, :], four[t][:, 2:, :], ADD)
-        for t in (2, 3):
-            nc.vector.tensor_tensor(res[1][:, t - 2, :], parts[t][:, 0, :], parts[t][:, 1, :], ADD)
-            nc.sync.dma_start(out_rows[:, t, :], res[1][:, t - 2, :])
-        res_b = held.tile([P, PACK * U], BF16, name="res_b", align_bytes=64)
-        for copy, cols in ((nc.scalar.copy, slice(0, ROUND_ON_SCALAR)), (nc.vector.tensor_copy, slice(ROUND_ON_SCALAR, U))):
-            copy(res_b[:].rearrange("p (c t) -> p c t", t=PACK)[:, cols], res_all[:].rearrange("p t c -> p c t")[:, cols])
+            if t == 3:
+                parts = held.tile([P, 2, U], F32, name="parts2", tag="g2_first", align_bytes=64)
+                nc.vector.tensor_tensor(parts[:], four[2][:, :2, :], four[2][:, 2:, :], ADD)
+            nc.vector.tensor_tensor(four[t][:, 1:D, :], plain[t][:], g2_rest[:], MULT)
+        nc.vector.tensor_tensor(res[1][:, 0, :], parts[:, 0, :], parts[:, 1, :], ADD)
+        nc.sync.dma_start(out_rows[:, 2, :], res[1][:, 0, :])
+        last_parts = [held.tile([P, 2, U // 2], F32, name="last_parts%d" % c) for c in range(2)]
+        for part, cols in zip(last_parts, halves):
+            nc.vector.tensor_tensor(part[:], four[3][:, :2, cols], four[3][:, 2:, cols], ADD)
+        for part, cols in zip(last_parts, halves):
+            nc.vector.tensor_tensor(res[1][:, 1, cols], part[:, 0, :], part[:, 1, :], ADD)
+        nc.sync.dma_start(out_rows[:, 3, :], res[1][:, 1, :])
+        res_b = [held.tile([P, PACK * U // 2], BF16, name="res_b%d" % c, align_bytes=64) for c in range(2)]
+        for copy, rounded, cols in zip((nc.scalar.copy, nc.vector.tensor_copy), res_b, halves):
+            copy(rounded[:].rearrange("p (c t) -> p c t", t=PACK), res_all[:].rearrange("p t c -> p c t")[:, cols])
         res_c = held.tile([P, U], I32, name="res_c", align_bytes=64)
         res_s = held.tile([P, U], U8, name="res_s", align_bytes=64)
-        for cols in halves:
-            nc.vector.quantize_mx(
-                out=res_c[:, cols].bitcast(FP8X4), scales=res_s[:, cols], in_=res_b[:, PACK * cols.start : PACK * cols.stop]
-            )
+        for rounded, cols in zip(res_b, halves):
+            nc.vector.quantize_mx(out=res_c[:, cols].bitcast(FP8X4), scales=res_s[:, cols], in_=rounded[:])
             nc.sync.dma_start(out_1[0].rearrange("p n t -> p (n t)").bitcast(I32)[:, cols], res_c[:, cols])
         for q in range(4):
             eng = nc.sync if q == 3 else nc.scalar

@@ -215,16 +215,16 @@ def tile_picked_zappnp_relu_po_kernel(
             return back
 
         def own(t):
-            return plain_gather("own%d" % t, y[t], cen_t, V)
+            return plain_gather("own%d" % t, y[t], cen_t, V, "ungated")
+
+        def near(t, d):
+            return gated_gather("near%d_%d" % (t, d), y[t], pos_t[d], g1[d][:], V)
+
+        def onward(t, d):
+            return gated_gather("next%d_%d" % (t, d), z[t], nxt_t[d], g2[d], U)
 
         def root_term(t):
-            return plain_gather("root%d" % t, y[t], root_t, U, ("near1_2", "near2_0")[t])
-
-        def near(t, d, tag=None):
-            return gated_gather("near%d_%d" % (t, d), y[t], pos_t[d], g1[d][:], V, tag)
-
-        def onward(t, d, tag=None):
-            return gated_gather("next%d_%d" % (t, d), z[t], nxt_t[d], g2[d], U, tag)
+            return plain_gather("root%d" % t, y[t], root_t, U, "ungated")
 
         def free_bank(width):
             return psum.tile([P, width], F32, name="bank")
@@ -234,99 +234,73 @@ def tile_picked_zappnp_relu_po_kernel(
         def finish_z(t, back):
             nc.scalar.activation(z[t][:], back[:], ACT.Copy, scale=0.8)
 
+        plain = [held.tile([P, D - 1, U], F32, name="plain%d" % t) for t in range(2)]
+
+        def plain_onward(t):
+            for d in range(1, D):
+                nc.scalar.activation(plain[t][:, d - 1, :], z[t][:].indirect(nxt_t[d][:]), ACT.Copy)
+
         fetch_y(0, second_product(0))
         w2_q.append(quantise_w2_pair(1, round_w2_pair(1, nc.vector.tensor_copy, "h_b896")))
         fetch_y(1, second_product(1))
         y_banks = [second_product(t) for t in range(2, PACK)]
-        turned = [sum_bank(V, 0)]
-        turn(turned[0], near(0, 0), opens=True)
-        turn(turned[0], near(0, 1))
-        turn(turned[0], near(0, 2))
-        turn(turned[0], own(0), closes=True)
+        turned = sum_bank(V, 0)
+        turn(turned, near(0, 0), opens=True)
+        turn(turned, own(0))
+        turn(turned, near(0, 1))
+        turn(turned, near(0, 2), closes=True)
         fetch_y(2, y_banks[0])
-        turned.append(sum_bank(V, 1))
-        turn(turned[1], near(1, 0), opens=True)
-        turn(turned[1], near(1, 1))
-        turn(turned[1], own(1))
-        turn(turned[1], near(1, 2), closes=True)
-        fetch_y(3, y_banks[1])
-        back0 = turn_back(fetch_sum("z_sum0", turned[0]), free_bank(V))
-        turned.append(sum_bank(V, 0))
-        turn(turned[2], near(2, 0), opens=True)
-        turn(turned[2], own(2))
-        turn(turned[2], near(2, 1))
-        finish_z(0, back0)
-        own3 = own(3)
-        back1 = turn_back(fetch_sum("z_sum1", turned[1]), free_bank(V))
-        turn(turned[2], near(2, 2), closes=True)
-        roots = [root_term(0), root_term(1)]
-        finish_z(1, back1)
-        back2 = turn_back(fetch_sum("z_sum2", turned[2]), sum_bank(V, 1))
-        z_halves = (slice(0, V // 2), slice(V // 2, V))
-        last_turned = [sum_bank(V // 2, side) for side in range(2)]
-        for i, term in enumerate((own3, near(3, 0), near(3, 1))):
-            for bank, cols in zip(last_turned, z_halves):
-                turn(bank, term[:, cols], opens=(i == 0))
-        for bank, cols in zip(last_turned, z_halves):
-            term = held.tile([P, V // 2], F32, name="near3_2_%d" % cols.start)
-            nc.vector.tensor_tensor(term[:], y[3][:].indirect(pos_t[2][:, cols.start // 16 : cols.stop // 16]), g1[2][:, cols], MULT)
-            turn(bank, term, closes=True)
-        four = {}
-        plain = {t: held.tile([P, D - 1, U], F32, name="plain%d" % t) for t in (2, 3)}
-
-        def root_as_fourth(t):
-            four[t] = held.tile([P, D + 1, U], F32, name="four%d" % t, tag={2: "near2_2", 3: "near2_1"}[t], align_bytes=64)
-            nc.scalar.activation(four[t][:, D, :], y[t][:].indirect(root_t[:]), ACT.Copy)
-
-        def plain_onward(t, d):
-            nc.scalar.activation(plain[t][:, d - 1, :], z[t][:].indirect(nxt_t[d][:]), ACT.Copy)
-
-        root_as_fourth(2)
-        root_as_fourth(3)
-        finish_z(2, back2)
-        plain_onward(2, 1)
-        plain_onward(2, 2)
-        last_back = [turn_back(fetch_sum("z_sum3_%d" % i, bank), free_bank(V // 2)) for i, bank in enumerate(last_turned)]
-
-        def finish_last_z(i):
-            nc.scalar.activation(z[3][:, z_halves[i]], last_back[i][:], ACT.Copy, scale=0.8)
-
-        finish_last_z(0)
+        for t in range(1, PACK):
+            before, turned = turned, sum_bank(V, t % 2)
+            turn(turned, own(t), opens=True)
+            if t == 1:
+                fetch_y(3, y_banks[1])
+            turn(turned, near(t, 0))
+            turn(turned, near(t, 1))
+            back = turn_back(fetch_sum("z_sum%d" % (t - 1), before), free_bank(V))
+            turn(turned, near(t, 2), closes=True)
+            finish_z(t - 1, back)
+            if t < 3:
+                plain_onward(t - 1)
+        finish_z(3, turn_back(fetch_sum("z_sum3", turned), free_bank(V)))
 
         out_rows = out_0.rearrange("(p t) x -> p t x", t=PACK)
         res_all = held.tile([P, PACK, U], F32, name="res_all")
-        res = [res_all[:, 0:2, :], res_all[:, 2:4, :]]
         halves = (slice(0, U // 2), slice(U // 2, U))
-        pair_sums = []
+        o_banks = []
         for t in range(2):
-            if t == 1:
-                finish_last_z(1)
-                for d in range(1, D):
-                    plain_onward(3, d)
             bank = sum_bank(U, t)
-            turn(bank, roots[t], opens=True)
-            for d in range(D):
-                turn(bank, onward(t, d, "g1_%d" % d if t == 0 else None), closes=(d == D - 1))
-            pair_sums.append(fetch_sum("o_sum%d" % t, bank))
-        pair_back = sum_bank(2 * U, 1)
-        for t in range(2):
-            turn_back(pair_sums[t], pair_back[:, t * U : (t + 1) * U])
-        nc.scalar.copy(res[0], pair_back[:].rearrange("p (t c) -> p t c", t=2))
-        nc.sync.dma_start(out_rows[:, 0:2, :], res[0])
-        for t in (2, 3):
-            nc.vector.tensor_tensor(four[t][:, 0, :], z[t][:].indirect(nxt_t[0][:]), g2[0], MULT)
-            if t == 3:
-                parts = held.tile([P, 2, U], F32, name="parts2", tag="g2_first", align_bytes=64)
-                nc.vector.tensor_tensor(parts[:], four[2][:, :2, :], four[2][:, 2:, :], ADD)
-            nc.vector.tensor_tensor(four[t][:, 1:D, :], plain[t][:], g2_rest[:], MULT)
-        nc.vector.tensor_tensor(res[1][:, 0, :], parts[:, 0, :], parts[:, 1, :], ADD)
-        nc.sync.dma_start(out_rows[:, 2, :], res[1][:, 0, :])
-        last_parts = [held.tile([P, 2, U // 2], F32, name="last_parts%d" % c) for c in range(2)]
+            turn(bank, root_term(t), opens=True)
+            turn(bank, onward(t, 0))
+            gated = held.tile([P, D - 1, U], F32, name="gated%d" % t)
+            nc.vector.tensor_tensor(gated[:], plain[t][:], g2_rest[:], MULT)
+            turn(bank, gated[:, 0, :])
+            turn(bank, gated[:, 1, :], closes=True)
+            o_banks.append(bank)
+        pair_back = free_bank(2 * U)
+        turn_back(fetch_sum("o_sum0", o_banks[0]), pair_back[:, :U])
+        bank = free_bank(U)
+        turn(bank, root_term(2), opens=True)
+        turn(bank, onward(2, 0))
+        turn(bank, onward(2, 1))
+        turn(bank, onward(2, 2), closes=True)
+        turn_back(fetch_sum("o_sum1", o_banks[1]), pair_back[:, U:])
+        pairs = [held.tile([P, 2, U], F32, name="pair%d" % i, tag=("pair0", "ungated")[i], align_bytes=64) for i in range(2)]
+        nc.scalar.activation(pairs[1][:, 1, :], y[3][:].indirect(root_t[:]), ACT.Copy)
+        last_back = turn_back(fetch_sum("o_sum2", bank), free_bank(U))
+        nc.scalar.copy(res_all[:, 0:2, :], pair_back[:].rearrange("p (t c) -> p t c", t=2))
+        nc.sync.dma_start(out_rows[:, 0:2, :], res_all[:, 0:2, :])
+        nc.scalar.copy(res_all[:, 2, :], last_back[:])
+        nc.sync.dma_start(out_rows[:, 2, :], res_all[:, 2, :])
+        for d in range(D):
+            nc.vector.tensor_tensor(pairs[d // 2][:, d % 2, :], z[3][:].indirect(nxt_t[d][:]), g2[d], MULT)
+        parts = held.tile([P, 2, 2, U // 2], F32, name="parts", tag="o_sum2", align_bytes=64)
+        last_parts = [parts[:, c] for c in range(2)]
         for part, cols in zip(last_parts, halves):
-            nc.vector.tensor_tensor(part[:], four[3][:, :2, cols], four[3][:, 2:, cols], ADD)
+            nc.vector.tensor_tensor(part, pairs[0][:, :, cols], pairs[1][:, :, cols], ADD)
         for part, cols in zip(last_parts, halves):
-            nc.vector.tensor_tensor(res[1][:, 1, cols], part[:, 0, :], part[:, 1, :], ADD)
-        nc.sync.dma_start(out_rows[:, 3, :], res[1][:, 1, :])
+            nc.vector.tensor_tensor(res_all[:, 3, cols], part[:, 0, :], part[:, 1, :], ADD)
+        nc.sync.dma_start(out_rows[:, 3, :], res_all[:, 3, :])
         res_b = [held.tile([P, PACK * U // 2], BF16, name="res_b%d" % c, align_bytes=64) for c in range(2)]
         for copy, rounded, cols in zip((nc.scalar.copy, nc.vector.tensor_copy), res_b, halves):
             copy(rounded[:].rearrange("p (c t) -> p c t", t=PACK), res_all[:].rearrange("p t c -> p c t")[:, cols])

@@ -68,13 +68,13 @@ def tile_picked_zappnp_relu_po_kernel(
         nc.sync.dma_start(w2_raw[:], w2.rearrange("(p j) c -> p j c", j=PACK))
         pos_t = [load_list("pos1_t", pos1), load_list("pos2_t", pos2), load_list("pos3_t", pos3)]
         cen_t = load_list("cen_t", cen)
+        root_t = load_list("root_t", root)
         g2_first = held.tile([P, U], F32, name="g2_first", align_bytes=64)
         g2_rest = held.tile([P, D - 1, U], F32, name="g2_rest")
         g2 = [g2_first[:]] + [g2_rest[:, d, :] for d in range(D - 1)]
         for d in range(D):
             nc.sync.dma_start(g2[d], gate2[d])
         nxt_t = [load_list("nxt1_t", nxt1), load_list("nxt2_t", nxt2), load_list("nxt3_t", nxt3)]
-        root_t = load_list("root_t", root)
 
         ident = held.tile([P, P], F32, name="ident")
         nc.vector.memset(ident[:], 0.0)
@@ -214,17 +214,17 @@ def tile_picked_zappnp_relu_po_kernel(
                 nc.tensor.transpose(back[:, c : c + P], total[:, c : c + P], ident[:])
             return back
 
-        def own(t):
-            return plain_gather("own%d" % t, y[t], cen_t, V, "ungated")
-
         def near(t, d):
             return gated_gather("near%d_%d" % (t, d), y[t], pos_t[d], g1[d][:], V)
 
-        def onward(t, d):
-            return gated_gather("next%d_%d" % (t, d), z[t], nxt_t[d], g2[d], U)
+        def own(t):
+            return plain_gather("own%d" % t, y[t], cen_t, V, "ungated")
 
-        def root_term(t):
-            return plain_gather("root%d" % t, y[t], root_t, U, "ungated")
+        def onward(t, d, tag=None):
+            return gated_gather("next%d_%d" % (t, d), z[t], nxt_t[d], g2[d], U, tag)
+
+        def root_term(t, tag=None):
+            return plain_gather("root%d" % t, y[t], root_t, U, tag)
 
         def free_bank(width):
             return psum.tile([P, width], F32, name="bank")
@@ -234,72 +234,95 @@ def tile_picked_zappnp_relu_po_kernel(
         def finish_z(t, back):
             nc.scalar.activation(z[t][:], back[:], ACT.Copy, scale=0.8)
 
-        plain = [held.tile([P, D - 1, U], F32, name="plain%d" % t) for t in range(2)]
-
-        def plain_onward(t):
+        def plain_onward(t, tag):
+            plain = held.tile([P, D - 1, U], F32, name="plain%d" % t, tag=tag, align_bytes=64)
             for d in range(1, D):
-                nc.scalar.activation(plain[t][:, d - 1, :], z[t][:].indirect(nxt_t[d][:]), ACT.Copy)
+                nc.scalar.activation(plain[:, d - 1, :], z[t][:].indirect(nxt_t[d][:]), ACT.Copy)
+            return plain
+
+        def gate_plain(t, plain, tag):
+            gated = held.tile([P, D - 1, U], F32, name="gated%d" % t, tag=tag, align_bytes=64)
+            nc.vector.tensor_tensor(gated[:], plain[:], g2_rest[:], MULT)
+            return gated
 
         fetch_y(0, second_product(0))
         w2_q.append(quantise_w2_pair(1, round_w2_pair(1, nc.vector.tensor_copy, "h_b896")))
-        fetch_y(1, second_product(1))
-        y_banks = [second_product(t) for t in range(2, PACK)]
+        y_banks = [second_product(t) for t in range(1, PACK)]
         turned = sum_bank(V, 0)
-        turn(turned, near(0, 0), opens=True)
-        turn(turned, own(0))
+        turn(turned, own(0), opens=True)
+        fetch_y(1, y_banks[0])
+        turn(turned, near(0, 0))
         turn(turned, near(0, 1))
+        fetch_y(2, y_banks[1])
+        o_banks = [free_bank(U)]
+        turn(o_banks[0], root_term(0), opens=True)
         turn(turned, near(0, 2), closes=True)
-        fetch_y(2, y_banks[0])
+        plain = []
         for t in range(1, PACK):
             before, turned = turned, sum_bank(V, t % 2)
             turn(turned, own(t), opens=True)
-            if t == 1:
-                fetch_y(3, y_banks[1])
             turn(turned, near(t, 0))
-            turn(turned, near(t, 1))
             back = turn_back(fetch_sum("z_sum%d" % (t - 1), before), free_bank(V))
-            turn(turned, near(t, 2), closes=True)
+            if t == 1:
+                fetch_y(3, y_banks[2])
+            if t == 3:
+                plain.append(plain_onward(1, "ungated"))
             finish_z(t - 1, back)
-            if t < 3:
-                plain_onward(t - 1)
-        finish_z(3, turn_back(fetch_sum("z_sum3", turned), free_bank(V)))
+            turn(turned, near(t, 1))
+            if t == 2:
+                plain.append(plain_onward(0, "near2_1"))
+            turn(turned, near(t, 2), closes=True)
 
         out_rows = out_0.rearrange("(p t) x -> p t x", t=PACK)
         res_all = held.tile([P, PACK, U], F32, name="res_all")
         halves = (slice(0, U // 2), slice(U // 2, U))
-        o_banks = []
-        for t in range(2):
-            bank = sum_bank(U, t)
-            turn(bank, root_term(t), opens=True)
-            turn(bank, onward(t, 0))
-            gated = held.tile([P, D - 1, U], F32, name="gated%d" % t)
-            nc.vector.tensor_tensor(gated[:], plain[t][:], g2_rest[:], MULT)
-            turn(bank, gated[:, 0, :])
-            turn(bank, gated[:, 1, :], closes=True)
-            o_banks.append(bank)
+        def close_out_sum(t, tag):
+            gated = gate_plain(t, plain[t], tag)
+            turn(o_banks[t], gated[:, 0, :])
+            turn(o_banks[t], gated[:, 1, :], closes=True)
+
+        turn(o_banks[0], onward(0, 0))
+        close_out_sum(0, "gated0")
+        root1 = root_term(1, "near3_1")
+        back = turn_back(fetch_sum("z_sum3", turned), free_bank(V))
+        root2 = root_term(2, "next0_0")
+        o_sum0 = fetch_sum("o_sum0", o_banks[0])
+        finish_z(3, back)
+        o_banks.append(sum_bank(U, 1))
+        turn(o_banks[1], root1, opens=True)
+        turn(o_banks[1], onward(1, 0, "near3_0"))
+        close_out_sum(1, "gated1")
+        four = held.tile([P, D, U], F32, name="four", align_bytes=64)
+        for d in range(D):
+            nc.vector.tensor_tensor(four[:, d, :], z[2][:].indirect(nxt_t[d][:]), g2[d], MULT)
         pair_back = free_bank(2 * U)
-        turn_back(fetch_sum("o_sum0", o_banks[0]), pair_back[:, :U])
-        bank = free_bank(U)
-        turn(bank, root_term(2), opens=True)
-        turn(bank, onward(2, 0))
-        turn(bank, onward(2, 1))
-        turn(bank, onward(2, 2), closes=True)
+        turn_back(o_sum0, pair_back[:, :U])
+        root3 = root_term(3, "near3_0")
         turn_back(fetch_sum("o_sum1", o_banks[1]), pair_back[:, U:])
-        pairs = [held.tile([P, 2, U], F32, name="pair%d" % i, tag=("pair0", "ungated")[i], align_bytes=64) for i in range(2)]
-        nc.scalar.activation(pairs[1][:, 1, :], y[3][:].indirect(root_t[:]), ACT.Copy)
-        last_back = turn_back(fetch_sum("o_sum2", bank), free_bank(U))
+
+        def add(out, a, b):
+            nc.vector.tensor_tensor(out, a, b, ADD)
+
+        first2 = held.tile([P, U], F32, name="first2")
+        second2 = held.tile([P, U], F32, name="second2")
+        add(first2[:], four[:, 0, :], four[:, 1, :])
+        for cols in halves:
+            add(second2[:, cols], four[:, 2, cols], root2[:, cols])
+        for cols in halves:
+            add(res_all[:, 2, cols], first2[:, cols], second2[:, cols])
+        terms3 = [onward(3, 0)]
+        nc.sync.dma_start(out_rows[:, 2, :], res_all[:, 2, :])
         nc.scalar.copy(res_all[:, 0:2, :], pair_back[:].rearrange("p (t c) -> p t c", t=2))
         nc.sync.dma_start(out_rows[:, 0:2, :], res_all[:, 0:2, :])
-        nc.scalar.copy(res_all[:, 2, :], last_back[:])
-        nc.sync.dma_start(out_rows[:, 2, :], res_all[:, 2, :])
-        for d in range(D):
-            nc.vector.tensor_tensor(pairs[d // 2][:, d % 2, :], z[3][:].indirect(nxt_t[d][:]), g2[d], MULT)
-        parts = held.tile([P, 2, 2, U // 2], F32, name="parts", tag="o_sum2", align_bytes=64)
-        last_parts = [parts[:, c] for c in range(2)]
-        for part, cols in zip(last_parts, halves):
-            nc.vector.tensor_tensor(part, pairs[0][:, :, cols], pairs[1][:, :, cols], ADD)
-        for part, cols in zip(last_parts, halves):
-            nc.vector.tensor_tensor(res_all[:, 3, cols], part[:, 0, :], part[:, 1, :], ADD)
+        terms3.append(onward(3, 1))
+        first3 = held.tile([P, U], F32, name="first3")
+        add(first3[:], terms3[0][:], root3[:])
+        terms3.append(onward(3, 2))
+        second3 = held.tile([P, U], F32, name="second3", tag="o_sum1", align_bytes=64)
+        for cols in halves:
+            add(second3[:, cols], first3[:, cols], terms3[1][:, cols])
+        for cols in halves:
+            add(res_all[:, 3, cols], second3[:, cols], terms3[2][:, cols])
         nc.sync.dma_start(out_rows[:, 3, :], res_all[:, 3, :])
         res_b = [held.tile([P, PACK * U // 2], BF16, name="res_b%d" % c, align_bytes=64) for c in range(2)]
         for copy, rounded, cols in zip((nc.scalar.copy, nc.vector.tensor_copy), res_b, halves):

@@ -36,6 +36,7 @@ def tile_picked_zappnp_relu_po_kernel(
     nc = tc.nc
     with ExitStack() as ctx:
         held = ctx.enter_context(tc.tile_pool(name="held", bufs=1))
+        shared = ctx.enter_context(tc.tile_pool(name="shared", bufs=1))
         psum = ctx.enter_context(tc.psum_pool(name="psum", bufs=6))
         sums = ctx.enter_context(tc.psum_pool(name="sums", bufs=1))
 
@@ -218,7 +219,7 @@ def tile_picked_zappnp_relu_po_kernel(
             return gated_gather("near%d_%d" % (t, d), y[t], pos_t[d], g1[d][:], V)
 
         def own(t):
-            return plain_gather("own%d" % t, y[t], cen_t, V, "ungated")
+            return plain_gather("own%d" % t, y[t], cen_t, V, "ungated" if t else None)
 
         def onward(t, d, tag=None):
             return gated_gather("next%d_%d" % (t, d), z[t], nxt_t[d], g2[d], U, tag)
@@ -249,28 +250,37 @@ def tile_picked_zappnp_relu_po_kernel(
         w2_q.append(quantise_w2_pair(1, round_w2_pair(1, nc.vector.tensor_copy, "h_b896")))
         y_banks = [second_product(t) for t in range(1, PACK)]
         turned = sum_bank(V, 0)
-        turn(turned, own(0), opens=True)
+        turn(turned, near(0, 0), opens=True)
+        turn(turned, own(0))
         fetch_y(1, y_banks[0])
-        turn(turned, near(0, 0))
-        turn(turned, near(0, 1))
+        ungated = own(1)
         fetch_y(2, y_banks[1])
-        o_banks = [free_bank(U)]
-        turn(o_banks[0], root_term(0), opens=True)
+        roots = [root_term(0)]
+        turn(turned, near(0, 1))
         turn(turned, near(0, 2), closes=True)
         plain = []
         for t in range(1, PACK):
             before, turned = turned, sum_bank(V, t % 2)
-            turn(turned, own(t), opens=True)
+            turn(turned, ungated, opens=True)
             turn(turned, near(t, 0))
             back = turn_back(fetch_sum("z_sum%d" % (t - 1), before), free_bank(V))
+            if t < PACK - 1:
+                ungated = own(t + 1)
+            else:
+                plain.append(plain_onward(0, "ungated"))
             if t == 1:
                 fetch_y(3, y_banks[2])
-            if t == 3:
-                plain.append(plain_onward(1, "ungated"))
             finish_z(t - 1, back)
-            turn(turned, near(t, 1))
+            if t < PACK - 1:
+                turn(turned, near(t, 1))
+            else:
+                term = shared.tile([P, V], F32, name="near3_1", offset=0)
+                nc.vector.tensor_tensor(term[:], y[t][:].indirect(pos_t[1][:]), g1[1][:], MULT)
+                turn(turned, term)
+                plain_a = shared.tile([P, U], F32, name="plain_a", offset=0)
+                nc.scalar.activation(plain_a[:], z[1][:].indirect(nxt_t[1][:]), ACT.Copy)
             if t == 2:
-                plain.append(plain_onward(0, "near2_1"))
+                roots.append(root_term(1, "near2_1"))
             turn(turned, near(t, 2), closes=True)
 
         out_rows = out_0.rearrange("(p t) x -> p t x", t=PACK)
@@ -281,48 +291,58 @@ def tile_picked_zappnp_relu_po_kernel(
             turn(o_banks[t], gated[:, 0, :])
             turn(o_banks[t], gated[:, 1, :], closes=True)
 
+        o_banks = [sum_bank(U, 0)]
+        turn(o_banks[0], roots[0], opens=True)
         turn(o_banks[0], onward(0, 0))
         close_out_sum(0, "gated0")
-        root1 = root_term(1, "near3_1")
         back = turn_back(fetch_sum("z_sum3", turned), free_bank(V))
-        root2 = root_term(2, "next0_0")
-        o_sum0 = fetch_sum("o_sum0", o_banks[0])
+        plain_b = held.tile([P, U], F32, name="plain_b", tag="next0_0", align_bytes=64)
+        nc.scalar.activation(plain_b[:], z[1][:].indirect(nxt_t[2][:]), ACT.Copy)
+        roots.append(root_term(2, "gated0"))
         finish_z(3, back)
+        o_sum0 = fetch_sum("o_sum0", o_banks[0])
+        plain3 = held.tile([P, U], F32, name="plain3", align_bytes=64)
+        nc.scalar.activation(plain3[:], z[3][:].indirect(nxt_t[D - 1][:]), ACT.Copy)
         o_banks.append(sum_bank(U, 1))
-        turn(o_banks[1], root1, opens=True)
-        turn(o_banks[1], onward(1, 0, "near3_0"))
-        close_out_sum(1, "gated1")
-        four = held.tile([P, D, U], F32, name="four", align_bytes=64)
-        for d in range(D):
-            nc.vector.tensor_tensor(four[:, d, :], z[2][:].indirect(nxt_t[d][:]), g2[d], MULT)
+        turn(o_banks[1], roots[1], opens=True)
+        term = shared.tile([P, U], F32, name="next1_0", offset=4 * U)
+        nc.vector.tensor_tensor(term[:], z[1][:].indirect(nxt_t[0][:]), g2[0], MULT)
+        turn(o_banks[1], term)
+        gated1 = [held.tile([P, U], F32, name="gated1_%d" % d) for d in (1, 2)]
+        nc.vector.tensor_tensor(gated1[0][:], plain_a[:], g2[1], MULT)
+        turn(o_banks[1], gated1[0])
+        terms2 = [onward(2, 0), onward(2, 1)]
+        nc.vector.tensor_tensor(gated1[1][:], plain_b[:], g2[2], MULT)
+        turn(o_banks[1], gated1[1], closes=True)
+        terms2.append(onward(2, 2, "z_sum3"))
         pair_back = free_bank(2 * U)
         turn_back(o_sum0, pair_back[:, :U])
-        root3 = root_term(3, "near3_0")
         turn_back(fetch_sum("o_sum1", o_banks[1]), pair_back[:, U:])
+        root3 = root_term(3, "o_sum0")
 
         def add(out, a, b):
             nc.vector.tensor_tensor(out, a, b, ADD)
 
-        first2 = held.tile([P, U], F32, name="first2")
-        second2 = held.tile([P, U], F32, name="second2")
-        add(first2[:], four[:, 0, :], four[:, 1, :])
+        parts2 = held.tile([P, 2, U], F32, name="parts2")
         for cols in halves:
-            add(second2[:, cols], four[:, 2, cols], root2[:, cols])
+            add(parts2[:, 0, cols], terms2[0][:, cols], roots[2][:, cols])
         for cols in halves:
-            add(res_all[:, 2, cols], first2[:, cols], second2[:, cols])
+            add(parts2[:, 1, cols], parts2[:, 0, cols], terms2[1][:, cols])
+        for cols in halves:
+            add(res_all[:, 2, cols], parts2[:, 1, cols], terms2[2][:, cols])
         terms3 = [onward(3, 0)]
         nc.sync.dma_start(out_rows[:, 2, :], res_all[:, 2, :])
         nc.scalar.copy(res_all[:, 0:2, :], pair_back[:].rearrange("p (t c) -> p t c", t=2))
         nc.sync.dma_start(out_rows[:, 0:2, :], res_all[:, 0:2, :])
         terms3.append(onward(3, 1))
-        first3 = held.tile([P, U], F32, name="first3")
-        add(first3[:], terms3[0][:], root3[:])
-        terms3.append(onward(3, 2))
-        second3 = held.tile([P, U], F32, name="second3", tag="o_sum1", align_bytes=64)
+        gated3 = held.tile([P, U], F32, name="gated3")
+        nc.vector.tensor_tensor(gated3[:], plain3[:], g2[D - 1], MULT)
+        parts3 = held.tile([P, 2, U], F32, name="parts3", tag="o_sum1", align_bytes=64)
+        add(parts3[:, 0, :], terms3[0][:], terms3[1][:])
         for cols in halves:
-            add(second3[:, cols], first3[:, cols], terms3[1][:, cols])
+            add(parts3[:, 1, cols], gated3[:, cols], root3[:, cols])
         for cols in halves:
-            add(res_all[:, 3, cols], second3[:, cols], terms3[2][:, cols])
+            add(res_all[:, 3, cols], parts3[:, 0, cols], parts3[:, 1, cols])
         nc.sync.dma_start(out_rows[:, 3, :], res_all[:, 3, :])
         res_b = [held.tile([P, PACK * U // 2], BF16, name="res_b%d" % c, align_bytes=64) for c in range(2)]
         for copy, rounded, cols in zip((nc.scalar.copy, nc.vector.tensor_copy), res_b, halves):

@@ -345,8 +345,8 @@ def tile_picked_zappnp_relu_po_kernel(
             add(res_all[:, 3, cols], parts3[:, 0, cols], parts3[:, 1, cols])
         nc.sync.dma_start(out_rows[:, 3, :], res_all[:, 3, :])
         res_b = [held.tile([P, PACK * U // 2], BF16, name="res_b%d" % c, align_bytes=64) for c in range(2)]
-        for copy, rounded, cols in zip((nc.scalar.copy, nc.vector.tensor_copy), res_b, halves):
-            copy(rounded[:].rearrange("p (c t) -> p c t", t=PACK), res_all[:].rearrange("p t c -> p c t")[:, cols])
+        for rounded, cols in zip(res_b, halves):
+            nc.vector.tensor_copy(rounded[:].rearrange("p (c t) -> p c t", t=PACK), res_all[:].rearrange("p t c -> p c t")[:, cols])
         res_c = held.tile([P, U], I32, name="res_c", align_bytes=64)
         res_s = held.tile([P, U], U8, name="res_s", align_bytes=64)
         for rounded, cols in zip(res_b, halves):

@@ -205,8 +205,11 @@ def tile_picked_zappnp_relu_po_kernel(
                     start=(opens and c == 0), stop=(closes and c == width - P),
                 )
 
-        def fetch_sum(name, turned):
-            total = held.tile(list(turned.shape), F32, name=name, align_bytes=64)
+        def fetch_sum(name, turned, offset=None):
+            if offset is None:
+                total = held.tile(list(turned.shape), F32, name=name, align_bytes=64)
+            else:
+                total = shared.tile(list(turned.shape), F32, name=name, offset=offset)
             nc.scalar.copy(total[:], turned[:])
             return total
 
@@ -284,7 +287,6 @@ def tile_picked_zappnp_relu_po_kernel(
             turn(turned, near(t, 2), closes=True)
 
         out_rows = out_0.rearrange("(p t) x -> p t x", t=PACK)
-        res_all = held.tile([P, PACK, U], F32, name="res_all")
         halves = (slice(0, U // 2), slice(U // 2, U))
         def close_out_sum(t, tag):
             gated = gate_plain(t, plain[t], tag)
@@ -295,12 +297,12 @@ def tile_picked_zappnp_relu_po_kernel(
         turn(o_banks[0], roots[0], opens=True)
         turn(o_banks[0], onward(0, 0))
         close_out_sum(0, "gated0")
-        back = turn_back(fetch_sum("z_sum3", turned), free_bank(V))
+        back = turn_back(fetch_sum("z_sum3", turned, 4 * V), free_bank(V))
         plain_b = held.tile([P, U], F32, name="plain_b", tag="next0_0", align_bytes=64)
         nc.scalar.activation(plain_b[:], z[1][:].indirect(nxt_t[2][:]), ACT.Copy)
         roots.append(root_term(2, "gated0"))
         finish_z(3, back)
-        o_sum0 = fetch_sum("o_sum0", o_banks[0])
+        o_sum0 = fetch_sum("o_sum0", o_banks[0], 8 * V)
         plain3 = held.tile([P, U], F32, name="plain3", align_bytes=64)
         nc.scalar.activation(plain3[:], z[3][:].indirect(nxt_t[D - 1][:]), ACT.Copy)
         o_banks.append(sum_bank(U, 1))
@@ -308,38 +310,37 @@ def tile_picked_zappnp_relu_po_kernel(
         term = shared.tile([P, U], F32, name="next1_0", offset=4 * U)
         nc.vector.tensor_tensor(term[:], z[1][:].indirect(nxt_t[0][:]), g2[0], MULT)
         turn(o_banks[1], term)
-        gated1 = [held.tile([P, U], F32, name="gated1_%d" % d) for d in (1, 2)]
+        gated1 = [held.tile([P, U], F32, name="gated1_%d" % d, align_bytes=64) for d in (1, 2)]
         nc.vector.tensor_tensor(gated1[0][:], plain_a[:], g2[1], MULT)
         turn(o_banks[1], gated1[0])
         terms2 = [onward(2, 0), onward(2, 1)]
         nc.vector.tensor_tensor(gated1[1][:], plain_b[:], g2[2], MULT)
         turn(o_banks[1], gated1[1], closes=True)
-        terms2.append(onward(2, 2, "z_sum3"))
+        terms2.append(shared.tile([P, U], F32, name="next2_2", offset=4 * V))
+        nc.vector.tensor_tensor(terms2[2][:], z[2][:].indirect(nxt_t[2][:]), g2[2], MULT)
         pair_back = free_bank(2 * U)
         turn_back(o_sum0, pair_back[:, :U])
         turn_back(fetch_sum("o_sum1", o_banks[1]), pair_back[:, U:])
-        root3 = root_term(3, "o_sum0")
+        root3 = root_term(3, "gated1_2")
 
         def add(out, a, b):
             nc.vector.tensor_tensor(out, a, b, ADD)
 
-        parts2 = held.tile([P, 2, U], F32, name="parts2")
-        for cols in halves:
-            add(parts2[:, 0, cols], terms2[0][:, cols], roots[2][:, cols])
-        for cols in halves:
-            add(parts2[:, 1, cols], parts2[:, 0, cols], terms2[1][:, cols])
-        for cols in halves:
-            add(res_all[:, 2, cols], parts2[:, 1, cols], terms2[2][:, cols])
-        terms3 = [onward(3, 0)]
+        first2 = shared.tile([P, U], F32, name="first2", offset=4 * V + 4 * U)
+        second2 = held.tile([P, U], F32, name="second2")
+        add(first2[:], terms2[0][:], terms2[1][:])
+        add(second2[:], terms2[2][:], roots[2][:])
+        terms3 = [onward(3, 0), onward(3, 1)]
+        gated3 = held.tile([P, U], F32, name="gated3")
+        nc.vector.tensor_tensor(gated3[:], plain3[:], g2[D - 1], MULT)
+        res_all = shared.tile([P, PACK, U], F32, name="res_all", offset=8 * V)
+        add(res_all[:, 2, :], first2[:], second2[:])
         nc.sync.dma_start(out_rows[:, 2, :], res_all[:, 2, :])
         nc.scalar.copy(res_all[:, 0:2, :], pair_back[:].rearrange("p (t c) -> p t c", t=2))
         nc.sync.dma_start(out_rows[:, 0:2, :], res_all[:, 0:2, :])
-        terms3.append(onward(3, 1))
-        gated3 = held.tile([P, U], F32, name="gated3")
-        nc.vector.tensor_tensor(gated3[:], plain3[:], g2[D - 1], MULT)
         parts3 = held.tile([P, 2, U], F32, name="parts3", tag="o_sum1", align_bytes=64)
-        add(parts3[:, 0, :], terms3[0][:], terms3[1][:])
         for cols in halves:
+            add(parts3[:, 0, cols], terms3[0][:, cols], terms3[1][:, cols])
             add(parts3[:, 1, cols], gated3[:, cols], root3[:, cols])
         for cols in halves:
             add(res_all[:, 3, cols], parts3[:, 0, cols], parts3[:, 1, cols])

@@ -45,9 +45,9 @@ def tile_picked_zappnp_relu_po_kernel(
             nc.sync.dma_start(tl[:], src)
             return tl
 
-        offs_t = load_list("offs_t", offs)
         w1_raw = held.tile([P, PACK, H], F32, name="w1_raw")
         nc.sync.dma_start(w1_raw[:], w1.rearrange("(p j) c -> p j c", j=PACK))
+        offs_t = load_list("offs_t", offs)
         xs = held.tile([P, T], U8, name="xs", align_bytes=64)
         nc.vector.memset(xs[:].bitcast(I32), 0)
         for hf in range(2):

@@ -24,7 +24,7 @@ BLK = 128
 RELU_BLOCKS = tuple((c, BLK) for c in range(0, S, BLK))
 RELU_ON_VECTOR = (512,)
 X_PIECES = ((0, 256), (256, 256), (512, 512))
-WARM_UPS = 3
+WARM_UPS = (512, 512, 128)
 H_PIECES = ((0, 256), (256, 256), (512, 256), (768, 128), (896, 128))
 Y_PIECES = ((0, 512), (512, 256), (768, 128), (896, 128))
 
@@ -103,11 +103,11 @@ def tile_picked_zappnp_relu_po_kernel(
                 nc.tensor.transpose(bank[:, b * P : (b + 1) * P], gate_cols[:, j : j + 1].to_broadcast([P, P]), ident[:])
             nc.scalar.activation(g1[d][:], bank[:], ACT.Copy, scale=4.0)
 
-        for i in range(WARM_UPS):
-            bank = psum.tile([P, HALF], F32, name="bank")
+        for width in WARM_UPS:
+            bank = psum.tile([P, width], F32, name="bank")
             nc.tensor.matmul_mx(
                 out=bank[:], lhsT=w1_c[:, :P].bitcast(FP8X4), lhsT_scale=w1_s[:, :P],
-                rhs=w1_c[:].bitcast(FP8X4), rhs_scale=w1_s[:], start=True, stop=True,
+                rhs=w1_c[:, :width].bitcast(FP8X4), rhs_scale=w1_s[:, :width], start=True, stop=True,
             )
         xw_g = []
         for c0, width in X_PIECES:

@@ -45,10 +45,10 @@ def tile_picked_zappnp_relu_po_kernel(
             nc.sync.dma_start(tl[:], src)
             return tl
 
-        w1_raw = held.tile([P, PACK, H], F32, name="w1_raw")
+        w1_raw = held.tile([P, PACK, H], F32, name="w1_raw", align_bytes=256)
         nc.sync.dma_start(w1_raw[:], w1.rearrange("(p j) c -> p j c", j=PACK))
         offs_t = load_list("offs_t", offs)
-        xs = held.tile([P, T], U8, name="xs", align_bytes=64)
+        xs = held.tile([P, T], U8, name="xs", align_bytes=256)
         nc.vector.memset(xs[:].bitcast(I32), 0)
         for hf in range(2):
             nc.sync.dma_start(xs[64 * hf : 64 * hf + 32 : 4, :].bitcast(I32), x_scales[0, 8 * hf : 8 * hf + 8, :].bitcast(I32))
@@ -56,22 +56,22 @@ def tile_picked_zappnp_relu_po_kernel(
         nc.gpsimd.memset(gate_rows[:], 0.0)
         pieces = D * V // P
         nc.scalar.dma_start(gate_rows[:pieces, :], gate.rearrange("d p (b c) -> (d p b) c", c=P)[0 : D * V : P + 1, :])
-        xw = held.tile([P, T], I32, name="xw", align_bytes=64)
+        xw = held.tile([P, T], I32, name="xw", align_bytes=256)
         nc.sync.dma_start(xw[:], x_words[0].rearrange("p n t -> p (n t)").bitcast(I32))
-        xs_picked = held.tile([P, S], U8, name="xs_picked", align_bytes=64)
+        xs_picked = held.tile([P, S], U8, name="xs_picked", align_bytes=256)
         nc.vector.tensor_copy(xs_picked[:], xs[:].indirect(offs_t[:]))
-        xs_g = held.tile([P, S], U8, name="xs_g", align_bytes=64)
+        xs_g = held.tile([P, S], U8, name="xs_g", align_bytes=256)
         nc.vector.memset(xs_g[:].bitcast(I32), 0)
         for q in range(4):
             first = 64 * (q // 2) + 16 * (q % 2)
             nc.sync.dma_start(xs_g[32 * q : 32 * q + 4, :].bitcast(I32), xs_picked[first : first + 16 : 4, :].bitcast(I32))
-        w2_raw = held.tile([P, PACK, N], F32, name="w2_raw")
+        w2_raw = held.tile([P, PACK, N], F32, name="w2_raw", align_bytes=256)
         nc.sync.dma_start(w2_raw[:], w2.rearrange("(p j) c -> p j c", j=PACK))
         pos_t = [load_list("pos1_t", pos1), load_list("pos2_t", pos2), load_list("pos3_t", pos3)]
         cen_t = load_list("cen_t", cen)
         root_t = load_list("root_t", root)
-        g2_first = held.tile([P, U], F32, name="g2_first", align_bytes=64)
-        g2_rest = held.tile([P, D - 1, U], F32, name="g2_rest")
+        g2_first = held.tile([P, U], F32, name="g2_first", align_bytes=256)
+        g2_rest = held.tile([P, D - 1, U], F32, name="g2_rest", align_bytes=256)
         g2 = [g2_first[:]] + [g2_rest[:, d, :] for d in range(D - 1)]
         for d in range(D):
             nc.sync.dma_start(g2[d], gate2[d])
@@ -333,7 +333,7 @@ def tile_picked_zappnp_relu_po_kernel(
         terms3 = [onward(3, 0), onward(3, 1)]
         gated3 = held.tile([P, U], F32, name="gated3")
         nc.vector.tensor_tensor(gated3[:], plain3[:], g2[D - 1], MULT)
-        res_all = shared.tile([P, PACK, U], F32, name="res_all", offset=8 * V)
+        res_all = shared.tile([P, PACK, U], F32, name="res_all", offset=8 * V, align_bytes=256)
         add(res_all[:, 2, :], first2[:], second2[:])
         nc.sync.dma_start(out_rows[:, 2, :], res_all[:, 2, :])
         nc.scalar.copy(res_all[:, 0:2, :], pair_back[:].rearrange("p (t c) -> p t c", t=2))
@@ -348,8 +348,8 @@ def tile_picked_zappnp_relu_po_kernel(
         res_b = [held.tile([P, PACK * U // 2], BF16, name="res_b%d" % c, align_bytes=64) for c in range(2)]
         for rounded, cols in zip(res_b, halves):
             nc.vector.tensor_copy(rounded[:].rearrange("p (c t) -> p c t", t=PACK), res_all[:].rearrange("p t c -> p c t")[:, cols])
-        res_c = held.tile([P, U], I32, name="res_c", align_bytes=64)
-        res_s = held.tile([P, U], U8, name="res_s", align_bytes=64)
+        res_c = held.tile([P, U], I32, name="res_c", align_bytes=256)
+        res_s = held.tile([P, U], U8, name="res_s", align_bytes=256)
         for rounded, cols in zip(res_b, halves):
             nc.vector.quantize_mx(out=res_c[:, cols].bitcast(FP8X4), scales=res_s[:, cols], in_=rounded[:])
             nc.sync.dma_start(out_1[0].rearrange("p n t -> p (n t)").bitcast(I32)[:, cols], res_c[:, cols])

from contextlib import ExitStack

import concourse.mybir as mybir
from concourse.masks import make_identity

K, T, S, D, V, H, N, U = 512, 4096, 1024, 3, 512, 512, 512, 256
FLOPS = 2 * K * H * S + 2 * H * N * S

F32 = mybir.dt.float32
BF16 = mybir.dt.bfloat16
I32 = mybir.dt.int32
U32 = mybir.dt.uint32
U16 = mybir.dt.uint16
U8 = mybir.dt.uint8
FP8X4 = mybir.dt.float8_e4m3fn_x4
MULT = mybir.AluOpType.mult
ADD = mybir.AluOpType.add
ACT = mybir.ActivationFunctionType

P = 128
PACK = 4
HALF = S // 2
BLK = 128
RELU_BLOCKS = tuple((c, BLK) for c in range(0, S, BLK))
RELU_ON_VECTOR = (512,)
X_PIECES = ((0, 256), (256, 256), (512, 512))
WARM_UPS = (512, 512, 128)
H_PIECES = ((0, 256), (256, 256), (512, 256), (768, 128), (896, 128))
Y_PIECES = ((0, 512), (512, 256), (768, 128), (896, 128))


def tile_picked_zappnp_relu_po_kernel(
    tc, x_words, x_scales, w1, w2, gate, gate2, offs, cen, pos1, pos2, pos3, nxt1, nxt2, nxt3, root,
    out_0, out_1, out_2,
):
    nc = tc.nc
    with ExitStack() as ctx:
        held = ctx.enter_context(tc.tile_pool(name="held", bufs=1))
        shared = ctx.enter_context(tc.tile_pool(name="shared", bufs=1))
        psum = ctx.enter_context(tc.psum_pool(name="psum", bufs=6))
        sums = ctx.enter_context(tc.psum_pool(name="sums", bufs=1))

        def load_list(name, src):
            tl = held.tile(list(src.shape), U16, name=name)
            nc.sync.dma_start(tl[:], src)
            return tl

        w1_raw = held.tile([P, PACK, H], F32, name="w1_raw", align_bytes=256)
        nc.sync.dma_start(w1_raw[:], w1.rearrange("(p j) c -> p j c", j=PACK))
        offs_t = load_list("offs_t", offs)
        xs = held.tile([P, T], U8, name="xs", align_bytes=256)
        nc.vector.memset(xs[:].bitcast(I32), 0)
        for hf in range(2):
            nc.sync.dma_start(xs[64 * hf : 64 * hf + 32 : 4, :].bitcast(I32), x_scales[0, 8 * hf : 8 * hf + 8, :].bitcast(I32))
        gate_rows = held.tile([P, P], F32, name="gate_rows")
        nc.gpsimd.memset(gate_rows[:], 0.0)
        pieces = D * V // P
        nc.scalar.dma_start(gate_rows[:pieces, :], gate.rearrange("d p (b c) -> (d p b) c", c=P)[0 : D * V : P + 1, :])
        xw = held.tile([P, T], I32, name="xw", align_bytes=256)
        nc.sync.dma_start(xw[:], x_words[0].rearrange("p n t -> p (n t)").bitcast(I32))
        xs_picked = held.tile([P, S], U8, name="xs_picked", align_bytes=256)
        nc.vector.tensor_copy(xs_picked[:], xs[:].indirect(offs_t[:]))
        xs_g = held.tile([P, S], U8, name="xs_g", align_bytes=256)
        nc.vector.memset(xs_g[:].bitcast(I32), 0)
        for q in range(4):
            first = 64 * (q // 2) + 16 * (q % 2)
            nc.sync.dma_start(xs_g[32 * q : 32 * q + 4, :].bitcast(I32), xs_picked[first : first + 16 : 4, :].bitcast(I32))
        w2_raw = held.tile([P, PACK, N], F32, name="w2_raw", align_bytes=256)
        nc.sync.dma_start(w2_raw[:], w2.rearrange("(p j) c -> p j c", j=PACK))
        pos_t = [load_list("pos1_t", pos1), load_list("pos2_t", pos2), load_list("pos3_t", pos3)]
        cen_t = load_list("cen_t", cen)
        root_t = load_list("root_t", root)
        g2_first = held.tile([P, U], F32, name="g2_first", align_bytes=256)
        g2_rest = held.tile([P, D - 1, U], F32, name="g2_rest", align_bytes=256)
        g2 = [g2_first[:]] + [g2_rest[:, d, :] for d in range(D - 1)]
        for d in range(D):
            nc.sync.dma_start(g2[d], gate2[d])
        nxt_t = [load_list("nxt1_t", nxt1), load_list("nxt2_t", nxt2), load_list("nxt3_t", nxt3)]

        ident = held.tile([P, P], F32, name="ident")
        nc.vector.memset(ident[:], 0.0)
        make_identity(nc, ident[:], nomemset=True)

        w1_b = held.tile([P, PACK * H], BF16, name="w1_b", align_bytes=64)
        for copy, m in ((nc.vector.tensor_copy, slice(0, P // 4)), (nc.scalar.copy, slice(P // 4, P))):
            copy(
                w1_b[:].rearrange("p (t m j) -> p m j t", t=PACK, j=PACK)[:, m],
                w1_raw[:].rearrange("p j (m t) -> p m j t", t=PACK)[:, m],
            )
        w1_c = held.tile([P, H], U32, name="w1_c", align_bytes=64)
        w1_s = held.tile([P, H], U8, name="w1_s", align_bytes=64)
        nc.vector.quantize_mx(out=w1_c[:].bitcast(FP8X4), scales=w1_s[:], in_=w1_b[:])

        bank = psum.tile([P, P], F32, name="bank")
        nc.tensor.transpose(bank[:], gate_rows[:], ident[:])
        gate_cols = held.tile([P, pieces], F32, name="gate_cols")
        nc.scalar.copy(gate_cols[:], bank[:, :pieces])
        g1 = [held.tile([P, V], F32, name="g1_%d" % d, align_bytes=64) for d in range(D)]
        for d in range(D):
            bank = psum.tile([P, V], F32, name="bank")
            for b in range(V // P):
                j = d * V // P + b
                nc.tensor.transpose(bank[:, b * P : (b + 1) * P], gate_cols[:, j : j + 1].to_broadcast([P, P]), ident[:])
            nc.scalar.activation(g1[d][:], bank[:], ACT.Copy, scale=4.0)

        for width in WARM_UPS:
            bank = psum.tile([P, width], F32, name="bank")
            nc.tensor.matmul_mx(
                out=bank[:], lhsT=w1_c[:, :P].bitcast(FP8X4), lhsT_scale=w1_s[:, :P],
                rhs=w1_c[:, :width].bitcast(FP8X4), rhs_scale=w1_s[:, :width], start=True, stop=True,
            )
        xw_g = []
        for c0, width in X_PIECES:
            tl = held.tile([P, width], U32, name="xw_g%d" % c0, align_bytes=64)
            nc.vector.tensor_copy(tl[:], xw[:].bitcast(U32).indirect(offs_t[:, c0 // 16 : (c0 + width) // 16]))
            xw_g = xw_g + [tl[:, c : c + BLK] for c in range(0, width, BLK)]

        def round_w2_pair(pair, engine_copy, tag):
            w2_b = held.tile([P, 2 * PACK * P], BF16, name="w2_b%d" % pair, tag=tag, align_bytes=64)
            engine_copy(
                w2_b[:].rearrange("p (t m j) -> p m j t", t=2, j=PACK),
                w2_raw[:].rearrange("p j (m t) -> p m j t", t=PACK)[:, :, :, 2 * pair : 2 * pair + 2],
            )
            return w2_b

        def quantise_w2_pair(pair, w2_b):
            w2_c = held.tile([P, 2 * P], U32, name="w2_c%d" % pair, align_bytes=64)
            w2_s = held.tile([P, 2 * P], U8, name="w2_s%d" % pair, align_bytes=64)
            nc.vector.quantize_mx(out=w2_c[:].bitcast(FP8X4), scales=w2_s[:], in_=w2_b[:])
            return w2_c, w2_s

        w2_first = round_w2_pair(0, nc.vector.tensor_copy, "w2_b0")
        w2_q = []

        h_c = [held.tile([P, HALF], U32, name="h_c%d" % hf, align_bytes=64) for hf in range(2)]
        h_s = [held.tile([P, HALF], U8, name="h_s%d" % hf, align_bytes=64) for hf in range(2)]
        for p0, width in H_PIECES:
            h_b = held.tile([P, PACK * width], BF16, name="h_b%d" % p0, align_bytes=64)
            for c0, n in [blk for blk in RELU_BLOCKS if p0 <= blk[0] < p0 + width]:
                if c0 in (640, 768):
                    bank = sums.tile([P, PACK, n], F32, name="relu_bank", tag="sum_%d" % (c0 // BLK % 2))
                else:
                    bank = psum.tile([P, PACK, n], F32, name="bank")
                for t in range(PACK):
                    nc.tensor.matmul_mx(
                        out=bank[:, t, :],
                        lhsT=w1_c[:, t * P : (t + 1) * P].bitcast(FP8X4), lhsT_scale=w1_s[:, t * P : (t + 1) * P],
                        rhs=xw_g[c0 // BLK].bitcast(FP8X4), rhs_scale=xs_g[:, c0 : c0 + n],
                        start=True, stop=True,
                    )
                dst = h_b[:, PACK * (c0 - p0) : PACK * (c0 - p0 + n)].rearrange("p (n t) -> p n t", t=PACK)
                src = bank[:].rearrange("p t n -> p n t")
                if c0 in RELU_ON_VECTOR:
                    nc.vector.tensor_scalar_max(dst, src, 0.0)
                else:
                    nc.scalar.activation(dst, src, ACT.Relu)
            hf, c = divmod(p0, HALF)
            nc.vector.quantize_mx(out=h_c[hf][:, c : c + width].bitcast(FP8X4), scales=h_s[hf][:, c : c + width], in_=h_b[:])
            if p0 == 0:
                w2_q.append(quantise_w2_pair(0, w2_first))

        y = [held.tile([P, S], F32, name="y%d" % t) for t in range(PACK)]

        def second_product(t):
            w2_c, w2_s = w2_q[t // 2]
            rows = slice(t % 2 * P, (t % 2 + 1) * P)
            pieces_out = []
            for c0, width in Y_PIECES if t == 0 else ((0, HALF), (HALF, HALF)):
                hf, c = divmod(c0, HALF)
                bank = psum.tile([P, width], F32, name="bank")
                nc.tensor.matmul_mx(
                    out=bank[:],
                    lhsT=w2_c[:, rows].bitcast(FP8X4), lhsT_scale=w2_s[:, rows],
                    rhs=h_c[hf][:, c : c + width].bitcast(FP8X4), rhs_scale=h_s[hf][:, c : c + width],
                    start=True, stop=True,
                )
                pieces_out.append((c0, width, bank))
            return pieces_out

        def fetch_y(t, banks):
            for c0, width, bank in banks:
                if t == 0 and c0 == HALF:
                    nc.vector.tensor_scalar_mul(y[t][:, c0 : c0 + width], bank[:], 0.2)
                else:
                    nc.scalar.activation(y[t][:, c0 : c0 + width], bank[:], ACT.Copy, scale=0.2)

        def plain_gather(name, window, offsets, width, tag=None):
            term = held.tile([P, width], F32, name=name, tag=tag or name, align_bytes=64)
            nc.scalar.activation(term[:], window[:].indirect(offsets[:]), ACT.Copy)
            return term

        def gated_gather(name, window, offsets, gates, width, tag=None):
            term = held.tile([P, width], F32, name=name, tag=tag or name, align_bytes=64)
            nc.vector.tensor_tensor(term[:], window[:].indirect(offsets[:]), gates, MULT)
            return term

        def sum_bank(width, side):
            return sums.tile([P, width], F32, name="turned", tag="sum_%d" % side)

        def turn(turned, term, first_column=0, opens=False, closes=False):
            width = term.shape[1]
            for c in range(0, width, P):
                nc.tensor.matmul(
                    turned[:, first_column + c : first_column + c + P], term[:, c : c + P], ident[:], is_transpose=True,
                    start=(opens and c == 0), stop=(closes and c == width - P),
                )

        def fetch_sum(name, turned, offset=None):
            if offset is None:
                total = held.tile(list(turned.shape), F32, name=name, align_bytes=64)
            else:
                total = shared.tile(list(turned.shape), F32, name=name, offset=offset)
            nc.scalar.copy(total[:], turned[:])
            return total

        def turn_back(total, back):
            for c in range(0, total.shape[1], P):
                nc.tensor.transpose(back[:, c : c + P], total[:, c : c + P], ident[:])
            return back

        def near(t, d):
            return gated_gather("near%d_%d" % (t, d), y[t], pos_t[d], g1[d][:], V)

        def own(t):
            return plain_gather("own%d" % t, y[t], cen_t, V, "ungated" if t else None)

        def onward(t, d, tag=None):
            return gated_gather("next%d_%d" % (t, d), z[t], nxt_t[d], g2[d], U, tag)

        def root_term(t, tag=None):
            return plain_gather("root%d" % t, y[t], root_t, U, tag)

        def free_bank(width):
            return psum.tile([P, width], F32, name="bank")

        z = [held.tile([P, V], F32, name="z%d" % t) for t in range(PACK)]

        def finish_z(t, back):
            nc.scalar.activation(z[t][:], back[:], ACT.Copy, scale=0.8)

        def plain_onward(t, tag):
            plain = held.tile([P, D - 1, U], F32, name="plain%d" % t, tag=tag, align_bytes=64)
            for d in range(1, D):
                nc.scalar.activation(plain[:, d - 1, :], z[t][:].indirect(nxt_t[d][:]), ACT.Copy)
            return plain

        def gate_plain(t, plain, tag):
            gated = held.tile([P, D - 1, U], F32, name="gated%d" % t, tag=tag, align_bytes=64)
            nc.vector.tensor_tensor(gated[:], plain[:], g2_rest[:], MULT)
            return gated

        fetch_y(0, second_product(0))
        w2_q.append(quantise_w2_pair(1, round_w2_pair(1, nc.vector.tensor_copy, "h_b896")))
        y_banks = [second_product(t) for t in range(1, PACK)]
        turned = sum_bank(V, 0)
        turn(turned, near(0, 0), opens=True)
        turn(turned, own(0))
        fetch_y(1, y_banks[0])
        ungated = own(1)
        fetch_y(2, y_banks[1])
        roots = [root_term(0)]
        turn(turned, near(0, 1))
        turn(turned, near(0, 2), closes=True)
        plain = []
        for t in range(1, PACK):
            before, turned = turned, sum_bank(V, t % 2)
            turn(turned, ungated, opens=True)
            turn(turned, near(t, 0))
            back = turn_back(fetch_sum("z_sum%d" % (t - 1), before), free_bank(V))
            if t < PACK - 1:
                ungated = own(t + 1)
            else:
                plain.append(plain_onward(0, "ungated"))
            if t == 1:
                fetch_y(3, y_banks[2])
            finish_z(t - 1, back)
            if t < PACK - 1:
                turn(turned, near(t, 1))
            else:
                term = shared.tile([P, V], F32, name="near3_1", offset=0)
                nc.vector.tensor_tensor(term[:], y[t][:].indirect(pos_t[1][:]), g1[1][:], MULT)
                turn(turned, term)
                plain_a = shared.tile([P, U], F32, name="plain_a", offset=0)
                nc.scalar.activation(plain_a[:], z[1][:].indirect(nxt_t[1][:]), ACT.Copy)
            if t == 2:
                roots.append(root_term(1, "near2_1"))
            turn(turned, near(t, 2), closes=True)

        out_rows = out_0.rearrange("(p t) x -> p t x", t=PACK)
        halves = (slice(0, U // 2), slice(U // 2, U))
        def close_out_sum(t, tag):
            gated = gate_plain(t, plain[t], tag)
            turn(o_banks[t], gated[:, 0, :])
            turn(o_banks[t], gated[:, 1, :], closes=True)

        o_banks = [sum_bank(U, 0)]
        turn(o_banks[0], roots[0], opens=True)
        turn(o_banks[0], onward(0, 0))
        close_out_sum(0, "gated0")
        back = turn_back(fetch_sum("z_sum3", turned, 4 * V), free_bank(V))
        plain_b = held.tile([P, U], F32, name="plain_b", tag="next0_0", align_bytes=64)
        nc.scalar.activation(plain_b[:], z[1][:].indirect(nxt_t[2][:]), ACT.Copy)
        roots.append(root_term(2, "gated0"))
        finish_z(3, back)
        o_sum0 = fetch_sum("o_sum0", o_banks[0], 8 * V)
        plain3 = held.tile([P, U], F32, name="plain3", align_bytes=64)
        nc.scalar.activation(plain3[:], z[3][:].indirect(nxt_t[D - 1][:]), ACT.Copy)
        o_banks.append(sum_bank(U, 1))
        turn(o_banks[1], roots[1], opens=True)
        term = shared.tile([P, U], F32, name="next1_0", offset=4 * U)
        nc.vector.tensor_tensor(term[:], z[1][:].indirect(nxt_t[0][:]), g2[0], MULT)
        turn(o_banks[1], term)
        gated1 = [held.tile([P, U], F32, name="gated1_%d" % d, align_bytes=64) for d in (1, 2)]
        nc.vector.tensor_tensor(gated1[0][:], plain_a[:], g2[1], MULT)
        turn(o_banks[1], gated1[0])
        terms2 = [onward(2, 0), onward(2, 1)]
        nc.vector.tensor_tensor(gated1[1][:], plain_b[:], g2[2], MULT)
        turn(o_banks[1], gated1[1], closes=True)
        terms2.append(shared.tile([P, U], F32, name="next2_2", offset=4 * V))
        nc.vector.tensor_tensor(terms2[2][:], z[2][:].indirect(nxt_t[2][:]), g2[2], MULT)
        pair_back = free_bank(2 * U)
        turn_back(o_sum0, pair_back[:, :U])
        turn_back(fetch_sum("o_sum1", o_banks[1]), pair_back[:, U:])
        root3 = root_term(3, "gated1_2")

        def add(out, a, b):
            nc.vector.tensor_tensor(out, a, b, ADD)

        first2 = shared.tile([P, U], F32, name="first2", offset=4 * V + 4 * U)
        second2 = held.tile([P, U], F32, name="second2")
        add(first2[:], terms2[0][:], terms2[1][:])
        add(second2[:], terms2[2][:], roots[2][:])
        terms3 = [onward(3, 0), onward(3, 1)]
        gated3 = held.tile([P, U], F32, name="gated3")
        nc.vector.tensor_tensor(gated3[:], plain3[:], g2[D - 1], MULT)
        res_all = shared.tile([P, PACK, U], F32, name="res_all", offset=8 * V, align_bytes=256)
        add(res_all[:, 2, :], first2[:], second2[:])
        nc.sync.dma_start(out_rows[:, 2, :], res_all[:, 2, :])
        nc.scalar.copy(res_all[:, 0:2, :], pair_back[:].rearrange("p (t c) -> p t c", t=2))
        nc.sync.dma_start(out_rows[:, 0:2, :], res_all[:, 0:2, :])
        parts3 = held.tile([P, 2, U], F32, name="parts3", tag="o_sum1", align_bytes=64)
        for cols in halves:
            add(parts3[:, 0, cols], terms3[0][:, cols], terms3[1][:, cols])
            add(parts3[:, 1, cols], gated3[:, cols], root3[:, cols])
        for cols in halves:
            add(res_all[:, 3, cols], parts3[:, 0, cols], parts3[:, 1, cols])
        nc.sync.dma_start(out_rows[:, 3, :], res_all[:, 3, :])
        res_b = [held.tile([P, PACK * U // 2], BF16, name="res_b%d" % c, align_bytes=64) for c in range(2)]
        for rounded, cols in zip(res_b, halves):
            nc.vector.tensor_copy(rounded[:].rearrange("p (c t) -> p c t", t=PACK), res_all[:].rearrange("p t c -> p c t")[:, cols])
        res_c = held.tile([P, U], I32, name="res_c", align_bytes=256)
        res_s = held.tile([P, U], U8, name="res_s", align_bytes=256)
        for rounded, cols in zip(res_b, halves):
            nc.vector.quantize_mx(out=res_c[:, cols].bitcast(FP8X4), scales=res_s[:, cols], in_=rounded[:])
            nc.sync.dma_start(out_1[0].rearrange("p n t -> p (n t)").bitcast(I32)[:, cols], res_c[:, cols])
        for q in range(4):
            eng = nc.sync if q == 3 else nc.scalar
            eng.dma_start(out_2[0, 4 * q : 4 * q + 4, :].bitcast(I32), res_s[32 * q : 32 * q + 4, :].bitcast(I32))
